import numpy as np
import ml_dtypes


def mxq(x, axis, fmt="e4m3"):
    dtype, down = {"e4m3": (ml_dtypes.float8_e4m3fn, 7), "e5m2": (ml_dtypes.float8_e5m2, 14)}[fmt]
    v = np.moveaxis(np.asarray(x, np.float32).astype(ml_dtypes.bfloat16).astype(np.float64), axis, -1)
    blocks = v.reshape(v.shape[:-1] + (-1, 32))
    amax = np.abs(blocks).max(-1, keepdims=True)
    byte = np.maximum(np.where(amax > 0, np.frexp(amax)[1] - 1 + 127, 0) - down, 1)
    scale = np.exp2(byte - 127.0)
    codes = (blocks / scale).astype(np.float32).astype(dtype).astype(np.float64)
    return np.moveaxis((codes * scale).reshape(v.shape), -1, axis)


WIDE = False


def mx_kscale(k):
    if not WIDE:
        return np.ones(k)
    levels = np.array([24, -24, 12, -12, 0])
    if k % 512:
        return np.exp2(np.random.permutation(np.resize(levels, k // 32))).repeat(32)
    a = np.empty((k // 512, 16))
    for p in range(k // 512):
        a[p, :8] = np.random.permutation(np.resize(levels, 8))
        for g in range(8):
            far = levels[np.abs(levels - a[p, g]) >= 10]
            a[p, g + 8] = far[np.random.randint(len(far))]
    return np.exp2(a.ravel()).repeat(32)


def f64(x):
    return np.asarray(x).astype(np.float64)


def striped(idx):
    return np.tile(idx.reshape(-1, 16).T, (8, 1)).astype(np.uint16)


def unstriped(offs):
    return offs[:16].T.reshape(-1).astype(np.int64)


E2M1 = np.array([0.0, 0.5, 1.0, 1.5, 2.0, 3.0, 4.0, 6.0, -0.0, -0.5, -1.0, -1.5, -2.0, -3.0, -4.0, -6.0])


def pack_weight(w, fmt):
    k, n = w.shape
    w = f64(np.asarray(w, np.float32).astype(ml_dtypes.bfloat16)).reshape(k // 32, 32, n)
    amax = np.abs(w).max(1)
    if fmt == "e4m3":
        byte = np.frexp(amax)[1] - 1 + 127 - 7
    else:
        mant, ex = np.frexp(amax / 6.0)
        byte = np.where(mant > 0.5, ex, ex - 1) + 127
    byte = np.clip(np.where(amax > 0, byte, 1), 1, 254)
    scaled = (w * np.exp2(127.0 - byte)[:, None, :]).reshape(k, n).astype(np.float32)
    by_word = np.ascontiguousarray(scaled.reshape(k // 512, 128, 4, n).transpose(0, 1, 3, 2))
    if fmt == "e4m3":
        words = by_word.astype(ml_dtypes.float8_e4m3fn).view(np.uint8)
    else:
        c = by_word.astype(ml_dtypes.float4_e2m1fn).view(np.uint8) & 0xF
        words = (c[..., 0::2] | (c[..., 1::2] << 4)).reshape(k // 512, 128, 2 * n)
    return np.ascontiguousarray(words), np.ascontiguousarray(byte.astype(np.uint8).reshape(k // 512, 16, n))


def unpack_weight(words, scales, fmt):
    g, _, n = scales.shape
    words = np.ascontiguousarray(words).reshape(g, 128, n, -1)
    if fmt == "e4m3":
        vals = words.view(ml_dtypes.float8_e4m3fn).astype(np.float64)
    else:
        nib = np.empty((g, 128, n, 4), np.uint8)
        nib[..., 0::2] = words & 0xF
        nib[..., 1::2] = words >> 4
        vals = E2M1[nib]
    vals = vals * np.repeat(np.exp2(scales.astype(np.float64) - 127.0), 8, axis=1)[..., None]
    return vals.transpose(0, 1, 3, 2).reshape(g * 512, n)


def pack_table4(v):
    words, scales = pack_weight(v, "e2m1")
    g, t = words.shape[0] // 2, v.shape[1]
    return np.ascontiguousarray(words.reshape(g, 2, 128, t, 2).transpose(0, 2, 3, 1, 4).reshape(g, 128, t, 4)), scales


def unpack_table4(words, scales):
    g, _, t, _ = words.shape
    return unpack_weight(words.reshape(g, 128, t, 2, 2).transpose(0, 3, 1, 2, 4).reshape(2 * g, 128, 2 * t), scales, "e2m1")


def sigm(f):
    return 1.0 / (1.0 + np.exp(-np.maximum(f, -700.0)))


K, N, T, J = 1024, 512, 2048, 1024


def setup_inputs():
    n = np.random.standard_normal
    s = mx_kscale(K)[:, None]
    wg = n((K, N)) / np.sqrt(K) / s
    p_tab = pack_table4(n((K, T)) * s)
    p_wg8 = pack_weight(wg[:512], "e4m3")
    p_wg4 = pack_weight(wg[512:], "e2m1")
    return {
        "tab_words": p_tab[0],
        "tab_scales": p_tab[1],
        "wg8_words": p_wg8[0],
        "wg8_scales": p_wg8[1],
        "wg4_words": p_wg4[0],
        "wg4_scales": p_wg4[1],
        "wh": (n((K, N)) / np.sqrt(K) / s).astype(np.float32),
        "bg": (0.3 * n(N) - 1.0).astype(np.float32),
        "rT": (n((N, T))).astype(np.float32),
        "offs": striped(np.random.permutation(T)[:J]),
    }


def reference(tab_words, tab_scales, wg8_words, wg8_scales, wg4_words, wg4_scales, wh, bg, rT, offs):
    idx = unstriped(offs)
    tab_ = unpack_table4(tab_words, tab_scales)[:, idx]
    wg8_ = unpack_weight(wg8_words, wg8_scales, "e4m3")
    wg4_ = unpack_weight(wg4_words, wg4_scales, "e2m1")
    wh_ = mxq(f64(wh), 0, "e4m3")
    ga = wg8_.T @ tab_[:512] + wg4_.T @ tab_[512:]
    gate = sigm(ga + f64(bg)[:, None])
    ha = wh_.T @ tab_
    return f64(rT)[:, idx] + gate * (np.maximum(ha, 0.0) - f64(rT)[:, idx])

@@ -1,0 +1,181 @@
+from contextlib import ExitStack
+
+import concourse.mybir as mybir
+
+K, N, T, J = 1024, 512, 2048, 1024
+FLOPS = 2 * 2 * K * N * J
+
+F32 = mybir.dt.float32
+BF16 = mybir.dt.bfloat16
+I32 = mybir.dt.int32
+U32 = mybir.dt.uint32
+U16 = mybir.dt.uint16
+U8 = mybir.dt.uint8
+FP8X4 = mybir.dt.float8_e4m3fn_x4
+FP4X4 = mybir.dt.float4_e2m1fn_x4
+ALU = mybir.AluOpType
+ACT = mybir.ActivationFunctionType
+
+P = 128
+PACK = 4
+K_PASS = P * PACK
+QUADS = 4
+HALF = 512
+LIST_COLS = HALF // 16
+W_HALF = N // 2
+SC_ROWS = 32
+
+
+def tile_list_hwayt_mix_relu_kernel(
+    tc, tab_words, tab_scales, wg8_words, wg8_scales, wg4_words, wg4_scales, wh, bg, rT, offs, out
+):
+    nc = tc.nc
+    with ExitStack() as ctx:
+        held = ctx.enter_context(tc.tile_pool(name="held", bufs=1))
+        windows = ctx.enter_context(tc.tile_pool(name="windows", bufs=2))
+        stage = ctx.enter_context(tc.tile_pool(name="stage", bufs=2))
+        work = ctx.enter_context(tc.tile_pool(name="work", bufs=4))
+        psum = ctx.enter_context(tc.psum_pool(name="psum", bufs=4))
+
+        offsets = held.tile([P, J // 16], U16, name="offsets")
+        nc.sync.dma_start(offsets[:], offs)
+
+        def listed(h):
+            return offsets[:, h * LIST_COLS : (h + 1) * LIST_COLS]
+
+        tab_sc = held.tile([P, T], U8, name="tab_sc", align_bytes=64)
+        nc.sync.dma_start(tab_sc[0:SC_ROWS, :].bitcast(I32), tab_scales.rearrange("a q t -> q a t").bitcast(I32))
+        nc.vector.memset(tab_sc[32:64, :].bitcast(I32), 0)
+        nc.vector.memset(tab_sc[64:128, :].bitcast(I32), 0)
+
+        table = windows.tile([P, T], I32, name="table", tag="window", align_bytes=64)
+        nc.sync.dma_start(table[:], tab_words[0].rearrange("p t b -> p (t b)").bitcast(I32))
+
+        warm = held.tile([P, 8], F32, name="warm")
+        warm_out = held.tile([P, 8], F32, name="warm_out")
+        nc.gpsimd.memset(warm[:], 0.0)
+        nc.scalar.activation(warm_out[:], warm[:], ACT.Sigmoid)
+
+        joined = held.tile([SC_ROWS, J + N], U8, name="joined", align_bytes=64)
+        nc.sync.dma_start(joined[0:SC_ROWS:2, J:].bitcast(I32), wg8_scales[0].bitcast(I32))
+        nc.sync.dma_start(joined[1:SC_ROWS:2, J:].bitcast(I32), wg4_scales[0].bitcast(I32))
+        planes = held.tile([P, 2, J + N], U8, name="planes", align_bytes=64)
+        nc.gpsimd.memset(planes[:].rearrange("p a c -> p (a c)").bitcast(I32), 0)
+
+        wg8 = held.tile([P, N], I32, name="wg8", align_bytes=64)
+        nc.sync.dma_start(wg8[:], wg8_words[0].rearrange("p n b -> p (n b)").bitcast(I32))
+        wg4 = held.tile([P, 2 * N], U8, name="wg4", align_bytes=64)
+        nc.sync.dma_start(wg4[:].bitcast(I32), wg4_words[0].bitcast(I32))
+
+        bias = held.tile([P, N // P], F32, name="bias")
+        with nc.allow_non_contiguous_dma(reason="one bias value for each partition and block"):
+            nc.sync.dma_start(bias[:], bg.rearrange("(b p) -> p b", p=P))
+        neg_bias = held.tile([P, N // P], F32, name="neg_bias")
+        nc.gpsimd.tensor_scalar(neg_bias[:], bias[:], -1.0, 0.0, ALU.mult, ALU.add)
+
+        def load_wh(w):
+            raws = []
+            for a in range(2):
+                raw = stage.tile([P, PACK, W_HALF], F32, name="raw", tag="raw")
+                rows = wh[a * K_PASS : (a + 1) * K_PASS, w * W_HALF : (w + 1) * W_HALF]
+                nc.sync.dma_start(raw[:], rows.rearrange("(p i) n -> p i n", i=PACK))
+                raws.append(raw)
+            return raws
+
+        def round_wh(raws):
+            grouped = stage.tile([P, 2, W_HALF, PACK], BF16, name="grouped", tag="grouped", align_bytes=64)
+            for a in range(2):
+                nc.scalar.copy(
+                    grouped[:, a].rearrange("p (c e) i -> p c i e", e=4),
+                    raws[a][:].rearrange("p i (c e) -> p c i e", e=4),
+                )
+            return grouped
+
+        def quantize_wh(grouped):
+            codes = stage.tile([P, 2 * W_HALF], U32, name="codes", tag="codes", align_bytes=64)
+            scales = stage.tile([P, 2 * W_HALF], U8, name="scales", tag="scales", align_bytes=64)
+            nc.vector.quantize_mx(
+                out=codes[:].bitcast(FP8X4), scales=scales[:], in_=grouped[:].rearrange("p a n i -> p (a n i)")
+            )
+            return codes, scales
+
+        def load_r(b):
+            carried = windows.tile([P, T], F32, name="carried", tag="window", align_bytes=64)
+            nc.sync.dma_start(carried[:], rT[b * P : (b + 1) * P, :])
+            return carried
+
+        raws = load_wh(0)
+        r_tiles = [load_r(0)]
+
+        picked_sc = held.tile([P, J], U8, name="picked_sc", align_bytes=64)
+        nc.vector.tensor_copy(picked_sc[:], tab_sc[:].indirect(offsets[:]))
+        nc.vector.tensor_copy(joined[:, 0:J].bitcast(I32), picked_sc[0:SC_ROWS, :].bitcast(I32))
+        for q in range(QUADS):
+            nc.scalar.dma_start(
+                planes[32 * q : 32 * q + 4].bitcast(I32), joined[8 * q : 8 * q + 8, :].bitcast(I32)
+            )
+        picked = []
+        for h in range(2):
+            words = held.tile([P, HALF], U32, name=f"picked_{h}", align_bytes=64)
+            nc.vector.tensor_copy(words[:], table[:].bitcast(U32).indirect(listed(h)))
+            picked.append(words)
+        moving = []
+        for h in range(2):
+            parted = held.tile([P, 2, HALF], U16, name=f"parted_{h}", align_bytes=64)
+            nc.vector.tensor_copy(parted[:], picked[h][:].bitcast(U16).rearrange("p (t d) -> p d t", d=2))
+            moving.append([(parted[:, a, :], planes[:, a, h * HALF : (h + 1) * HALF]) for a in range(2)])
+
+        wh_q = [quantize_wh(round_wh(raws))]
+        r_tiles.append(load_r(1))
+        raws = load_wh(1)
+
+        def products(b, h):
+            cols = slice(b * P, (b + 1) * P)
+            g_cols = slice(J + b * P, J + (b + 1) * P)
+            ga = psum.tile([P, HALF], F32, name="ga", tag="ga")
+            nc.tensor.matmul_mx(
+                out=ga[:], lhsT=wg8[:, cols].bitcast(FP8X4), lhsT_scale=planes[:, 0, g_cols],
+                rhs=moving[h][0][0].bitcast(FP4X4), rhs_scale=moving[h][0][1], start=True, stop=False,
+            )
+            nc.tensor.matmul_mx(
+                out=ga[:], lhsT=wg4[:, 2 * b * P : 2 * (b + 1) * P].bitcast(FP4X4), lhsT_scale=planes[:, 1, g_cols],
+                rhs=moving[h][1][0].bitcast(FP4X4), rhs_scale=moving[h][1][1], start=False, stop=True,
+            )
+            ha = psum.tile([P, HALF], F32, name="ha", tag="ha")
+            codes, scales = wh_q[b // 2]
+            for a in range(2):
+                w_cols = slice(a * W_HALF + (b % 2) * P, a * W_HALF + (b % 2 + 1) * P)
+                nc.tensor.matmul_mx(
+                    out=ha[:], lhsT=codes[:, w_cols].bitcast(FP8X4), lhsT_scale=scales[:, w_cols],
+                    rhs=moving[h][a][0].bitcast(FP4X4), rhs_scale=moving[h][a][1], start=(a == 0), stop=(a == 1),
+                )
+            keep = work.tile([P, HALF], F32, name="keep", tag="keep")
+            nc.scalar.activation(keep[:], ga[:], ACT.Sigmoid, bias=neg_bias[:, b : b + 1], scale=-1.0)
+            gate = work.tile([P, HALF], F32, name="gate", tag="gate")
+            nc.scalar.activation(gate[:], ga[:], ACT.Sigmoid, bias=bias[:, b : b + 1])
+            return ha, keep, gate
+
+        def terms(b, h, ha, keep, gate):
+            made = work.tile([P, HALF], F32, name="made", tag="made")
+            nc.vector.scalar_tensor_tensor(made[:], ha[:], 0.0, gate[:], ALU.max, ALU.mult)
+            kept = work.tile([P, HALF], F32, name="kept", tag="kept")
+            nc.vector.tensor_tensor(kept[:], r_tiles[b][:].indirect(listed(h)), keep[:], ALU.mult)
+            return made, kept
+
+        def finish(b, h, made, kept):
+            result = work.tile([P, HALF], F32, name="result", tag="result", bufs=8)
+            nc.vector.tensor_tensor(result[:], made[:], kept[:], ALU.add)
+            nc.sync.dma_start(out[b * P : (b + 1) * P, h * HALF : (h + 1) * HALF], result[:])
+
+        pending = None
+        for b in range(N // P):
+            if b == 1:
+                wh_q.append(quantize_wh(round_wh(raws)))
+            for h in range(2):
+                pair = terms(b, h, *products(b, h))
+                if pending is not None:
+                    finish(*pending)
+                pending = (b, h) + pair
+            if b + 2 < N // P:
+                r_tiles.append(load_r(b + 2))
+        finish(*pending)

@@ -32,7 +32,7 @@ def tile_list_hwayt_mix_relu_kernel(
     nc = tc.nc
     with ExitStack() as ctx:
         held = ctx.enter_context(tc.tile_pool(name="held", bufs=1))
-        windows = ctx.enter_context(tc.tile_pool(name="windows", bufs=2))
+        windows = ctx.enter_context(tc.tile_pool(name="windows", bufs=1))
         stage = ctx.enter_context(tc.tile_pool(name="stage", bufs=2))
         work = ctx.enter_context(tc.tile_pool(name="work", bufs=4))
         psum = ctx.enter_context(tc.psum_pool(name="psum", bufs=4))
@@ -48,7 +48,7 @@ def tile_list_hwayt_mix_relu_kernel(
         nc.vector.memset(tab_sc[32:64, :].bitcast(I32), 0)
         nc.vector.memset(tab_sc[64:128, :].bitcast(I32), 0)
 
-        table = windows.tile([P, T], I32, name="table", tag="window", align_bytes=64)
+        table = windows.tile([P, T], I32, name="table", tag="slot1", align_bytes=64)
         nc.sync.dma_start(table[:], tab_words[0].rearrange("p t b -> p (t b)").bitcast(I32))
 
         warm = held.tile([P, 8], F32, name="warm")
@@ -82,8 +82,8 @@ def tile_list_hwayt_mix_relu_kernel(
                 raws.append(raw)
             return raws
 
-        def round_wh(raws):
-            grouped = stage.tile([P, 2, W_HALF, PACK], BF16, name="grouped", tag="grouped", align_bytes=64)
+        def round_wh(raws, tag):
+            grouped = windows.tile([P, 2, W_HALF, PACK], BF16, name="grouped", tag=tag, align_bytes=64)
             for a in range(2):
                 nc.scalar.copy(
                     grouped[:, a].rearrange("p (c e) i -> p c i e", e=4),
@@ -100,34 +100,36 @@ def tile_list_hwayt_mix_relu_kernel(
             return codes, scales
 
         def load_r(b):
-            carried = windows.tile([P, T], F32, name="carried", tag="window", align_bytes=64)
+            carried = windows.tile([P, T], F32, name="carried", tag=f"slot{b % 3}", align_bytes=64)
             nc.sync.dma_start(carried[:], rT[b * P : (b + 1) * P, :])
             return carried
 
         raws = load_wh(0)
-        r_tiles = [load_r(0)]
 
-        picked_sc = held.tile([P, J], U8, name="picked_sc", align_bytes=64)
+
+        picked_sc = windows.tile([P, J], U8, name="picked_sc", tag="slot0", align_bytes=64)
         nc.vector.tensor_copy(picked_sc[:], tab_sc[:].indirect(offsets[:]))
         nc.vector.tensor_copy(joined[:, 0:J].bitcast(I32), picked_sc[0:SC_ROWS, :].bitcast(I32))
         for q in range(QUADS):
-            nc.scalar.dma_start(
-                planes[32 * q : 32 * q + 4].bitcast(I32), joined[8 * q : 8 * q + 8, :].bitcast(I32)
+            nc.sync.dma_start(
+                planes[32 * q : 32 * q + 4].bitcast(I32), joined[8 * q : 8 * q + 8, :].bitcast(I32),
             )
+        r_tiles = [load_r(0)]
         picked = []
         for h in range(2):
             words = held.tile([P, HALF], U32, name=f"picked_{h}", align_bytes=64)
             nc.vector.tensor_copy(words[:], table[:].bitcast(U32).indirect(listed(h)))
             picked.append(words)
+        r_tiles.append(load_r(1))
         moving = []
         for h in range(2):
             parted = held.tile([P, 2, HALF], U16, name=f"parted_{h}", align_bytes=64)
             nc.vector.tensor_copy(parted[:], picked[h][:].bitcast(U16).rearrange("p (t d) -> p d t", d=2))
             moving.append([(parted[:, a, :], planes[:, a, h * HALF : (h + 1) * HALF]) for a in range(2)])
 
-        wh_q = [quantize_wh(round_wh(raws))]
-        r_tiles.append(load_r(1))
+        wh_q = [quantize_wh(round_wh(raws, "slot2"))]
         raws = load_wh(1)
+        r_tiles.append(load_r(2))
 
         def products(b, h):
             cols = slice(b * P, (b + 1) * P)
@@ -158,24 +160,30 @@ def tile_list_hwayt_mix_relu_kernel(
         def terms(b, h, ha, keep, gate):
             made = work.tile([P, HALF], F32, name="made", tag="made")
             nc.vector.scalar_tensor_tensor(made[:], ha[:], 0.0, gate[:], ALU.max, ALU.mult)
-            kept = work.tile([P, HALF], F32, name="kept", tag="kept")
+            if (b, h) == (1, 1):
+                kept = windows.tile([P, HALF], F32, name="kept", tag="slot3", align_bytes=64)
+            else:
+                kept = work.tile([P, HALF], F32, name="kept", tag="kept")
             nc.vector.tensor_tensor(kept[:], r_tiles[b][:].indirect(listed(h)), keep[:], ALU.mult)
             return made, kept
 
-        def finish(b, h, made, kept):
-            result = work.tile([P, HALF], F32, name="result", tag="result", bufs=8)
-            nc.vector.tensor_tensor(result[:], made[:], kept[:], ALU.add)
-            nc.sync.dma_start(out[b * P : (b + 1) * P, h * HALF : (h + 1) * HALF], result[:])
+        def finish(b, h, made, kept, pieces):
+            width = HALF // pieces
+            for c in range(pieces):
+                cols = slice(c * width, (c + 1) * width)
+                result = work.tile([P, width], F32, name="result", tag="result", bufs=8)
+                nc.vector.tensor_tensor(result[:], made[:, cols], kept[:, cols], ALU.add)
+                first = h * HALF + c * width
+                nc.sync.dma_start(out[b * P : (b + 1) * P, first : first + width], result[:])
 
+        units = [(b, h) for b in range(N // P) for h in range(2)]
         pending = None
-        for b in range(N // P):
-            if b == 1:
-                wh_q.append(quantize_wh(round_wh(raws)))
-            for h in range(2):
-                pair = terms(b, h, *products(b, h))
-                if pending is not None:
-                    finish(*pending)
-                pending = (b, h) + pair
-            if b + 2 < N // P:
-                r_tiles.append(load_r(b + 2))
-        finish(*pending)
+        for u, (b, h) in enumerate(units):
+            if u == 2:
+                wh_q.append(quantize_wh(round_wh(raws, "slot3")))
+                r_tiles.append(load_r(3))
+            pair = terms(b, h, *products(b, h))
+            if pending is not None:
+                finish(*pending, 1)
+            pending = (b, h) + pair
+        finish(*pending, 2)

@@ -1,6 +1,7 @@
 from contextlib import ExitStack
 
 import concourse.mybir as mybir
+from concourse.masks import make_identity
 
 K, N, T, J = 1024, 512, 2048, 1024
 FLOPS = 2 * 2 * K * N * J
@@ -24,6 +25,7 @@ HALF = 512
 LIST_COLS = HALF // 16
 W_HALF = N // 2
 SC_ROWS = 32
+TENSOR_SUMS = range(2, 6)
 
 
 def tile_list_hwayt_mix_relu_kernel(
@@ -34,7 +36,7 @@ def tile_list_hwayt_mix_relu_kernel(
         held = ctx.enter_context(tc.tile_pool(name="held", bufs=1))
         windows = ctx.enter_context(tc.tile_pool(name="windows", bufs=1))
         stage = ctx.enter_context(tc.tile_pool(name="stage", bufs=2))
-        work = ctx.enter_context(tc.tile_pool(name="work", bufs=4))
+        work = ctx.enter_context(tc.tile_pool(name="work", bufs=8))
         psum = ctx.enter_context(tc.psum_pool(name="psum", bufs=4))
 
         offsets = held.tile([P, J // 16], U16, name="offsets")
@@ -61,11 +63,6 @@ def tile_list_hwayt_mix_relu_kernel(
         nc.sync.dma_start(joined[1:SC_ROWS:2, J:].bitcast(I32), wg4_scales[0].bitcast(I32))
         planes = held.tile([P, 2, J + N], U8, name="planes", align_bytes=64)
         nc.gpsimd.memset(planes[:].rearrange("p a c -> p (a c)").bitcast(I32), 0)
-
-        wg8 = held.tile([P, N], I32, name="wg8", align_bytes=64)
-        nc.sync.dma_start(wg8[:], wg8_words[0].rearrange("p n b -> p (n b)").bitcast(I32))
-        wg4 = held.tile([P, 2 * N], U8, name="wg4", align_bytes=64)
-        nc.sync.dma_start(wg4[:].bitcast(I32), wg4_words[0].bitcast(I32))
 
         bias = held.tile([P, N // P], F32, name="bias")
         with nc.allow_non_contiguous_dma(reason="one bias value for each partition and block"):
@@ -94,9 +91,13 @@ def tile_list_hwayt_mix_relu_kernel(
         def quantize_wh(grouped):
             codes = stage.tile([P, 2 * W_HALF], U32, name="codes", tag="codes", align_bytes=64)
             scales = stage.tile([P, 2 * W_HALF], U8, name="scales", tag="scales", align_bytes=64)
-            nc.vector.quantize_mx(
-                out=codes[:].bitcast(FP8X4), scales=scales[:], in_=grouped[:].rearrange("p a n i -> p (a n i)")
-            )
+            for a in range(2):
+                cols = slice(a * W_HALF, (a + 1) * W_HALF)
+                nc.vector.quantize_mx(
+                    out=codes[:, cols].bitcast(FP8X4),
+                    scales=scales[:, cols],
+                    in_=grouped[:, a].rearrange("p n i -> p (n i)"),
+                )
             return codes, scales
 
         def load_r(b):
@@ -105,6 +106,13 @@ def tile_list_hwayt_mix_relu_kernel(
             return carried
 
         raws = load_wh(0)
+        wg8 = held.tile([P, N], I32, name="wg8", align_bytes=64)
+        nc.sync.dma_start(wg8[:], wg8_words[0].rearrange("p n b -> p (n b)").bitcast(I32))
+        wg4 = held.tile([P, 2 * N], U8, name="wg4", align_bytes=64)
+        nc.sync.dma_start(wg4[:].bitcast(I32), wg4_words[0].bitcast(I32))
+
+        ident = held.tile([P, P], F32, name="ident")
+        make_identity(nc, ident[:])
 
 
         picked_sc = windows.tile([P, J], U8, name="picked_sc", tag="slot0", align_bytes=64)
@@ -115,18 +123,15 @@ def tile_list_hwayt_mix_relu_kernel(
                 planes[32 * q : 32 * q + 4].bitcast(I32), joined[8 * q : 8 * q + 8, :].bitcast(I32),
             )
         r_tiles = [load_r(0)]
-        picked = []
-        for h in range(2):
-            words = held.tile([P, HALF], U32, name=f"picked_{h}", align_bytes=64)
-            nc.vector.tensor_copy(words[:], table[:].bitcast(U32).indirect(listed(h)))
-            picked.append(words)
-        r_tiles.append(load_r(1))
         moving = []
         for h in range(2):
+            picked = held.tile([P, HALF], U32, name="picked", tag="picked", align_bytes=64)
+            nc.vector.tensor_copy(picked[:], table[:].bitcast(U32).indirect(listed(h)))
             parted = held.tile([P, 2, HALF], U16, name=f"parted_{h}", align_bytes=64)
-            nc.vector.tensor_copy(parted[:], picked[h][:].bitcast(U16).rearrange("p (t d) -> p d t", d=2))
+            nc.vector.tensor_copy(parted[:], picked[:].bitcast(U16).rearrange("p (t d) -> p d t", d=2))
             moving.append([(parted[:, a, :], planes[:, a, h * HALF : (h + 1) * HALF]) for a in range(2)])
 
+        r_tiles.append(load_r(1))
         wh_q = [quantize_wh(round_wh(raws, "slot2"))]
         raws = load_wh(1)
         r_tiles.append(load_r(2))
@@ -151,10 +156,10 @@ def tile_list_hwayt_mix_relu_kernel(
                     out=ha[:], lhsT=codes[:, w_cols].bitcast(FP8X4), lhsT_scale=scales[:, w_cols],
                     rhs=moving[h][a][0].bitcast(FP4X4), rhs_scale=moving[h][a][1], start=(a == 0), stop=(a == 1),
                 )
-            keep = work.tile([P, HALF], F32, name="keep", tag="keep")
-            nc.scalar.activation(keep[:], ga[:], ACT.Sigmoid, bias=neg_bias[:, b : b + 1], scale=-1.0)
             gate = work.tile([P, HALF], F32, name="gate", tag="gate")
             nc.scalar.activation(gate[:], ga[:], ACT.Sigmoid, bias=bias[:, b : b + 1])
+            keep = work.tile([P, HALF], F32, name="keep", tag="keep")
+            nc.scalar.activation(keep[:], ga[:], ACT.Sigmoid, bias=neg_bias[:, b : b + 1], scale=-1.0)
             return ha, keep, gate
 
         def terms(b, h, ha, keep, gate):
@@ -176,14 +181,39 @@ def tile_list_hwayt_mix_relu_kernel(
                 first = h * HALF + c * width
                 nc.sync.dma_start(out[b * P : (b + 1) * P, first : first + width], result[:])
 
+        def turned_sum(made, kept):
+            acc = psum.tile([P, HALF], F32, name="acc", tag="ga")
+            for c in range(HALF // P):
+                cols = slice(c * P, (c + 1) * P)
+                nc.tensor.matmul(acc[:, cols], made[:, cols], ident[:], start=True, stop=False, is_transpose=True)
+                nc.tensor.matmul(acc[:, cols], kept[:, cols], ident[:], start=False, stop=True, is_transpose=True)
+            turned = work.tile([P, HALF], F32, name="turned", tag="turned")
+            nc.scalar.copy(turned[:], acc[:])
+            return turned
+
+        def turn_back(b, h, turned):
+            back = psum.tile([P, HALF], F32, name="back", tag="ga")
+            for c in range(HALF // P):
+                cols = slice(c * P, (c + 1) * P)
+                nc.tensor.transpose(back[:, cols], turned[:, cols], ident[:])
+            result = work.tile([P, HALF], F32, name="result", tag="summed", bufs=4)
+            nc.scalar.copy(result[:], back[:])
+            nc.scalar.dma_start(out[b * P : (b + 1) * P, h * HALF : (h + 1) * HALF], result[:])
+
         units = [(b, h) for b in range(N // P) for h in range(2)]
-        pending = None
+        pairs = []
         for u, (b, h) in enumerate(units):
             if u == 2:
                 wh_q.append(quantize_wh(round_wh(raws, "slot3")))
                 r_tiles.append(load_r(3))
-            pair = terms(b, h, *products(b, h))
-            if pending is not None:
-                finish(*pending, 1)
-            pending = (b, h) + pair
-        finish(*pending, 2)
+            pairs.append(terms(b, h, *products(b, h)))
+            if u > 0 and u - 1 not in TENSOR_SUMS:
+                finish(*units[u - 1], *pairs[u - 1], 1)
+        finish(*units[-1], *pairs[-1], 2)
+        waiting = None
+        for u in TENSOR_SUMS:
+            turned = turned_sum(*pairs[u])
+            if waiting is not None:
+                turn_back(*waiting)
+            waiting = (*units[u], turned)
+        turn_back(*waiting)

@@ -66,7 +66,7 @@ def tile_list_hwayt_mix_relu_kernel(
 
         bias = held.tile([P, N // P], F32, name="bias")
         with nc.allow_non_contiguous_dma(reason="one bias value for each partition and block"):
-            nc.sync.dma_start(bias[:], bg.rearrange("(b p) -> p b", p=P))
+            nc.scalar.dma_start(bias[:], bg.rearrange("(b p) -> p b", p=P))
         neg_bias = held.tile([P, N // P], F32, name="neg_bias")
         nc.gpsimd.tensor_scalar(neg_bias[:], bias[:], -1.0, 0.0, ALU.mult, ALU.add)
 
@@ -181,6 +181,13 @@ def tile_list_hwayt_mix_relu_kernel(
                 first = h * HALF + c * width
                 nc.sync.dma_start(out[b * P : (b + 1) * P, first : first + width], result[:])
 
+        def gpsimd_sum(b, h, made, kept):
+            result = work.tile([P, HALF], F32, name="result", tag="result", bufs=8)
+            for c in range(2):
+                cols = slice(c * HALF // 2, (c + 1) * HALF // 2)
+                nc.gpsimd.tensor_tensor(result[:, cols], made[:, cols], kept[:, cols], ALU.add)
+            nc.sync.dma_start(out[b * P : (b + 1) * P, h * HALF : (h + 1) * HALF], result[:])
+
         def turned_sum(made, kept):
             acc = psum.tile([P, HALF], F32, name="acc", tag="ga")
             for c in range(HALF // P):
@@ -207,7 +214,9 @@ def tile_list_hwayt_mix_relu_kernel(
                 wh_q.append(quantize_wh(round_wh(raws, "slot3")))
                 r_tiles.append(load_r(3))
             pairs.append(terms(b, h, *products(b, h)))
-            if u > 0 and u - 1 not in TENSOR_SUMS:
+            if u < TENSOR_SUMS.start:
+                gpsimd_sum(*units[u], *pairs[u])
+            if u - 1 >= TENSOR_SUMS.stop:
                 finish(*units[u - 1], *pairs[u - 1], 1)
         finish(*units[-1], *pairs[-1], 2)
         waiting = None

@@ -25,7 +25,6 @@ HALF = 512
 LIST_COLS = HALF // 16
 W_HALF = N // 2
 SC_ROWS = 32
-TENSOR_SUMS = range(2, 6)
 
 
 def tile_list_hwayt_mix_relu_kernel(
@@ -34,23 +33,31 @@ def tile_list_hwayt_mix_relu_kernel(
     nc = tc.nc
     with ExitStack() as ctx:
         held = ctx.enter_context(tc.tile_pool(name="held", bufs=1))
-        windows = ctx.enter_context(tc.tile_pool(name="windows", bufs=1))
-        stage = ctx.enter_context(tc.tile_pool(name="stage", bufs=2))
         work = ctx.enter_context(tc.tile_pool(name="work", bufs=8))
-        psum = ctx.enter_context(tc.psum_pool(name="psum", bufs=4))
+        psum = ctx.enter_context(tc.psum_pool(name="psum", bufs=1))
 
         offsets = held.tile([P, J // 16], U16, name="offsets")
         nc.sync.dma_start(offsets[:], offs)
 
-        def listed(h):
-            return offsets[:, h * LIST_COLS : (h + 1) * LIST_COLS]
+        def listed(first, count):
+            return offsets[:, first // 16 : (first + count) // 16]
+
+        def half(h):
+            return slice(h * HALF, (h + 1) * HALF)
 
         tab_sc = held.tile([P, T], U8, name="tab_sc", align_bytes=64)
         nc.sync.dma_start(tab_sc[0:SC_ROWS, :].bitcast(I32), tab_scales.rearrange("a q t -> q a t").bitcast(I32))
         nc.vector.memset(tab_sc[32:64, :].bitcast(I32), 0)
         nc.vector.memset(tab_sc[64:128, :].bitcast(I32), 0)
 
-        table = windows.tile([P, T], I32, name="table", tag="slot1", align_bytes=64)
+        joined = held.tile([SC_ROWS, J + N], U8, name="joined", align_bytes=64)
+        nc.sync.dma_start(joined[0:SC_ROWS:2, J:].bitcast(I32), wg8_scales[0].bitcast(I32))
+        nc.sync.dma_start(joined[1:SC_ROWS:2, J:].bitcast(I32), wg4_scales[0].bitcast(I32))
+        planes = held.tile([P, 2, J + N], U8, name="planes", align_bytes=64)
+        wg4 = held.tile([P, 2 * N], U8, name="wg4", align_bytes=64)
+        nc.sync.dma_start(wg4[:].bitcast(I32), wg4_words[0].bitcast(I32))
+
+        table = held.tile([P, T], I32, name="table", tag="after_words", align_bytes=64)
         nc.sync.dma_start(table[:], tab_words[0].rearrange("p t b -> p (t b)").bitcast(I32))
 
         warm = held.tile([P, 8], F32, name="warm")
@@ -58,88 +65,99 @@ def tile_list_hwayt_mix_relu_kernel(
         nc.gpsimd.memset(warm[:], 0.0)
         nc.scalar.activation(warm_out[:], warm[:], ACT.Sigmoid)
 
-        joined = held.tile([SC_ROWS, J + N], U8, name="joined", align_bytes=64)
-        nc.sync.dma_start(joined[0:SC_ROWS:2, J:].bitcast(I32), wg8_scales[0].bitcast(I32))
-        nc.sync.dma_start(joined[1:SC_ROWS:2, J:].bitcast(I32), wg4_scales[0].bitcast(I32))
-        planes = held.tile([P, 2, J + N], U8, name="planes", align_bytes=64)
-        nc.gpsimd.memset(planes[:].rearrange("p a c -> p (a c)").bitcast(I32), 0)
-
         bias = held.tile([P, N // P], F32, name="bias")
         with nc.allow_non_contiguous_dma(reason="one bias value for each partition and block"):
-            nc.scalar.dma_start(bias[:], bg.rearrange("(b p) -> p b", p=P))
+            nc.gpsimd.dma_start(bias[:], bg.rearrange("(b p) -> p b", p=P))
+        ident = held.tile([P, P], F32, name="ident")
+        make_identity(nc, ident[:])
         neg_bias = held.tile([P, N // P], F32, name="neg_bias")
         nc.gpsimd.tensor_scalar(neg_bias[:], bias[:], -1.0, 0.0, ALU.mult, ALU.add)
 
-        def load_wh(w):
-            raws = []
-            for a in range(2):
-                raw = stage.tile([P, PACK, W_HALF], F32, name="raw", tag="raw")
-                rows = wh[a * K_PASS : (a + 1) * K_PASS, w * W_HALF : (w + 1) * W_HALF]
-                nc.sync.dma_start(raw[:], rows.rearrange("(p i) n -> p i n", i=PACK))
-                raws.append(raw)
-            return raws
+        raws = {}
+        wh_q = {}
+        r_tiles = {}
 
-        def round_wh(raws, tag):
-            grouped = windows.tile([P, 2, W_HALF, PACK], BF16, name="grouped", tag=tag, align_bytes=64)
-            for a in range(2):
+        def load_wh(w, a, tag):
+            raw = held.tile([P, PACK, W_HALF], F32, name=f"raw_{w}{a}", tag=tag, align_bytes=64)
+            rows = wh[a * K_PASS : (a + 1) * K_PASS, w * W_HALF : (w + 1) * W_HALF]
+            nc.sync.dma_start(raw[:], rows.rearrange("(p i) n -> p i n", i=PACK))
+            raws[w, a] = raw
+
+        def round_wh(w, a, grouped):
+            if w == 1:
                 nc.scalar.copy(
-                    grouped[:, a].rearrange("p (c e) i -> p c i e", e=4),
-                    raws[a][:].rearrange("p i (c e) -> p c i e", e=4),
+                    grouped.rearrange("p (c e) i -> p c i e", e=4),
+                    raws[w, a][:].rearrange("p i (c e) -> p c i e", e=4),
                 )
-            return grouped
+            else:
+                for cols, sign in ((slice(0, P), 1.0), (slice(P, 2 * P), -1.0)):
+                    nc.scalar.activation(
+                        grouped[:, cols, :].rearrange("p (c e) i -> p c i e", e=4),
+                        raws[w, a][:, :, cols].rearrange("p i (c e) -> p c i e", e=4),
+                        ACT.Copy,
+                        scale=sign,
+                    )
 
-        def quantize_wh(grouped):
-            codes = stage.tile([P, 2 * W_HALF], U32, name="codes", tag="codes", align_bytes=64)
-            scales = stage.tile([P, 2 * W_HALF], U8, name="scales", tag="scales", align_bytes=64)
-            for a in range(2):
-                cols = slice(a * W_HALF, (a + 1) * W_HALF)
-                nc.vector.quantize_mx(
-                    out=codes[:, cols].bitcast(FP8X4),
-                    scales=scales[:, cols],
-                    in_=grouped[:, a].rearrange("p n i -> p (n i)"),
-                )
-            return codes, scales
+        def quantize_wh(w, passes, tag=None):
+            name = f"{w}{passes[-1]}"
+            width = len(passes) * W_HALF
+            grouped = held.tile([P, width, PACK], BF16, name=f"grouped_{name}", tag=f"after_quantise_{name}", align_bytes=64)
+            for place, a in enumerate(passes):
+                round_wh(w, a, grouped[:, place * W_HALF : (place + 1) * W_HALF, :])
+            codes = held.tile([P, width], U32, name=f"codes_{name}", tag=tag or f"codes_{name}", align_bytes=64)
+            scales = held.tile([P, width], U8, name=f"scales_{name}", align_bytes=64)
+            nc.vector.quantize_mx(
+                out=codes[:].bitcast(FP8X4), scales=scales[:], in_=grouped[:].rearrange("p n i -> p (n i)")
+            )
+            for place, a in enumerate(passes):
+                cols = slice(place * W_HALF, (place + 1) * W_HALF)
+                wh_q[w, a] = (codes[:, cols], scales[:, cols])
 
-        def load_r(b):
-            carried = windows.tile([P, T], F32, name="carried", tag=f"slot{b % 3}", align_bytes=64)
+        def load_r(b, tag):
+            carried = held.tile([P, T], F32, name=f"carried_{b}", tag=tag, align_bytes=64)
             nc.sync.dma_start(carried[:], rT[b * P : (b + 1) * P, :])
-            return carried
+            r_tiles[b] = carried
 
-        raws = load_wh(0)
+        load_wh(0, 0, "raw_00")
+        load_wh(0, 1, "raw_01")
         wg8 = held.tile([P, N], I32, name="wg8", align_bytes=64)
         nc.sync.dma_start(wg8[:], wg8_words[0].rearrange("p n b -> p (n b)").bitcast(I32))
-        wg4 = held.tile([P, 2 * N], U8, name="wg4", align_bytes=64)
-        nc.sync.dma_start(wg4[:].bitcast(I32), wg4_words[0].bitcast(I32))
 
-        ident = held.tile([P, P], F32, name="ident")
-        make_identity(nc, ident[:])
-
-
-        picked_sc = windows.tile([P, J], U8, name="picked_sc", tag="slot0", align_bytes=64)
+        picked_sc = held.tile([P, J], U8, name="picked_sc", tag="after_join", align_bytes=64)
         nc.vector.tensor_copy(picked_sc[:], tab_sc[:].indirect(offsets[:]))
         nc.vector.tensor_copy(joined[:, 0:J].bitcast(I32), picked_sc[0:SC_ROWS, :].bitcast(I32))
         for q in range(QUADS):
-            nc.sync.dma_start(
-                planes[32 * q : 32 * q + 4].bitcast(I32), joined[8 * q : 8 * q + 8, :].bitcast(I32),
-            )
-        r_tiles = [load_r(0)]
+            nc.sync.dma_start(planes[32 * q : 32 * q + 4].bitcast(I32), joined[8 * q : 8 * q + 8, :].bitcast(I32))
+        load_r(0, "after_join")
+
+        picked = held.tile([P, J], U32, name="picked", tag="after_parting", align_bytes=64)
+        nc.vector.tensor_copy(picked[:], table[:].bitcast(U32).indirect(offsets[:]))
         moving = []
         for h in range(2):
-            picked = held.tile([P, HALF], U32, name="picked", tag="picked", align_bytes=64)
-            nc.vector.tensor_copy(picked[:], table[:].bitcast(U32).indirect(listed(h)))
             parted = held.tile([P, 2, HALF], U16, name=f"parted_{h}", align_bytes=64)
-            nc.vector.tensor_copy(parted[:], picked[:].bitcast(U16).rearrange("p (t d) -> p d t", d=2))
-            moving.append([(parted[:, a, :], planes[:, a, h * HALF : (h + 1) * HALF]) for a in range(2)])
+            nc.vector.tensor_copy(parted[:], picked[:, half(h)].bitcast(U16).rearrange("p (t d) -> p d t", d=2))
+            moving.append([(parted[:, a, :], planes[:, a, half(h)]) for a in range(2)])
+        load_r(2, "after_words")
+        load_wh(1, 0, "after_parting")
 
-        r_tiles.append(load_r(1))
-        wh_q = [quantize_wh(round_wh(raws, "slot2"))]
-        raws = load_wh(1)
-        r_tiles.append(load_r(2))
+        def unit_tile(kind, b, h, tag=None):
+            name = f"{kind}_{b}{h}"
+            return held.tile([P, HALF], F32, name=name, tag=tag or name, align_bytes=64)
 
-        def products(b, h):
+        gates = {}
+        keeps = {}
+
+        def bank(name, number):
+            return psum.tile([P, HALF], F32, name=name, tag=f"bank_{number}")
+
+        gate_banks = {0: 0, 2: 2, 1: 6, 3: 0}
+        feature_banks = {0: 4, 2: 4, 3: 6, 1: 2}
+        sum_banks = [0, 1, 4, 5, 6, 7]
+
+        def gate_product(b, h):
             cols = slice(b * P, (b + 1) * P)
             g_cols = slice(J + b * P, J + (b + 1) * P)
-            ga = psum.tile([P, HALF], F32, name="ga", tag="ga")
+            ga = bank("ga", gate_banks[b] + h)
             nc.tensor.matmul_mx(
                 out=ga[:], lhsT=wg8[:, cols].bitcast(FP8X4), lhsT_scale=planes[:, 0, g_cols],
                 rhs=moving[h][0][0].bitcast(FP4X4), rhs_scale=moving[h][0][1], start=True, stop=False,
@@ -148,81 +166,123 @@ def tile_list_hwayt_mix_relu_kernel(
                 out=ga[:], lhsT=wg4[:, 2 * b * P : 2 * (b + 1) * P].bitcast(FP4X4), lhsT_scale=planes[:, 1, g_cols],
                 rhs=moving[h][1][0].bitcast(FP4X4), rhs_scale=moving[h][1][1], start=False, stop=True,
             )
-            ha = psum.tile([P, HALF], F32, name="ha", tag="ha")
-            codes, scales = wh_q[b // 2]
+            return ga
+
+        def keep_of(b, h, place=None):
+            keeps[b, h] = unit_tile("keep", b, h)[:] if place is None else place
+            nc.scalar.activation(keeps[b, h], banks[b, h][:], ACT.Sigmoid, bias=neg_bias[:, b : b + 1], scale=-1.0)
+
+        def gate_of(b, h, place=None):
+            gates[b, h] = unit_tile("gate", b, h)[:] if place is None else place
+            nc.scalar.activation(gates[b, h], banks[b, h][:], ACT.Sigmoid, bias=bias[:, b : b + 1])
+
+        def feature_product(b, h):
+            ha = bank("ha", feature_banks[b] + h)
+            w_cols = slice((b % 2) * P, (b % 2 + 1) * P)
             for a in range(2):
-                w_cols = slice(a * W_HALF + (b % 2) * P, a * W_HALF + (b % 2 + 1) * P)
+                codes, scales = wh_q[b // 2, a]
                 nc.tensor.matmul_mx(
                     out=ha[:], lhsT=codes[:, w_cols].bitcast(FP8X4), lhsT_scale=scales[:, w_cols],
                     rhs=moving[h][a][0].bitcast(FP4X4), rhs_scale=moving[h][a][1], start=(a == 0), stop=(a == 1),
                 )
-            gate = work.tile([P, HALF], F32, name="gate", tag="gate")
-            nc.scalar.activation(gate[:], ga[:], ACT.Sigmoid, bias=bias[:, b : b + 1])
-            keep = work.tile([P, HALF], F32, name="keep", tag="keep")
-            nc.scalar.activation(keep[:], ga[:], ACT.Sigmoid, bias=neg_bias[:, b : b + 1], scale=-1.0)
-            return ha, keep, gate
+            return ha
 
-        def terms(b, h, ha, keep, gate):
-            made = work.tile([P, HALF], F32, name="made", tag="made")
-            nc.vector.scalar_tensor_tensor(made[:], ha[:], 0.0, gate[:], ALU.max, ALU.mult)
-            if (b, h) == (1, 1):
-                kept = windows.tile([P, HALF], F32, name="kept", tag="slot3", align_bytes=64)
-            else:
-                kept = work.tile([P, HALF], F32, name="kept", tag="kept")
-            nc.vector.tensor_tensor(kept[:], r_tiles[b][:].indirect(listed(h)), keep[:], ALU.mult)
-            return made, kept
+        def made_term(b, h, made):
+            nc.vector.scalar_tensor_tensor(made, feature_product(b, h)[:], 0.0, gates[b, h], ALU.max, ALU.mult)
 
-        def finish(b, h, made, kept, pieces):
-            width = HALF // pieces
-            for c in range(pieces):
-                cols = slice(c * width, (c + 1) * width)
-                result = work.tile([P, width], F32, name="result", tag="result", bufs=8)
-                nc.vector.tensor_tensor(result[:], made[:, cols], kept[:, cols], ALU.add)
-                first = h * HALF + c * width
-                nc.sync.dma_start(out[b * P : (b + 1) * P, first : first + width], result[:])
+        def kept_term(b, h, place=None):
+            kept = unit_tile("kept", b, h) if place is None else place
+            nc.vector.tensor_tensor(kept[:], r_tiles[b][:].indirect(listed(h * HALF, HALF)), keeps[b, h], ALU.mult)
+            return kept[:]
 
-        def gpsimd_sum(b, h, made, kept):
-            result = work.tile([P, HALF], F32, name="result", tag="result", bufs=8)
-            for c in range(2):
-                cols = slice(c * HALF // 2, (c + 1) * HALF // 2)
-                nc.gpsimd.tensor_tensor(result[:, cols], made[:, cols], kept[:, cols], ALU.add)
-            nc.sync.dma_start(out[b * P : (b + 1) * P, h * HALF : (h + 1) * HALF], result[:])
+        def store(b, cols, result):
+            nc.sync.dma_start(out[b * P : (b + 1) * P, cols], result)
 
-        def turned_sum(made, kept):
-            acc = psum.tile([P, HALF], F32, name="acc", tag="ga")
+        def turned_sum(b, h, one, other):
+            acc = bank("acc", sum_banks.pop(0))
             for c in range(HALF // P):
                 cols = slice(c * P, (c + 1) * P)
-                nc.tensor.matmul(acc[:, cols], made[:, cols], ident[:], start=True, stop=False, is_transpose=True)
-                nc.tensor.matmul(acc[:, cols], kept[:, cols], ident[:], start=False, stop=True, is_transpose=True)
-            turned = work.tile([P, HALF], F32, name="turned", tag="turned")
+                nc.tensor.matmul(acc[:, cols], one[:, cols], ident[:], start=True, stop=False, is_transpose=True)
+                nc.tensor.matmul(acc[:, cols], other[:, cols], ident[:], start=False, stop=True, is_transpose=True)
+            turned = unit_tile("turned", b, h)
             nc.scalar.copy(turned[:], acc[:])
-            return turned
+            return b, h, turned
 
         def turn_back(b, h, turned):
-            back = psum.tile([P, HALF], F32, name="back", tag="ga")
+            back = bank("back", sum_banks.pop(0))
             for c in range(HALF // P):
                 cols = slice(c * P, (c + 1) * P)
                 nc.tensor.transpose(back[:, cols], turned[:, cols], ident[:])
-            result = work.tile([P, HALF], F32, name="result", tag="summed", bufs=4)
+            result = work.tile([P, HALF], F32, name="result", tag="result")
             nc.scalar.copy(result[:], back[:])
-            nc.scalar.dma_start(out[b * P : (b + 1) * P, h * HALF : (h + 1) * HALF], result[:])
+            store(b, half(h), result[:])
 
-        units = [(b, h) for b in range(N // P) for h in range(2)]
-        pairs = []
-        for u, (b, h) in enumerate(units):
-            if u == 2:
-                wh_q.append(quantize_wh(round_wh(raws, "slot3")))
-                r_tiles.append(load_r(3))
-            pairs.append(terms(b, h, *products(b, h)))
-            if u < TENSOR_SUMS.start:
-                gpsimd_sum(*units[u], *pairs[u])
-            if u - 1 >= TENSOR_SUMS.stop:
-                finish(*units[u - 1], *pairs[u - 1], 1)
-        finish(*units[-1], *pairs[-1], 2)
+        def gpsimd_sum(b, h, place=None):
+            result = unit_tile("summed", b, h)[:] if place is None else place
+            nc.gpsimd.tensor_tensor(result, mades[b, h], kepts[b, h], ALU.add)
+            store(b, half(h), result)
+
+        def raw_made_term(b, h, made):
+            nc.vector.scalar_tensor_tensor(made, keeps[b, h], 1.0, feature_product(b, h)[:], ALU.subtract, ALU.mult)
+
+        mades = {}
+        kepts = {}
+        quantize_wh(0, (0,))
+        load_wh(1, 1, "after_quantise_00")
+        quantize_wh(0, (1,))
+        load_r(3, "after_quantise_01")
+        banks = {(b, h): gate_product(b, h) for b in (0, 2, 1) for h in range(2)}
+        for b in (0, 2):
+            for h in range(2):
+                keep_of(b, h)
+        for h in range(2):
+            gate_of(0, h)
+        for h in range(2):
+            kepts[0, h] = kept_term(0, h)
+        load_r(1, "after_join")
+        for h in range(2):
+            kepts[2, h] = kept_term(2, h)
+        for h in range(2):
+            mades[0, h] = unit_tile("made", 0, h)[:]
+            made_term(0, h, mades[0, h])
+        quantize_wh(1, (0, 1))
+        for h in range(2):
+            banks[3, h] = gate_product(3, h)
+        keep_of(3, 0, unit_tile("keep", 3, 0, "after_parting")[:])
+        late_keeps = held.tile([P, 3 * HALF], F32, name="late_keeps", tag="after_quantise_00", align_bytes=64)
+        keep_of(3, 1, late_keeps[:, half(0)])
+        for h in range(2):
+            keep_of(1, h, late_keeps[:, half(1 + h)])
+        gates_2 = held.tile([P, J], F32, name="gates_2", tag="after_quantise_11", align_bytes=64)
+        for h in range(2):
+            gate_of(2, h, gates_2[:, half(h)])
+        for h in range(2):
+            kepts[3, h] = kept_term(3, h)
+        gates_3 = held.tile([P, J], F32, name="gates_3", tag="after_parting", align_bytes=64)
+        for h in range(2):
+            gate_of(3, h, gates_3[:, half(h)])
+        late_mades = held.tile([P, 3 * J + HALF], F32, name="late_mades", tag="after_quantise_01", align_bytes=64)
+        gpsimd_sum(0, 0, late_mades[:, half(6)])
+        for place, b in enumerate((2, 3, 1)):
+            for h in range(2):
+                mades[b, h] = late_mades[:, half(2 * place + h)]
+                (raw_made_term if b == 1 else made_term)(b, h, mades[b, h])
+        gpsimd_sum(2, 1)
+        gpsimd_sum(3, 1)
+        kept_1 = held.tile([P, J], F32, name="kept_1", tag="after_parting", align_bytes=64)
+        for h in range(2):
+            kepts[1, h] = kept_term(1, h, kept_1[:, half(h)])
+
         waiting = None
-        for u in TENSOR_SUMS:
-            turned = turned_sum(*pairs[u])
+        for b, h in ((0, 1), (2, 0), (3, 0)):
+            turned = turned_sum(b, h, mades[b, h], kepts[b, h])
             if waiting is not None:
                 turn_back(*waiting)
-            waiting = (*units[u], turned)
+            waiting = turned
         turn_back(*waiting)
+
+        for h, first, width in ((0, 0, HALF), (1, 0, HALF // 2), (1, HALF // 2, HALF // 2)):
+            cols = slice(first, first + width)
+            result = work.tile([P, width], F32, name="result", tag="result")
+            nc.vector.scalar_tensor_tensor(result[:], mades[1, h][:, cols], 0.0, kepts[1, h][:, cols], ALU.max, ALU.add)
+            store(1, slice(h * HALF + first, h * HALF + first + width), result[:])

@@ -25,6 +25,7 @@ HALF = 512
 LIST_COLS = HALF // 16
 W_HALF = N // 2
 SC_ROWS = 32
+GPSIMD_LAST = 384
 
 
 def tile_list_hwayt_mix_relu_kernel(
@@ -34,6 +35,7 @@ def tile_list_hwayt_mix_relu_kernel(
     with ExitStack() as ctx:
         held = ctx.enter_context(tc.tile_pool(name="held", bufs=1))
         work = ctx.enter_context(tc.tile_pool(name="work", bufs=8))
+        laid = ctx.enter_context(tc.tile_pool(name="laid", bufs=1))
         psum = ctx.enter_context(tc.psum_pool(name="psum", bufs=1))
 
         offsets = held.tile([P, J // 16], U16, name="offsets")
@@ -46,7 +48,7 @@ def tile_list_hwayt_mix_relu_kernel(
             return slice(h * HALF, (h + 1) * HALF)
 
         tab_sc = held.tile([P, T], U8, name="tab_sc", align_bytes=64)
-        nc.sync.dma_start(tab_sc[0:SC_ROWS, :].bitcast(I32), tab_scales.rearrange("a q t -> q a t").bitcast(I32))
+        nc.scalar.dma_start(tab_sc[0:SC_ROWS, :].bitcast(I32), tab_scales.rearrange("a q t -> q a t").bitcast(I32))
         nc.vector.memset(tab_sc[32:64, :].bitcast(I32), 0)
         nc.vector.memset(tab_sc[64:128, :].bitcast(I32), 0)
 
@@ -65,20 +67,27 @@ def tile_list_hwayt_mix_relu_kernel(
         nc.gpsimd.memset(warm[:], 0.0)
         nc.scalar.activation(warm_out[:], warm[:], ACT.Sigmoid)
 
-        bias = held.tile([P, N // P], F32, name="bias")
-        with nc.allow_non_contiguous_dma(reason="one bias value for each partition and block"):
-            nc.gpsimd.dma_start(bias[:], bg.rearrange("(b p) -> p b", p=P))
         ident = held.tile([P, P], F32, name="ident")
         make_identity(nc, ident[:])
+        bias_rows = held.tile([P, P], F32, name="bias_rows")
+        nc.gpsimd.memset(bias_rows[:], 0.0)
+        nc.gpsimd.dma_start(bias_rows[0 : N // P, :], bg.rearrange("(b p) -> b p", p=P))
+        bias_bank = psum.tile([P, P], F32, name="bias_bank", tag="bank_7")
+        nc.tensor.transpose(bias_bank[:], bias_rows[:], ident[:])
+        bias = held.tile([P, N // P], F32, name="bias")
+        nc.scalar.copy(bias[:], bias_bank[:, 0 : N // P])
         neg_bias = held.tile([P, N // P], F32, name="neg_bias")
-        nc.gpsimd.tensor_scalar(neg_bias[:], bias[:], -1.0, 0.0, ALU.mult, ALU.add)
+        nc.scalar.activation(neg_bias[:], bias_bank[:, 0 : N // P], ACT.Copy, scale=-1.0)
 
         raws = {}
         wh_q = {}
         r_tiles = {}
 
         def load_wh(w, a, tag):
-            raw = held.tile([P, PACK, W_HALF], F32, name=f"raw_{w}{a}", tag=tag, align_bytes=64)
+            if tag is None:
+                raw = laid.tile([P, PACK, W_HALF], F32, name=f"raw_{w}{a}", offset=3072, align_bytes=64)
+            else:
+                raw = held.tile([P, PACK, W_HALF], F32, name=f"raw_{w}{a}", tag=tag, align_bytes=64)
             rows = wh[a * K_PASS : (a + 1) * K_PASS, w * W_HALF : (w + 1) * W_HALF]
             nc.sync.dma_start(raw[:], rows.rearrange("(p i) n -> p i n", i=PACK))
             raws[w, a] = raw
@@ -130,15 +139,16 @@ def tile_list_hwayt_mix_relu_kernel(
             nc.sync.dma_start(planes[32 * q : 32 * q + 4].bitcast(I32), joined[8 * q : 8 * q + 8, :].bitcast(I32))
         load_r(0, "after_join")
 
-        picked = held.tile([P, J], U32, name="picked", tag="after_parting", align_bytes=64)
-        nc.vector.tensor_copy(picked[:], table[:].bitcast(U32).indirect(offsets[:]))
+        picked = [laid.tile([P, HALF], U32, name=f"picked_{h}", offset=5120 - 2048 * h, align_bytes=64) for h in range(2)]
+        for h in range(2):
+            nc.vector.tensor_copy(picked[h][:], table[:].bitcast(U32).indirect(listed(h * HALF, HALF)))
         moving = []
         for h in range(2):
             parted = held.tile([P, 2, HALF], U16, name=f"parted_{h}", align_bytes=64)
-            nc.vector.tensor_copy(parted[:], picked[:, half(h)].bitcast(U16).rearrange("p (t d) -> p d t", d=2))
+            nc.vector.tensor_copy(parted[:], picked[h][:].bitcast(U16).rearrange("p (t d) -> p d t", d=2))
             moving.append([(parted[:, a, :], planes[:, a, half(h)]) for a in range(2)])
         load_r(2, "after_words")
-        load_wh(1, 0, "after_parting")
+        load_wh(1, 0, None)
 
         def unit_tile(kind, b, h, tag=None):
             name = f"{kind}_{b}{h}"
@@ -217,10 +227,10 @@ def tile_list_hwayt_mix_relu_kernel(
             nc.scalar.copy(result[:], back[:])
             store(b, half(h), result[:])
 
-        def gpsimd_sum(b, h, place=None):
+        def gpsimd_sum(b, h, width, place=None):
             result = unit_tile("summed", b, h)[:] if place is None else place
-            nc.gpsimd.tensor_tensor(result, mades[b, h], kepts[b, h], ALU.add)
-            store(b, half(h), result)
+            nc.gpsimd.tensor_tensor(result[:, 0:width], mades[b, h][:, 0:width], kepts[b, h][:, 0:width], ALU.add)
+            store(b, slice(h * HALF, h * HALF + width), result[:, 0:width])
 
         def raw_made_term(b, h, made):
             nc.vector.scalar_tensor_tensor(made, keeps[b, h], 1.0, feature_product(b, h)[:], ALU.subtract, ALU.mult)
@@ -248,7 +258,7 @@ def tile_list_hwayt_mix_relu_kernel(
         quantize_wh(1, (0, 1))
         for h in range(2):
             banks[3, h] = gate_product(3, h)
-        keep_of(3, 0, unit_tile("keep", 3, 0, "after_parting")[:])
+        keep_of(3, 0, laid.tile([P, HALF], F32, name="keep_30", offset=3072, align_bytes=64)[:])
         late_keeps = held.tile([P, 3 * HALF], F32, name="late_keeps", tag="after_quantise_00", align_bytes=64)
         keep_of(3, 1, late_keeps[:, half(0)])
         for h in range(2):
@@ -258,18 +268,18 @@ def tile_list_hwayt_mix_relu_kernel(
             gate_of(2, h, gates_2[:, half(h)])
         for h in range(2):
             kepts[3, h] = kept_term(3, h)
-        gates_3 = held.tile([P, J], F32, name="gates_3", tag="after_parting", align_bytes=64)
+        gates_3 = laid.tile([P, J], F32, name="gates_3", offset=0, align_bytes=64)
         for h in range(2):
             gate_of(3, h, gates_3[:, half(h)])
-        late_mades = held.tile([P, 3 * J + HALF], F32, name="late_mades", tag="after_quantise_01", align_bytes=64)
-        gpsimd_sum(0, 0, late_mades[:, half(6)])
+        late_mades = held.tile([P, 3 * J], F32, name="late_mades", tag="after_quantise_01", align_bytes=64)
+        gpsimd_sum(0, 0, HALF, laid.tile([P, HALF], F32, name="summed_00", offset=4096, align_bytes=64)[:])
         for place, b in enumerate((2, 3, 1)):
             for h in range(2):
                 mades[b, h] = late_mades[:, half(2 * place + h)]
                 (raw_made_term if b == 1 else made_term)(b, h, mades[b, h])
-        gpsimd_sum(2, 1)
-        gpsimd_sum(3, 1)
-        kept_1 = held.tile([P, J], F32, name="kept_1", tag="after_parting", align_bytes=64)
+        gpsimd_sum(2, 1, HALF)
+        gpsimd_sum(3, 1, GPSIMD_LAST)
+        kept_1 = laid.tile([P, J], F32, name="kept_1", offset=0, align_bytes=64)
         for h in range(2):
             kepts[1, h] = kept_term(1, h, kept_1[:, half(h)])
 
@@ -281,6 +291,9 @@ def tile_list_hwayt_mix_relu_kernel(
             waiting = turned
         turn_back(*waiting)
 
+        rest = work.tile([P, HALF - GPSIMD_LAST], F32, name="rest", tag="result")
+        nc.vector.tensor_tensor(rest[:], mades[3, 1][:, GPSIMD_LAST:], kepts[3, 1][:, GPSIMD_LAST:], ALU.add)
+        store(3, slice(HALF + GPSIMD_LAST, J), rest[:])
         for h, first, width in ((0, 0, HALF), (1, 0, HALF // 2), (1, HALF // 2, HALF // 2)):
             cols = slice(first, first + width)
             result = work.tile([P, width], F32, name="result", tag="result")

@@ -48,7 +48,7 @@ def tile_list_hwayt_mix_relu_kernel(
             return slice(h * HALF, (h + 1) * HALF)
 
         tab_sc = held.tile([P, T], U8, name="tab_sc", align_bytes=64)
-        nc.scalar.dma_start(tab_sc[0:SC_ROWS, :].bitcast(I32), tab_scales.rearrange("a q t -> q a t").bitcast(I32))
+        nc.sync.dma_start(tab_sc[0:SC_ROWS, :].bitcast(I32), tab_scales.rearrange("a q t -> q a t").bitcast(I32))
         nc.vector.memset(tab_sc[32:64, :].bitcast(I32), 0)
         nc.vector.memset(tab_sc[64:128, :].bitcast(I32), 0)
 
@@ -56,8 +56,6 @@ def tile_list_hwayt_mix_relu_kernel(
         nc.sync.dma_start(joined[0:SC_ROWS:2, J:].bitcast(I32), wg8_scales[0].bitcast(I32))
         nc.sync.dma_start(joined[1:SC_ROWS:2, J:].bitcast(I32), wg4_scales[0].bitcast(I32))
         planes = held.tile([P, 2, J + N], U8, name="planes", align_bytes=64)
-        wg4 = held.tile([P, 2 * N], U8, name="wg4", align_bytes=64)
-        nc.sync.dma_start(wg4[:].bitcast(I32), wg4_words[0].bitcast(I32))
 
         table = held.tile([P, T], I32, name="table", tag="after_words", align_bytes=64)
         nc.sync.dma_start(table[:], tab_words[0].rearrange("p t b -> p (t b)").bitcast(I32))
@@ -84,8 +82,8 @@ def tile_list_hwayt_mix_relu_kernel(
         r_tiles = {}
 
         def load_wh(w, a, tag):
-            if tag is None:
-                raw = laid.tile([P, PACK, W_HALF], F32, name=f"raw_{w}{a}", offset=3072, align_bytes=64)
+            if tag in (3072, 10240):
+                raw = laid.tile([P, PACK, W_HALF], F32, name=f"raw_{w}{a}", offset=tag, align_bytes=64)
             else:
                 raw = held.tile([P, PACK, W_HALF], F32, name=f"raw_{w}{a}", tag=tag, align_bytes=64)
             rows = wh[a * K_PASS : (a + 1) * K_PASS, w * W_HALF : (w + 1) * W_HALF]
@@ -110,7 +108,10 @@ def tile_list_hwayt_mix_relu_kernel(
         def quantize_wh(w, passes, tag=None):
             name = f"{w}{passes[-1]}"
             width = len(passes) * W_HALF
-            grouped = held.tile([P, width, PACK], BF16, name=f"grouped_{name}", tag=f"after_quantise_{name}", align_bytes=64)
+            if name == "00":
+                grouped = laid.tile([P, width, PACK], BF16, name=f"grouped_{name}", offset=3072, align_bytes=64)
+            else:
+                grouped = held.tile([P, width, PACK], BF16, name=f"grouped_{name}", tag=f"after_quantise_{name}", align_bytes=64)
             for place, a in enumerate(passes):
                 round_wh(w, a, grouped[:, place * W_HALF : (place + 1) * W_HALF, :])
             codes = held.tile([P, width], U32, name=f"codes_{name}", tag=tag or f"codes_{name}", align_bytes=64)
@@ -127,10 +128,11 @@ def tile_list_hwayt_mix_relu_kernel(
             nc.sync.dma_start(carried[:], rT[b * P : (b + 1) * P, :])
             r_tiles[b] = carried
 
-        load_wh(0, 0, "raw_00")
-        load_wh(0, 1, "raw_01")
         wg8 = held.tile([P, N], I32, name="wg8", align_bytes=64)
         nc.sync.dma_start(wg8[:], wg8_words[0].rearrange("p n b -> p (n b)").bitcast(I32))
+        wg4 = held.tile([P, 2 * N], U8, name="wg4", align_bytes=64)
+        nc.sync.dma_start(wg4[:].bitcast(I32), wg4_words[0].bitcast(I32))
+        load_wh(0, 0, "raw_00")
 
         picked_sc = held.tile([P, J], U8, name="picked_sc", tag="after_join", align_bytes=64)
         nc.vector.tensor_copy(picked_sc[:], tab_sc[:].indirect(offsets[:]))
@@ -139,16 +141,16 @@ def tile_list_hwayt_mix_relu_kernel(
             nc.sync.dma_start(planes[32 * q : 32 * q + 4].bitcast(I32), joined[8 * q : 8 * q + 8, :].bitcast(I32))
         load_r(0, "after_join")
 
-        picked = [laid.tile([P, HALF], U32, name=f"picked_{h}", offset=5120 - 2048 * h, align_bytes=64) for h in range(2)]
-        for h in range(2):
-            nc.vector.tensor_copy(picked[h][:], table[:].bitcast(U32).indirect(listed(h * HALF, HALF)))
         moving = []
         for h in range(2):
+            picked = laid.tile([P, HALF], U32, name=f"picked_{h}", offset=9216 - 1024 * h, align_bytes=64)
+            nc.vector.tensor_copy(picked[:], table[:].bitcast(U32).indirect(listed(h * HALF, HALF)))
             parted = held.tile([P, 2, HALF], U16, name=f"parted_{h}", align_bytes=64)
-            nc.vector.tensor_copy(parted[:], picked[h][:].bitcast(U16).rearrange("p (t d) -> p d t", d=2))
+            nc.vector.tensor_copy(parted[:], picked[:].bitcast(U16).rearrange("p (t d) -> p d t", d=2))
             moving.append([(parted[:, a, :], planes[:, a, half(h)]) for a in range(2)])
+            if h == 0:
+                load_wh(0, 1, 10240)
         load_r(2, "after_words")
-        load_wh(1, 0, None)
 
         def unit_tile(kind, b, h, tag=None):
             name = f"{kind}_{b}{h}"
@@ -238,20 +240,24 @@ def tile_list_hwayt_mix_relu_kernel(
         mades = {}
         kepts = {}
         quantize_wh(0, (0,))
-        load_wh(1, 1, "after_quantise_00")
-        quantize_wh(0, (1,))
-        load_r(3, "after_quantise_01")
+        load_wh(1, 0, 3072)
         banks = {(b, h): gate_product(b, h) for b in (0, 2, 1) for h in range(2)}
-        for b in (0, 2):
-            for h in range(2):
-                keep_of(b, h)
         for h in range(2):
-            gate_of(0, h)
+            keep_of(0, h)
+        keep_of(2, 0)
+        kepts[0, 0] = kept_term(0, 0)
+        load_wh(1, 1, "keep_00")
+        kepts[0, 1] = kept_term(0, 1)
+        load_r(3, "keep_01")
+        quantize_wh(0, (1,))
+        early_sigmoids = laid.tile([P, 3 * HALF], F32, name="early_sigmoids", offset=10240, align_bytes=64)
+        keep_of(2, 1, early_sigmoids[:, half(0)])
         for h in range(2):
-            kepts[0, h] = kept_term(0, h)
-        load_r(1, "after_join")
-        for h in range(2):
-            kepts[2, h] = kept_term(2, h)
+            gate_of(0, h, early_sigmoids[:, half(1 + h)])
+        kept_2 = held.tile([P, J], F32, name="kept_2", tag="after_quantise_01", align_bytes=64)
+        kepts[2, 0] = kept_term(2, 0, kept_2[:, half(0)])
+        load_r(1, "keep_20")
+        kepts[2, 1] = kept_term(2, 1, kept_2[:, half(1)])
         for h in range(2):
             mades[0, h] = unit_tile("made", 0, h)[:]
             made_term(0, h, mades[0, h])
@@ -259,7 +265,7 @@ def tile_list_hwayt_mix_relu_kernel(
         for h in range(2):
             banks[3, h] = gate_product(3, h)
         keep_of(3, 0, laid.tile([P, HALF], F32, name="keep_30", offset=3072, align_bytes=64)[:])
-        late_keeps = held.tile([P, 3 * HALF], F32, name="late_keeps", tag="after_quantise_00", align_bytes=64)
+        late_keeps = held.tile([P, 3 * HALF], F32, name="late_keeps", tag="keep_00", align_bytes=64)
         keep_of(3, 1, late_keeps[:, half(0)])
         for h in range(2):
             keep_of(1, h, late_keeps[:, half(1 + h)])
@@ -271,7 +277,7 @@ def tile_list_hwayt_mix_relu_kernel(
         gates_3 = laid.tile([P, J], F32, name="gates_3", offset=0, align_bytes=64)
         for h in range(2):
             gate_of(3, h, gates_3[:, half(h)])
-        late_mades = held.tile([P, 3 * J], F32, name="late_mades", tag="after_quantise_01", align_bytes=64)
+        late_mades = held.tile([P, 3 * J], F32, name="late_mades", tag="keep_01", align_bytes=64)
         gpsimd_sum(0, 0, HALF, laid.tile([P, HALF], F32, name="summed_00", offset=4096, align_bytes=64)[:])
         for place, b in enumerate((2, 3, 1)):
             for h in range(2):

@@ -25,7 +25,6 @@ HALF = 512
 LIST_COLS = HALF // 16
 W_HALF = N // 2
 SC_ROWS = 32
-GPSIMD_LAST = 384
 
 
 def tile_list_hwayt_mix_relu_kernel(
@@ -163,8 +162,8 @@ def tile_list_hwayt_mix_relu_kernel(
             return psum.tile([P, HALF], F32, name=name, tag=f"bank_{number}")
 
         gate_banks = {0: 0, 2: 2, 1: 6, 3: 0}
-        feature_banks = {0: 4, 2: 4, 3: 6, 1: 2}
-        sum_banks = [0, 1, 4, 5, 6, 7]
+        feature_banks = {(0, 0): 4, (0, 1): 5, (1, 0): 6, (2, 0): 4, (2, 1): 5, (3, 0): 6, (3, 1): 7, (1, 1): 3}
+        sum_banks = [0, 1, 4, 5, 7, 2, 6, 3]
 
         def gate_product(b, h):
             cols = slice(b * P, (b + 1) * P)
@@ -189,7 +188,7 @@ def tile_list_hwayt_mix_relu_kernel(
             nc.scalar.activation(gates[b, h], banks[b, h][:], ACT.Sigmoid, bias=bias[:, b : b + 1])
 
         def feature_product(b, h):
-            ha = bank("ha", feature_banks[b] + h)
+            ha = bank("ha", feature_banks[b, h])
             w_cols = slice((b % 2) * P, (b % 2 + 1) * P)
             for a in range(2):
                 codes, scales = wh_q[b // 2, a]
@@ -210,29 +209,31 @@ def tile_list_hwayt_mix_relu_kernel(
         def store(b, cols, result):
             nc.sync.dma_start(out[b * P : (b + 1) * P, cols], result)
 
-        def turned_sum(b, h, one, other):
+        def turned_sum(b, first, width):
+            h, start = divmod(first, HALF)
             acc = bank("acc", sum_banks.pop(0))
-            for c in range(HALF // P):
+            for c in range(width // P):
                 cols = slice(c * P, (c + 1) * P)
-                nc.tensor.matmul(acc[:, cols], one[:, cols], ident[:], start=True, stop=False, is_transpose=True)
-                nc.tensor.matmul(acc[:, cols], other[:, cols], ident[:], start=False, stop=True, is_transpose=True)
-            turned = unit_tile("turned", b, h)
-            nc.scalar.copy(turned[:], acc[:])
-            return b, h, turned
+                source = slice(start + c * P, start + (c + 1) * P)
+                nc.tensor.matmul(acc[:, cols], mades[b, h][:, source], ident[:], start=True, stop=False, is_transpose=True)
+                nc.tensor.matmul(acc[:, cols], kepts[b, h][:, source], ident[:], start=False, stop=True, is_transpose=True)
+            turned = work.tile([P, width], F32, name="turned", tag="turned", bufs=4)
+            nc.scalar.copy(turned[:], acc[:, 0:width])
+            return b, first, width, turned
 
-        def turn_back(b, h, turned):
+        def turn_back(b, first, width, turned):
             back = bank("back", sum_banks.pop(0))
-            for c in range(HALF // P):
+            for c in range(width // P):
                 cols = slice(c * P, (c + 1) * P)
                 nc.tensor.transpose(back[:, cols], turned[:, cols], ident[:])
-            result = work.tile([P, HALF], F32, name="result", tag="result")
-            nc.scalar.copy(result[:], back[:])
-            store(b, half(h), result[:])
+            result = work.tile([P, width], F32, name="result", tag="result")
+            nc.scalar.copy(result[:], back[:, 0:width])
+            store(b, slice(first, first + width), result[:])
 
-        def gpsimd_sum(b, h, width, place=None):
+        def gpsimd_sum(b, h, place=None):
             result = unit_tile("summed", b, h)[:] if place is None else place
-            nc.gpsimd.tensor_tensor(result[:, 0:width], mades[b, h][:, 0:width], kepts[b, h][:, 0:width], ALU.add)
-            store(b, slice(h * HALF, h * HALF + width), result[:, 0:width])
+            nc.gpsimd.tensor_tensor(result, mades[b, h], kepts[b, h], ALU.add)
+            store(b, half(h), result)
 
         def raw_made_term(b, h, made):
             nc.vector.scalar_tensor_tensor(made, keeps[b, h], 1.0, feature_product(b, h)[:], ALU.subtract, ALU.mult)
@@ -250,10 +251,11 @@ def tile_list_hwayt_mix_relu_kernel(
         kepts[0, 1] = kept_term(0, 1)
         load_r(3, "keep_01")
         quantize_wh(0, (1,))
-        early_sigmoids = laid.tile([P, 3 * HALF], F32, name="early_sigmoids", offset=10240, align_bytes=64)
+        early_sigmoids = laid.tile([P, 4 * HALF], F32, name="early_sigmoids", offset=10240, align_bytes=64)
         keep_of(2, 1, early_sigmoids[:, half(0)])
         for h in range(2):
             gate_of(0, h, early_sigmoids[:, half(1 + h)])
+        keep_of(1, 0, early_sigmoids[:, half(3)])
         kept_2 = held.tile([P, J], F32, name="kept_2", tag="after_quantise_01", align_bytes=64)
         kepts[2, 0] = kept_term(2, 0, kept_2[:, half(0)])
         load_r(1, "keep_20")
@@ -261,14 +263,16 @@ def tile_list_hwayt_mix_relu_kernel(
         for h in range(2):
             mades[0, h] = unit_tile("made", 0, h)[:]
             made_term(0, h, mades[0, h])
+        mades[1, 0] = unit_tile("made", 1, 0)[:]
+        raw_made_term(1, 0, mades[1, 0])
+        gpsimd_sum(0, 0)
         quantize_wh(1, (0, 1))
         for h in range(2):
             banks[3, h] = gate_product(3, h)
         keep_of(3, 0, laid.tile([P, HALF], F32, name="keep_30", offset=3072, align_bytes=64)[:])
-        late_keeps = held.tile([P, 3 * HALF], F32, name="late_keeps", tag="keep_00", align_bytes=64)
+        late_keeps = held.tile([P, J], F32, name="late_keeps", tag="keep_00", align_bytes=64)
         keep_of(3, 1, late_keeps[:, half(0)])
-        for h in range(2):
-            keep_of(1, h, late_keeps[:, half(1 + h)])
+        keep_of(1, 1, late_keeps[:, half(1)])
         gates_2 = held.tile([P, J], F32, name="gates_2", tag="after_quantise_11", align_bytes=64)
         for h in range(2):
             gate_of(2, h, gates_2[:, half(h)])
@@ -277,29 +281,23 @@ def tile_list_hwayt_mix_relu_kernel(
         gates_3 = laid.tile([P, J], F32, name="gates_3", offset=0, align_bytes=64)
         for h in range(2):
             gate_of(3, h, gates_3[:, half(h)])
-        late_mades = held.tile([P, 3 * J], F32, name="late_mades", tag="keep_01", align_bytes=64)
-        gpsimd_sum(0, 0, HALF, laid.tile([P, HALF], F32, name="summed_00", offset=4096, align_bytes=64)[:])
-        for place, b in enumerate((2, 3, 1)):
-            for h in range(2):
-                mades[b, h] = late_mades[:, half(2 * place + h)]
-                (raw_made_term if b == 1 else made_term)(b, h, mades[b, h])
-        gpsimd_sum(2, 1, HALF)
-        gpsimd_sum(3, 1, GPSIMD_LAST)
+        late_mades = held.tile([P, 5 * HALF], F32, name="late_mades", tag="keep_01", align_bytes=64)
+        gpsimd_sum(0, 1, laid.tile([P, HALF], F32, name="summed_01", offset=4096, align_bytes=64)[:])
+        for place, (b, h) in enumerate(((2, 0), (2, 1), (3, 0), (3, 1), (1, 1))):
+            mades[b, h] = late_mades[:, half(place)]
+            (raw_made_term if b == 1 else made_term)(b, h, mades[b, h])
+        gpsimd_sum(2, 1)
         kept_1 = laid.tile([P, J], F32, name="kept_1", offset=0, align_bytes=64)
         for h in range(2):
             kepts[1, h] = kept_term(1, h, kept_1[:, half(h)])
 
-        waiting = None
-        for b, h in ((0, 1), (2, 0), (3, 0)):
-            turned = turned_sum(b, h, mades[b, h], kepts[b, h])
-            if waiting is not None:
-                turn_back(*waiting)
-            waiting = turned
-        turn_back(*waiting)
+        sum_20 = turned_sum(2, 0, HALF)
+        sum_30 = turned_sum(3, 0, HALF)
+        turn_back(*sum_20)
+        sums_31 = [turned_sum(3, HALF + first, HALF // 2) for first in (0, HALF // 2)]
+        for turned in [sum_30] + sums_31:
+            turn_back(*turned)
 
-        rest = work.tile([P, HALF - GPSIMD_LAST], F32, name="rest", tag="result")
-        nc.vector.tensor_tensor(rest[:], mades[3, 1][:, GPSIMD_LAST:], kepts[3, 1][:, GPSIMD_LAST:], ALU.add)
-        store(3, slice(HALF + GPSIMD_LAST, J), rest[:])
         for h, first, width in ((0, 0, HALF), (1, 0, HALF // 2), (1, HALF // 2, HALF // 2)):
             cols = slice(first, first + width)
             result = work.tile([P, width], F32, name="result", tag="result")

@@ -163,7 +163,7 @@ def tile_list_hwayt_mix_relu_kernel(
 
         gate_banks = {0: 0, 2: 2, 1: 6, 3: 0}
         feature_banks = {(0, 0): 4, (0, 1): 5, (1, 0): 6, (2, 0): 4, (2, 1): 5, (3, 0): 6, (3, 1): 7, (1, 1): 3}
-        sum_banks = [0, 1, 4, 5, 7, 2, 6, 3]
+        sum_banks = [0, 1, 4, 5]
 
         def gate_product(b, h):
             cols = slice(b * P, (b + 1) * P)
@@ -287,6 +287,9 @@ def tile_list_hwayt_mix_relu_kernel(
             mades[b, h] = late_mades[:, half(place)]
             (raw_made_term if b == 1 else made_term)(b, h, mades[b, h])
         gpsimd_sum(2, 1)
+        result = work.tile([P, HALF], F32, name="result", tag="result")
+        nc.vector.tensor_tensor(result[:], mades[3, 1], kepts[3, 1], ALU.add)
+        store(3, half(1), result[:])
         kept_1 = laid.tile([P, J], F32, name="kept_1", offset=0, align_bytes=64)
         for h in range(2):
             kepts[1, h] = kept_term(1, h, kept_1[:, half(h)])
@@ -294,9 +297,7 @@ def tile_list_hwayt_mix_relu_kernel(
         sum_20 = turned_sum(2, 0, HALF)
         sum_30 = turned_sum(3, 0, HALF)
         turn_back(*sum_20)
-        sums_31 = [turned_sum(3, HALF + first, HALF // 2) for first in (0, HALF // 2)]
-        for turned in [sum_30] + sums_31:
-            turn_back(*turned)
+        turn_back(*sum_30)
 
         for h, first, width in ((0, 0, HALF), (1, 0, HALF // 2), (1, HALF // 2, HALF // 2)):
             cols = slice(first, first + width)

@@ -59,6 +59,9 @@ def tile_list_hwayt_mix_relu_kernel(
         table = held.tile([P, T], I32, name="table", tag="after_words", align_bytes=64)
         nc.sync.dma_start(table[:], tab_words[0].rearrange("p t b -> p (t b)").bitcast(I32))
 
+        bias_rows = held.tile([P, P], F32, name="bias_rows")
+        nc.gpsimd.memset(bias_rows[:], 0.0)
+        nc.scalar.dma_start(bias_rows[0 : N // P, :], bg.rearrange("(b p) -> b p", p=P))
         warm = held.tile([P, 8], F32, name="warm")
         warm_out = held.tile([P, 8], F32, name="warm_out")
         nc.gpsimd.memset(warm[:], 0.0)
@@ -66,9 +69,6 @@ def tile_list_hwayt_mix_relu_kernel(
 
         ident = held.tile([P, P], F32, name="ident")
         make_identity(nc, ident[:])
-        bias_rows = held.tile([P, P], F32, name="bias_rows")
-        nc.gpsimd.memset(bias_rows[:], 0.0)
-        nc.gpsimd.dma_start(bias_rows[0 : N // P, :], bg.rearrange("(b p) -> b p", p=P))
         bias_bank = psum.tile([P, P], F32, name="bias_bank", tag="bank_7")
         nc.tensor.transpose(bias_bank[:], bias_rows[:], ident[:])
         bias = held.tile([P, N // P], F32, name="bias")

@@ -136,7 +136,7 @@ def tile_list_hwayt_mix_relu_kernel(
         picked_sc = held.tile([P, J], U8, name="picked_sc", tag="after_join", align_bytes=64)
         nc.vector.tensor_copy(picked_sc[:], tab_sc[:].indirect(offsets[:]))
         nc.vector.tensor_copy(joined[:, 0:J].bitcast(I32), picked_sc[0:SC_ROWS, :].bitcast(I32))
-        for q in range(QUADS):
+        for q in (0, 2, 1, 3):
             nc.sync.dma_start(planes[32 * q : 32 * q + 4].bitcast(I32), joined[8 * q : 8 * q + 8, :].bitcast(I32))
         load_r(0, "after_join")
 

@@ -20,10 +20,11 @@ ACT = mybir.ActivationFunctionType
 P = 128
 PACK = 4
 K_PASS = P * PACK
-QUADS = 4
+PASSES = K // K_PASS
+BLOCKS = N // P
+LAST = BLOCKS - 1
 HALF = 512
-LIST_COLS = HALF // 16
-W_HALF = N // 2
+QUARTER = 256
 SC_ROWS = 32
 
 
@@ -33,9 +34,16 @@ def tile_list_hwayt_mix_relu_kernel(
     nc = tc.nc
     with ExitStack() as ctx:
         held = ctx.enter_context(tc.tile_pool(name="held", bufs=1))
-        work = ctx.enter_context(tc.tile_pool(name="work", bufs=8))
-        laid = ctx.enter_context(tc.tile_pool(name="laid", bufs=1))
         psum = ctx.enter_context(tc.psum_pool(name="psum", bufs=1))
+
+        def sbuf(shape, dtype, name, slot=None):
+            return held.tile(shape, dtype, name=name, tag=slot or name, align_bytes=64)
+
+        def bank(name, number, width=HALF):
+            return psum.tile([P, width], F32, name=name, tag=f"bank_{number}")
+
+        def half(h):
+            return slice(h * HALF, (h + 1) * HALF)
 
         offsets = held.tile([P, J // 16], U16, name="offsets")
         nc.sync.dma_start(offsets[:], offs)
@@ -43,264 +51,261 @@ def tile_list_hwayt_mix_relu_kernel(
         def listed(first, count):
             return offsets[:, first // 16 : (first + count) // 16]
 
-        def half(h):
-            return slice(h * HALF, (h + 1) * HALF)
-
-        tab_sc = held.tile([P, T], U8, name="tab_sc", align_bytes=64)
+        tab_sc = sbuf([P, T], U8, "tab_sc")
         nc.sync.dma_start(tab_sc[0:SC_ROWS, :].bitcast(I32), tab_scales.rearrange("a q t -> q a t").bitcast(I32))
         nc.vector.memset(tab_sc[32:64, :].bitcast(I32), 0)
         nc.vector.memset(tab_sc[64:128, :].bitcast(I32), 0)
 
-        joined = held.tile([SC_ROWS, J + N], U8, name="joined", align_bytes=64)
+        joined = sbuf([SC_ROWS, J + N], U8, "joined")
         nc.sync.dma_start(joined[0:SC_ROWS:2, J:].bitcast(I32), wg8_scales[0].bitcast(I32))
         nc.sync.dma_start(joined[1:SC_ROWS:2, J:].bitcast(I32), wg4_scales[0].bitcast(I32))
-        planes = held.tile([P, 2, J + N], U8, name="planes", align_bytes=64)
+        planes = sbuf([P, PASSES, J + N], U8, "planes")
 
-        table = held.tile([P, T], I32, name="table", tag="after_words", align_bytes=64)
+        table = sbuf([P, T], I32, "table")
         nc.sync.dma_start(table[:], tab_words[0].rearrange("p t b -> p (t b)").bitcast(I32))
 
-        bias_rows = held.tile([P, P], F32, name="bias_rows")
+        bias_rows = sbuf([P, P], F32, "bias_rows")
         nc.gpsimd.memset(bias_rows[:], 0.0)
-        nc.scalar.dma_start(bias_rows[0 : N // P, :], bg.rearrange("(b p) -> b p", p=P))
-        warm = held.tile([P, 8], F32, name="warm")
-        warm_out = held.tile([P, 8], F32, name="warm_out")
+        nc.scalar.dma_start(bias_rows[0:BLOCKS, :], bg.rearrange("(b p) -> b p", p=P))
+        warm = sbuf([P, 8], F32, "warm")
+        warm_out = sbuf([P, 8], F32, "warm_out")
         nc.gpsimd.memset(warm[:], 0.0)
         nc.scalar.activation(warm_out[:], warm[:], ACT.Sigmoid)
 
-        ident = held.tile([P, P], F32, name="ident")
+        ident = sbuf([P, P], F32, "ident")
         make_identity(nc, ident[:])
-        bias_bank = psum.tile([P, P], F32, name="bias_bank", tag="bank_7")
+        bias_bank = bank("bias_bank", 7, P)
         nc.tensor.transpose(bias_bank[:], bias_rows[:], ident[:])
-        bias = held.tile([P, N // P], F32, name="bias")
-        nc.scalar.copy(bias[:], bias_bank[:, 0 : N // P])
-        neg_bias = held.tile([P, N // P], F32, name="neg_bias")
-        nc.scalar.activation(neg_bias[:], bias_bank[:, 0 : N // P], ACT.Copy, scale=-1.0)
+        bias = sbuf([P, BLOCKS], F32, "bias")
+        nc.scalar.copy(bias[:], bias_bank[:, 0:BLOCKS])
+        neg_bias = sbuf([P, BLOCKS], F32, "neg_bias")
+        nc.scalar.activation(neg_bias[:], bias_bank[:, 0:BLOCKS], ACT.Copy, scale=-1.0)
 
-        raws = {}
-        wh_q = {}
-        r_tiles = {}
+        wg8 = sbuf([P, N], I32, "wg8")
+        nc.sync.dma_start(wg8[:], wg8_words[0].rearrange("p n b -> p (n b)").bitcast(I32))
+        wg4 = sbuf([P, 2 * N], U8, "wg4")
+        nc.sync.dma_start(wg4[:].bitcast(I32), wg4_words[0].bitcast(I32))
 
-        def load_wh(w, a, tag):
-            if tag in (3072, 10240):
-                raw = laid.tile([P, PACK, W_HALF], F32, name=f"raw_{w}{a}", offset=tag, align_bytes=64)
-            else:
-                raw = held.tile([P, PACK, W_HALF], F32, name=f"raw_{w}{a}", tag=tag, align_bytes=64)
-            rows = wh[a * K_PASS : (a + 1) * K_PASS, w * W_HALF : (w + 1) * W_HALF]
-            nc.sync.dma_start(raw[:], rows.rearrange("(p i) n -> p i n", i=PACK))
-            raws[w, a] = raw
+        raws, rounded, wh_q, carried = {}, {}, {}, {}
+        gate_banks, gates, keeps, mades, kepts = {}, {}, {}, {}, {}
 
-        def round_wh(w, a, grouped):
-            if w == 1:
-                nc.scalar.copy(
-                    grouped.rearrange("p (c e) i -> p c i e", e=4),
-                    raws[w, a][:].rearrange("p i (c e) -> p c i e", e=4),
-                )
-            else:
+        def load_wh(b, slot):
+            raws[b] = sbuf([P, PACK, PASSES, P], F32, f"raw_{b}", slot)
+            for a in range(PASSES):
+                rows = wh[a * K_PASS : (a + 1) * K_PASS, b * P : (b + 1) * P]
+                nc.sync.dma_start(raws[b][:, :, a, :], rows.rearrange("(p i) n -> p i n", i=PACK))
+
+        def round_wh(b):
+            rounded[b] = sbuf([P, PASSES * P, PACK], BF16, f"rounded_{b}")
+            nc.scalar.activation(
+                rounded[b][:].rearrange("p (c e) i -> p c i e", e=4),
+                raws[b][:].rearrange("p i a (c e) -> p (a c) i e", e=4),
+                ACT.Copy,
+            )
+
+        def quantize_wh(b):
+            codes = sbuf([P, PASSES * P], U32, f"codes_{b}")
+            scales = sbuf([P, PASSES * P], U8, f"scales_{b}")
+            nc.vector.quantize_mx(
+                out=codes[:].bitcast(FP8X4), scales=scales[:], in_=rounded[b][:].rearrange("p n i -> p (n i)")
+            )
+            wh_q[b] = [(codes[:, a * P : (a + 1) * P], scales[:, a * P : (a + 1) * P]) for a in range(PASSES)]
+
+        def load_late_wh(a, slot):
+            raws[2, a] = sbuf([P, PACK, 2 * P], F32, f"late_raw_{a}", slot)
+            rows = wh[a * K_PASS : (a + 1) * K_PASS, 2 * P :]
+            nc.sync.dma_start(raws[2, a][:], rows.rearrange("(p i) n -> p i n", i=PACK))
+
+        def quantize_late_wh():
+            late_rounded = sbuf([P, PASSES, 2 * P, PACK], BF16, "late_rounded")
+            for a in range(PASSES):
                 for cols, sign in ((slice(0, P), 1.0), (slice(P, 2 * P), -1.0)):
                     nc.scalar.activation(
-                        grouped[:, cols, :].rearrange("p (c e) i -> p c i e", e=4),
-                        raws[w, a][:, :, cols].rearrange("p i (c e) -> p c i e", e=4),
+                        late_rounded[:, a, cols, :].rearrange("p (c e) i -> p c i e", e=4),
+                        raws[2, a][:, :, cols].rearrange("p i (c e) -> p c i e", e=4),
                         ACT.Copy,
                         scale=sign,
                     )
-
-        def quantize_wh(w, passes, tag=None):
-            name = f"{w}{passes[-1]}"
-            width = len(passes) * W_HALF
-            if name == "00":
-                grouped = laid.tile([P, width, PACK], BF16, name=f"grouped_{name}", offset=3072, align_bytes=64)
-            else:
-                grouped = held.tile([P, width, PACK], BF16, name=f"grouped_{name}", tag=f"after_quantise_{name}", align_bytes=64)
-            for place, a in enumerate(passes):
-                round_wh(w, a, grouped[:, place * W_HALF : (place + 1) * W_HALF, :])
-            codes = held.tile([P, width], U32, name=f"codes_{name}", tag=tag or f"codes_{name}", align_bytes=64)
-            scales = held.tile([P, width], U8, name=f"scales_{name}", align_bytes=64)
+            codes = sbuf([P, PASSES * 2 * P], U32, "late_codes")
+            scales = sbuf([P, PASSES * 2 * P], U8, "late_scales")
             nc.vector.quantize_mx(
-                out=codes[:].bitcast(FP8X4), scales=scales[:], in_=grouped[:].rearrange("p n i -> p (n i)")
+                out=codes[:].bitcast(FP8X4), scales=scales[:], in_=late_rounded[:].rearrange("p a n i -> p (a n i)")
             )
-            for place, a in enumerate(passes):
-                cols = slice(place * W_HALF, (place + 1) * W_HALF)
-                wh_q[w, a] = (codes[:, cols], scales[:, cols])
+            for b in (2, 3):
+                wh_q[b] = [(codes[:, first : first + P], scales[:, first : first + P]) for first in ((b - 2) * P, b * P)]
 
-        def load_r(b, tag):
-            carried = held.tile([P, T], F32, name=f"carried_{b}", tag=tag, align_bytes=64)
-            nc.sync.dma_start(carried[:], rT[b * P : (b + 1) * P, :])
-            r_tiles[b] = carried
+        def load_r(b, slot):
+            carried[b] = sbuf([P, T], F32, f"carried_{b}", slot)
+            nc.sync.dma_start(carried[b][:], rT[b * P : (b + 1) * P, :])
 
-        wg8 = held.tile([P, N], I32, name="wg8", align_bytes=64)
-        nc.sync.dma_start(wg8[:], wg8_words[0].rearrange("p n b -> p (n b)").bitcast(I32))
-        wg4 = held.tile([P, 2 * N], U8, name="wg4", align_bytes=64)
-        nc.sync.dma_start(wg4[:].bitcast(I32), wg4_words[0].bitcast(I32))
-        load_wh(0, 0, "raw_00")
+        load_wh(0, "raw_0")
 
-        picked_sc = held.tile([P, J], U8, name="picked_sc", tag="after_join", align_bytes=64)
+        picked_sc = sbuf([P, J], U8, "picked_sc")
         nc.vector.tensor_copy(picked_sc[:], tab_sc[:].indirect(offsets[:]))
         nc.vector.tensor_copy(joined[:, 0:J].bitcast(I32), picked_sc[0:SC_ROWS, :].bitcast(I32))
         for q in (0, 2, 1, 3):
             nc.sync.dma_start(planes[32 * q : 32 * q + 4].bitcast(I32), joined[8 * q : 8 * q + 8, :].bitcast(I32))
-        load_r(0, "after_join")
+        load_r(0, "picked_sc")
 
-        moving = []
-        for h in range(2):
-            picked = laid.tile([P, HALF], U32, name=f"picked_{h}", offset=9216 - 1024 * h, align_bytes=64)
-            nc.vector.tensor_copy(picked[:], table[:].bitcast(U32).indirect(listed(h * HALF, HALF)))
-            parted = held.tile([P, 2, HALF], U16, name=f"parted_{h}", align_bytes=64)
-            nc.vector.tensor_copy(parted[:], picked[:].bitcast(U16).rearrange("p (t d) -> p d t", d=2))
-            moving.append([(parted[:, a, :], planes[:, a, half(h)]) for a in range(2)])
-            if h == 0:
-                load_wh(0, 1, 10240)
-        load_r(2, "after_words")
+        def gather_words(name, first, count):
+            picked = sbuf([P, count], U32, name)
+            nc.vector.tensor_copy(picked[:], table[:].bitcast(U32).indirect(listed(first, count)))
+            return picked
 
-        def unit_tile(kind, b, h, tag=None):
-            name = f"{kind}_{b}{h}"
-            return held.tile([P, HALF], F32, name=name, tag=tag or name, align_bytes=64)
+        def part_words(parted, picked):
+            nc.vector.tensor_copy(parted, picked[:].bitcast(U16).rearrange("p (t d) -> p d t", d=2))
 
-        gates = {}
-        keeps = {}
+        parted_0 = sbuf([P, PASSES, HALF], U16, "parted_0")
+        quarters = [gather_words(f"picked_0{c}", c * QUARTER, QUARTER) for c in range(2)]
+        for c in range(2):
+            part_words(parted_0[:, :, c * QUARTER : (c + 1) * QUARTER], quarters[c])
+        load_wh(1, "picked_00")
+        picked_1 = gather_words("picked_1", HALF, HALF)
+        load_r(1, "table")
+        round_wh(0)
+        quantize_wh(0)
+        parted_1 = sbuf([P, PASSES, HALF], U16, "parted_1", "raw_0")
+        part_words(parted_1[:], picked_1)
+        parted = (parted_0, parted_1)
 
-        def bank(name, number):
-            return psum.tile([P, HALF], F32, name=name, tag=f"bank_{number}")
-
-        gate_banks = {0: 0, 2: 2, 1: 6, 3: 0}
-        feature_banks = {(0, 0): 4, (0, 1): 5, (1, 0): 6, (2, 0): 4, (2, 1): 5, (3, 0): 6, (3, 1): 7, (1, 1): 3}
-        sum_banks = [0, 1, 4, 5]
+        def moving(a, h):
+            return dict(rhs=parted[h][:, a, :].bitcast(FP4X4), rhs_scale=planes[:, a, half(h)])
 
         def gate_product(b, h):
-            cols = slice(b * P, (b + 1) * P)
-            g_cols = slice(J + b * P, J + (b + 1) * P)
-            ga = bank("ga", gate_banks[b] + h)
+            ga = bank("ga", (0, 2, 0, 6)[b] + h)
+            scale_cols = slice(J + b * P, J + (b + 1) * P)
             nc.tensor.matmul_mx(
-                out=ga[:], lhsT=wg8[:, cols].bitcast(FP8X4), lhsT_scale=planes[:, 0, g_cols],
-                rhs=moving[h][0][0].bitcast(FP4X4), rhs_scale=moving[h][0][1], start=True, stop=False,
+                out=ga[:], lhsT=wg8[:, b * P : (b + 1) * P].bitcast(FP8X4), lhsT_scale=planes[:, 0, scale_cols],
+                start=True, stop=False, **moving(0, h),
             )
             nc.tensor.matmul_mx(
-                out=ga[:], lhsT=wg4[:, 2 * b * P : 2 * (b + 1) * P].bitcast(FP4X4), lhsT_scale=planes[:, 1, g_cols],
-                rhs=moving[h][1][0].bitcast(FP4X4), rhs_scale=moving[h][1][1], start=False, stop=True,
+                out=ga[:], lhsT=wg4[:, 2 * b * P : 2 * (b + 1) * P].bitcast(FP4X4), lhsT_scale=planes[:, 1, scale_cols],
+                start=False, stop=True, **moving(1, h),
             )
-            return ga
-
-        def keep_of(b, h, place=None):
-            keeps[b, h] = unit_tile("keep", b, h)[:] if place is None else place
-            nc.scalar.activation(keeps[b, h], banks[b, h][:], ACT.Sigmoid, bias=neg_bias[:, b : b + 1], scale=-1.0)
-
-        def gate_of(b, h, place=None):
-            gates[b, h] = unit_tile("gate", b, h)[:] if place is None else place
-            nc.scalar.activation(gates[b, h], banks[b, h][:], ACT.Sigmoid, bias=bias[:, b : b + 1])
+            gate_banks[b, h] = ga
 
         def feature_product(b, h):
-            ha = bank("ha", feature_banks[b, h])
-            w_cols = slice((b % 2) * P, (b % 2 + 1) * P)
-            for a in range(2):
-                codes, scales = wh_q[b // 2, a]
+            ha = bank("ha", (0 if b == LAST else 4) + h)
+            for a, (codes, scales) in enumerate(wh_q[b]):
                 nc.tensor.matmul_mx(
-                    out=ha[:], lhsT=codes[:, w_cols].bitcast(FP8X4), lhsT_scale=scales[:, w_cols],
-                    rhs=moving[h][a][0].bitcast(FP4X4), rhs_scale=moving[h][a][1], start=(a == 0), stop=(a == 1),
+                    out=ha[:], lhsT=codes.bitcast(FP8X4), lhsT_scale=scales,
+                    start=(a == 0), stop=(a == PASSES - 1), **moving(a, h),
                 )
             return ha
 
-        def made_term(b, h, made):
-            nc.vector.scalar_tensor_tensor(made, feature_product(b, h)[:], 0.0, gates[b, h], ALU.max, ALU.mult)
+        def unit(name, slot=None):
+            return sbuf([P, HALF], F32, name, slot)[:]
 
-        def kept_term(b, h, place=None):
-            kept = unit_tile("kept", b, h) if place is None else place
-            nc.vector.tensor_tensor(kept[:], r_tiles[b][:].indirect(listed(h * HALF, HALF)), keeps[b, h], ALU.mult)
-            return kept[:]
+        def keep_of(b, h, place):
+            keeps[b, h] = place
+            nc.scalar.activation(place, gate_banks[b, h][:], ACT.Sigmoid, bias=neg_bias[:, b : b + 1], scale=-1.0)
+
+        def gate_of(b, h, place):
+            gates[b, h] = place
+            nc.scalar.activation(place, gate_banks[b, h][:], ACT.Sigmoid, bias=bias[:, b : b + 1])
+
+        def kept_term(b, h, place):
+            kepts[b, h] = place
+            nc.vector.tensor_tensor(place, carried[b][:].indirect(listed(h * HALF, HALF)), keeps[b, h], ALU.mult)
+
+        def made_term(b, h, place):
+            mades[b, h] = place
+            ha = feature_product(b, h)
+            if b == LAST:
+                nc.vector.scalar_tensor_tensor(place, keeps[b, h], 1.0, ha[:], ALU.subtract, ALU.mult)
+            else:
+                nc.vector.scalar_tensor_tensor(place, ha[:], 0.0, gates[b, h], ALU.max, ALU.mult)
 
         def store(b, cols, result):
             nc.sync.dma_start(out[b * P : (b + 1) * P, cols], result)
 
-        def turned_sum(b, first, width):
-            h, start = divmod(first, HALF)
-            acc = bank("acc", sum_banks.pop(0))
-            for c in range(width // P):
-                cols = slice(c * P, (c + 1) * P)
-                source = slice(start + c * P, start + (c + 1) * P)
-                nc.tensor.matmul(acc[:, cols], mades[b, h][:, source], ident[:], start=True, stop=False, is_transpose=True)
-                nc.tensor.matmul(acc[:, cols], kepts[b, h][:, source], ident[:], start=False, stop=True, is_transpose=True)
-            turned = work.tile([P, width], F32, name="turned", tag="turned", bufs=4)
-            nc.scalar.copy(turned[:], acc[:, 0:width])
-            return b, first, width, turned
+        def gpsimd_sum(b, h, place):
+            nc.gpsimd.tensor_tensor(place, mades[b, h], kepts[b, h], ALU.add)
+            store(b, half(h), place)
 
-        def turn_back(b, first, width, turned):
-            back = bank("back", sum_banks.pop(0))
-            for c in range(width // P):
+        def turned_sum(b, h, number, place):
+            acc = bank("acc", number)
+            for c in range(HALF // P):
+                cols = slice(c * P, (c + 1) * P)
+                nc.tensor.matmul(acc[:, cols], mades[b, h][:, cols], ident[:], start=True, stop=False, is_transpose=True)
+                nc.tensor.matmul(acc[:, cols], kepts[b, h][:, cols], ident[:], start=False, stop=True, is_transpose=True)
+            nc.scalar.copy(place, acc[:])
+
+        def turn_back(b, h, number, turned):
+            back = bank("back", number)
+            for c in range(HALF // P):
                 cols = slice(c * P, (c + 1) * P)
                 nc.tensor.transpose(back[:, cols], turned[:, cols], ident[:])
-            result = work.tile([P, width], F32, name="result", tag="result")
-            nc.scalar.copy(result[:], back[:, 0:width])
-            store(b, slice(first, first + width), result[:])
-
-        def gpsimd_sum(b, h, place=None):
-            result = unit_tile("summed", b, h)[:] if place is None else place
-            nc.gpsimd.tensor_tensor(result, mades[b, h], kepts[b, h], ALU.add)
+            result = unit(f"result_{b}{h}")
+            nc.scalar.copy(result, back[:])
             store(b, half(h), result)
 
-        def raw_made_term(b, h, made):
-            nc.vector.scalar_tensor_tensor(made, keeps[b, h], 1.0, feature_product(b, h)[:], ALU.subtract, ALU.mult)
+        for h in range(2):
+            gate_product(0, h)
+        for h in range(2):
+            keep_of(0, h, unit(f"keep_0{h}"))
+        for h in range(2):
+            gate_of(0, h, unit(f"gate_0{h}"))
+        load_late_wh(0, "rounded_0")
+        load_late_wh(1, "picked_1")
+        for h in range(2):
+            kept_term(0, h, unit(f"kept_0{h}"))
+        load_r(2, "keep_01")
+        made_term(0, 0, unit("made_00", "keep_00"))
+        made_term(0, 1, unit("made_01"))
+        load_r(3, "gate_00")
 
-        mades = {}
-        kepts = {}
-        quantize_wh(0, (0,))
-        load_wh(1, 0, 3072)
-        banks = {(b, h): gate_product(b, h) for b in (0, 2, 1) for h in range(2)}
+        round_wh(1)
+        quantize_wh(1)
         for h in range(2):
-            keep_of(0, h)
-        keep_of(2, 0)
-        kepts[0, 0] = kept_term(0, 0)
-        load_wh(1, 1, "keep_00")
-        kepts[0, 1] = kept_term(0, 1)
-        load_r(3, "keep_01")
-        quantize_wh(0, (1,))
-        early_sigmoids = laid.tile([P, 4 * HALF], F32, name="early_sigmoids", offset=10240, align_bytes=64)
-        keep_of(2, 1, early_sigmoids[:, half(0)])
+            gate_product(1, h)
+        keep_of(1, 0, unit("keep_10", "picked_00"))
+        keep_of(1, 1, unit("keep_11"))
         for h in range(2):
-            gate_of(0, h, early_sigmoids[:, half(1 + h)])
-        keep_of(1, 0, early_sigmoids[:, half(3)])
-        kept_2 = held.tile([P, J], F32, name="kept_2", tag="after_quantise_01", align_bytes=64)
-        kepts[2, 0] = kept_term(2, 0, kept_2[:, half(0)])
-        load_r(1, "keep_20")
-        kepts[2, 1] = kept_term(2, 1, kept_2[:, half(1)])
+            gate_of(1, h, unit(f"gate_1{h}"))
         for h in range(2):
-            mades[0, h] = unit_tile("made", 0, h)[:]
-            made_term(0, h, mades[0, h])
-        mades[1, 0] = unit_tile("made", 1, 0)[:]
-        raw_made_term(1, 0, mades[1, 0])
-        gpsimd_sum(0, 0)
-        quantize_wh(1, (0, 1))
-        for h in range(2):
-            banks[3, h] = gate_product(3, h)
-        keep_of(3, 0, laid.tile([P, HALF], F32, name="keep_30", offset=3072, align_bytes=64)[:])
-        late_keeps = held.tile([P, J], F32, name="late_keeps", tag="keep_00", align_bytes=64)
-        keep_of(3, 1, late_keeps[:, half(0)])
-        keep_of(1, 1, late_keeps[:, half(1)])
-        gates_2 = held.tile([P, J], F32, name="gates_2", tag="after_quantise_11", align_bytes=64)
-        for h in range(2):
-            gate_of(2, h, gates_2[:, half(h)])
-        for h in range(2):
-            kepts[3, h] = kept_term(3, h)
-        gates_3 = laid.tile([P, J], F32, name="gates_3", offset=0, align_bytes=64)
-        for h in range(2):
-            gate_of(3, h, gates_3[:, half(h)])
-        late_mades = held.tile([P, 5 * HALF], F32, name="late_mades", tag="keep_01", align_bytes=64)
-        gpsimd_sum(0, 1, laid.tile([P, HALF], F32, name="summed_01", offset=4096, align_bytes=64)[:])
-        for place, (b, h) in enumerate(((2, 0), (2, 1), (3, 0), (3, 1), (1, 1))):
-            mades[b, h] = late_mades[:, half(place)]
-            (raw_made_term if b == 1 else made_term)(b, h, mades[b, h])
-        gpsimd_sum(2, 1)
-        result = work.tile([P, HALF], F32, name="result", tag="result")
-        nc.vector.tensor_tensor(result[:], mades[3, 1], kepts[3, 1], ALU.add)
-        store(3, half(1), result[:])
-        kept_1 = laid.tile([P, J], F32, name="kept_1", offset=0, align_bytes=64)
-        for h in range(2):
-            kepts[1, h] = kept_term(1, h, kept_1[:, half(h)])
+            kept_term(1, h, unit(f"kept_1{h}"))
+        made_term(1, 0, unit("made_10", "picked_00"))
+        made_term(1, 1, unit("made_11"))
+        gpsimd_sum(0, 0, unit("summed_00", "keep_11"))
 
-        sum_20 = turned_sum(2, 0, HALF)
-        sum_30 = turned_sum(3, 0, HALF)
-        turn_back(*sum_20)
-        turn_back(*sum_30)
+        quantize_late_wh()
+        for b in (2, 3):
+            for h in range(2):
+                gate_product(b, h)
+        late_sigmoids = sbuf([P, 7 * HALF], F32, "late_sigmoids", "rounded_0")
+        keep_of(2, 0, unit("keep_20", "picked_1"))
+        keep_of(2, 1, late_sigmoids[:, half(0)])
+        for h in (1, 0):
+            gate_of(2, h, late_sigmoids[:, half(1 + h)])
+        for h in range(2):
+            keep_of(3, h, late_sigmoids[:, half(3 + h)])
+        for h in range(2):
+            kept_term(2, h, unit(f"kept_2{h}"))
+        late_mades = sbuf([P, J], F32, "late_mades", "picked_1")
+        for h in (1, 0):
+            made_term(2, h, late_mades[:, half(h)])
+        for h in range(2):
+            made_term(3, h, unit(f"made_3{h}"))
+        late_sums = sbuf([P, J], F32, "late_sums", "keep_01")
+        gpsimd_sum(1, 1, late_sums[:, half(0)])
+        gpsimd_sum(2, 0, late_sums[:, half(1)])
+        kept_3 = sbuf([P, J], F32, "kept_3", "late_codes")
+        for h in range(2):
+            kept_term(3, h, kept_3[:, half(h)])
 
-        for h, first, width in ((0, 0, HALF), (1, 0, HALF // 2), (1, HALF // 2, HALF // 2)):
+        turned_01 = late_sigmoids[:, half(5)]
+        turned_10 = late_sigmoids[:, half(6)]
+        turned_21 = unit("turned_21")
+        turned_sum(0, 1, 2, turned_01)
+        turned_sum(1, 0, 3, turned_10)
+        turned_sum(2, 1, 5, turned_21)
+        turn_back(0, 1, 4, turned_01)
+        turn_back(1, 0, 0, turned_10)
+        turn_back(2, 1, 5, turned_21)
+
+        for h, first, width in ((0, 0, HALF), (1, 0, QUARTER), (1, QUARTER, QUARTER)):
             cols = slice(first, first + width)
-            result = work.tile([P, width], F32, name="result", tag="result")
-            nc.vector.scalar_tensor_tensor(result[:], mades[1, h][:, cols], 0.0, kepts[1, h][:, cols], ALU.max, ALU.add)
-            store(1, slice(h * HALF + first, h * HALF + first + width), result[:])
+            result = sbuf([P, width], F32, f"result_3{h}{first}")
+            nc.vector.scalar_tensor_tensor(result[:], mades[3, h][:, cols], 0.0, kepts[3, h][:, cols], ALU.max, ALU.add)
+            store(3, slice(h * HALF + first, h * HALF + first + width), result[:])

@@ -290,19 +290,18 @@ def tile_list_hwayt_mix_relu_kernel(
         late_sums = sbuf([P, J], F32, "late_sums", "keep_01")
         gpsimd_sum(1, 1, late_sums[:, half(0)])
         gpsimd_sum(2, 0, late_sums[:, half(1)])
-        kept_3 = sbuf([P, J], F32, "kept_3", "late_codes")
+        kept_3 = sbuf([P, J + HALF], F32, "kept_3", "late_codes")
+        nc.vector.tensor_tensor(kept_3[:, half(2)], mades[2, 1], kepts[2, 1], ALU.add)
+        store(2, half(1), kept_3[:, half(2)])
         for h in range(2):
             kept_term(3, h, kept_3[:, half(h)])
 
         turned_01 = late_sigmoids[:, half(5)]
         turned_10 = late_sigmoids[:, half(6)]
-        turned_21 = unit("turned_21")
         turned_sum(0, 1, 2, turned_01)
         turned_sum(1, 0, 3, turned_10)
-        turned_sum(2, 1, 5, turned_21)
-        turn_back(0, 1, 4, turned_01)
-        turn_back(1, 0, 0, turned_10)
-        turn_back(2, 1, 5, turned_21)
+        turn_back(0, 1, 5, turned_01)
+        turn_back(1, 0, 4, turned_10)
 
         for h, first, width in ((0, 0, HALF), (1, 0, QUARTER), (1, QUARTER, QUARTER)):
             cols = slice(first, first + width)

@@ -25,7 +25,10 @@ BLOCKS = N // P
 LAST = BLOCKS - 1
 HALF = 512
 QUARTER = 256
+PAIR = 2 * P
 SC_ROWS = 32
+UNIT_BYTES = 4 * HALF
+RAW_AT = 3 * UNIT_BYTES
 
 
 def tile_list_hwayt_mix_relu_kernel(
@@ -34,9 +37,12 @@ def tile_list_hwayt_mix_relu_kernel(
     nc = tc.nc
     with ExitStack() as ctx:
         held = ctx.enter_context(tc.tile_pool(name="held", bufs=1))
+        laid = ctx.enter_context(tc.tile_pool(name="laid", bufs=1))
         psum = ctx.enter_context(tc.psum_pool(name="psum", bufs=1))
 
         def sbuf(shape, dtype, name, slot=None):
+            if isinstance(slot, int):
+                return laid.tile(shape, dtype, name=name, offset=slot, align_bytes=64)
             return held.tile(shape, dtype, name=name, tag=slot or name, align_bytes=64)
 
         def bank(name, number, width=HALF):
@@ -56,13 +62,13 @@ def tile_list_hwayt_mix_relu_kernel(
         nc.vector.memset(tab_sc[32:64, :].bitcast(I32), 0)
         nc.vector.memset(tab_sc[64:128, :].bitcast(I32), 0)
 
+        table = sbuf([P, T], I32, "table")
+        nc.sync.dma_start(table[:], tab_words[0].rearrange("p t b -> p (t b)").bitcast(I32))
+
         joined = sbuf([SC_ROWS, J + N], U8, "joined")
         nc.sync.dma_start(joined[0:SC_ROWS:2, J:].bitcast(I32), wg8_scales[0].bitcast(I32))
         nc.sync.dma_start(joined[1:SC_ROWS:2, J:].bitcast(I32), wg4_scales[0].bitcast(I32))
         planes = sbuf([P, PASSES, J + N], U8, "planes")
-
-        table = sbuf([P, T], I32, "table")
-        nc.sync.dma_start(table[:], tab_words[0].rearrange("p t b -> p (t b)").bitcast(I32))
 
         bias_rows = sbuf([P, P], F32, "bias_rows")
         nc.gpsimd.memset(bias_rows[:], 0.0)
@@ -81,64 +87,53 @@ def tile_list_hwayt_mix_relu_kernel(
         neg_bias = sbuf([P, BLOCKS], F32, "neg_bias")
         nc.scalar.activation(neg_bias[:], bias_bank[:, 0:BLOCKS], ACT.Copy, scale=-1.0)
 
-        wg8 = sbuf([P, N], I32, "wg8")
-        nc.sync.dma_start(wg8[:], wg8_words[0].rearrange("p n b -> p (n b)").bitcast(I32))
-        wg4 = sbuf([P, 2 * N], U8, "wg4")
-        nc.sync.dma_start(wg4[:].bitcast(I32), wg4_words[0].bitcast(I32))
-
-        raws, rounded, wh_q, carried = {}, {}, {}, {}
+        wg8, wg4, raws, rounded, wh_q, carried = {}, {}, {}, {}, {}, {}
         gate_banks, gates, keeps, mades, kepts = {}, {}, {}, {}, {}
 
-        def load_wh(b, slot):
-            raws[b] = sbuf([P, PACK, PASSES, P], F32, f"raw_{b}", slot)
-            for a in range(PASSES):
-                rows = wh[a * K_PASS : (a + 1) * K_PASS, b * P : (b + 1) * P]
-                nc.sync.dma_start(raws[b][:, :, a, :], rows.rearrange("(p i) n -> p i n", i=PACK))
+        def load_wg(w, slot8, slot4):
+            wg8[w] = sbuf([P, PAIR], I32, f"wg8_{w}", slot8)
+            words8 = wg8_words[0].rearrange("p n b -> p (n b)").bitcast(I32)
+            nc.sync.dma_start(wg8[w][:], words8[:, w * PAIR : (w + 1) * PAIR])
+            wg4[w] = sbuf([P, 2 * PAIR], U8, f"wg4_{w}", slot4)
+            nc.sync.dma_start(wg4[w][:].bitcast(I32), wg4_words[0][:, 2 * w * PAIR : 2 * (w + 1) * PAIR].bitcast(I32))
 
-        def round_wh(b):
-            rounded[b] = sbuf([P, PASSES * P, PACK], BF16, f"rounded_{b}")
-            nc.scalar.activation(
-                rounded[b][:].rearrange("p (c e) i -> p c i e", e=4),
-                raws[b][:].rearrange("p i a (c e) -> p (a c) i e", e=4),
-                ACT.Copy,
-            )
+        def load_wh(w, a, slot):
+            raws[w, a] = sbuf([P, PACK, PAIR], F32, f"raw_{w}{a}", slot)
+            rows = wh[a * K_PASS : (a + 1) * K_PASS, w * PAIR : (w + 1) * PAIR]
+            nc.sync.dma_start(raws[w, a][:], rows.rearrange("(p i) n -> p i n", i=PACK))
 
-        def quantize_wh(b):
-            codes = sbuf([P, PASSES * P], U32, f"codes_{b}")
-            scales = sbuf([P, PASSES * P], U8, f"scales_{b}")
+        def round_wh(w, a, place):
+            pieces = ((slice(0, PAIR), 1.0),) if w == 0 else ((slice(0, P), 1.0), (slice(P, PAIR), -1.0))
+            for cols, sign in pieces:
+                nc.scalar.activation(
+                    place[:, cols, :].rearrange("p (c e) i -> p c i e", e=4),
+                    raws[w, a][:, :, cols].rearrange("p i (c e) -> p c i e", e=4),
+                    ACT.Copy,
+                    scale=sign,
+                )
+
+        def quantize_wh(w, passes):
+            name = f"{w}{passes[-1]}"
+            width = len(passes) * PAIR
+            grouped = sbuf([P, width, PACK], BF16, f"rounded_{name}")
+            for place, a in enumerate(passes):
+                round_wh(w, a, grouped[:, place * PAIR : (place + 1) * PAIR, :])
+            codes = sbuf([P, width], U32, f"codes_{name}")
+            scales = sbuf([P, width], U8, f"scales_{name}")
             nc.vector.quantize_mx(
-                out=codes[:].bitcast(FP8X4), scales=scales[:], in_=rounded[b][:].rearrange("p n i -> p (n i)")
+                out=codes[:].bitcast(FP8X4), scales=scales[:], in_=grouped[:].rearrange("p n i -> p (n i)")
             )
-            wh_q[b] = [(codes[:, a * P : (a + 1) * P], scales[:, a * P : (a + 1) * P]) for a in range(PASSES)]
-
-        def load_late_wh(a, slot):
-            raws[2, a] = sbuf([P, PACK, 2 * P], F32, f"late_raw_{a}", slot)
-            rows = wh[a * K_PASS : (a + 1) * K_PASS, 2 * P :]
-            nc.sync.dma_start(raws[2, a][:], rows.rearrange("(p i) n -> p i n", i=PACK))
-
-        def quantize_late_wh():
-            late_rounded = sbuf([P, PASSES, 2 * P, PACK], BF16, "late_rounded")
-            for a in range(PASSES):
-                for cols, sign in ((slice(0, P), 1.0), (slice(P, 2 * P), -1.0)):
-                    nc.scalar.activation(
-                        late_rounded[:, a, cols, :].rearrange("p (c e) i -> p c i e", e=4),
-                        raws[2, a][:, :, cols].rearrange("p i (c e) -> p c i e", e=4),
-                        ACT.Copy,
-                        scale=sign,
-                    )
-            codes = sbuf([P, PASSES * 2 * P], U32, "late_codes")
-            scales = sbuf([P, PASSES * 2 * P], U8, "late_scales")
-            nc.vector.quantize_mx(
-                out=codes[:].bitcast(FP8X4), scales=scales[:], in_=late_rounded[:].rearrange("p a n i -> p (a n i)")
-            )
-            for b in (2, 3):
-                wh_q[b] = [(codes[:, first : first + P], scales[:, first : first + P]) for first in ((b - 2) * P, b * P)]
+            for place, a in enumerate(passes):
+                for c in range(2):
+                    cols = slice(place * PAIR + c * P, place * PAIR + (c + 1) * P)
+                    wh_q[2 * w + c, a] = (codes[:, cols], scales[:, cols])
 
         def load_r(b, slot):
             carried[b] = sbuf([P, T], F32, f"carried_{b}", slot)
             nc.sync.dma_start(carried[b][:], rT[b * P : (b + 1) * P, :])
 
-        load_wh(0, "raw_0")
+        load_wg(0, "wg8_0", "wg4_0")
+        load_wh(0, 0, "raw_00")
 
         picked_sc = sbuf([P, J], U8, "picked_sc")
         nc.vector.tensor_copy(picked_sc[:], tab_sc[:].indirect(offsets[:]))
@@ -147,8 +142,8 @@ def tile_list_hwayt_mix_relu_kernel(
             nc.sync.dma_start(planes[32 * q : 32 * q + 4].bitcast(I32), joined[8 * q : 8 * q + 8, :].bitcast(I32))
         load_r(0, "picked_sc")
 
-        def gather_words(name, first, count):
-            picked = sbuf([P, count], U32, name)
+        def gather_words(name, first, count, slot=None):
+            picked = sbuf([P, count], U32, name, slot)
             nc.vector.tensor_copy(picked[:], table[:].bitcast(U32).indirect(listed(first, count)))
             return picked
 
@@ -156,37 +151,39 @@ def tile_list_hwayt_mix_relu_kernel(
             nc.vector.tensor_copy(parted, picked[:].bitcast(U16).rearrange("p (t d) -> p d t", d=2))
 
         parted_0 = sbuf([P, PASSES, HALF], U16, "parted_0")
-        quarters = [gather_words(f"picked_0{c}", c * QUARTER, QUARTER) for c in range(2)]
+        quarters = [gather_words(f"picked_0{c}", c * QUARTER, QUARTER, (RAW_AT, None)[c]) for c in range(2)]
         for c in range(2):
             part_words(parted_0[:, :, c * QUARTER : (c + 1) * QUARTER], quarters[c])
-        load_wh(1, "picked_00")
+        load_wh(0, 1, RAW_AT)
         picked_1 = gather_words("picked_1", HALF, HALF)
         load_r(1, "table")
-        round_wh(0)
-        quantize_wh(0)
-        parted_1 = sbuf([P, PASSES, HALF], U16, "parted_1", "raw_0")
+        parted_1 = sbuf([P, PASSES, HALF], U16, "parted_1")
         part_words(parted_1[:], picked_1)
+        quantize_wh(0, (0,))
+        load_wg(1, "picked_1", "raw_00")
         parted = (parted_0, parted_1)
 
         def moving(a, h):
             return dict(rhs=parted[h][:, a, :].bitcast(FP4X4), rhs_scale=planes[:, a, half(h)])
 
         def gate_product(b, h):
-            ga = bank("ga", (0, 2, 0, 6)[b] + h)
+            ga = bank("ga", 2 * (b % 2) + h)
             scale_cols = slice(J + b * P, J + (b + 1) * P)
+            own = slice((b % 2) * P, (b % 2 + 1) * P)
             nc.tensor.matmul_mx(
-                out=ga[:], lhsT=wg8[:, b * P : (b + 1) * P].bitcast(FP8X4), lhsT_scale=planes[:, 0, scale_cols],
+                out=ga[:], lhsT=wg8[b // 2][:, own].bitcast(FP8X4), lhsT_scale=planes[:, 0, scale_cols],
                 start=True, stop=False, **moving(0, h),
             )
             nc.tensor.matmul_mx(
-                out=ga[:], lhsT=wg4[:, 2 * b * P : 2 * (b + 1) * P].bitcast(FP4X4), lhsT_scale=planes[:, 1, scale_cols],
+                out=ga[:], lhsT=wg4[b // 2][:, 2 * own.start : 2 * own.stop].bitcast(FP4X4), lhsT_scale=planes[:, 1, scale_cols],
                 start=False, stop=True, **moving(1, h),
             )
             gate_banks[b, h] = ga
 
         def feature_product(b, h):
-            ha = bank("ha", (0 if b == LAST else 4) + h)
-            for a, (codes, scales) in enumerate(wh_q[b]):
+            ha = bank("ha", (4, 6, 4, 0)[b] + h)
+            for a in range(PASSES):
+                codes, scales = wh_q[b, a]
                 nc.tensor.matmul_mx(
                     out=ha[:], lhsT=codes.bitcast(FP8X4), lhsT_scale=scales,
                     start=(a == 0), stop=(a == PASSES - 1), **moving(a, h),
@@ -240,49 +237,47 @@ def tile_list_hwayt_mix_relu_kernel(
             nc.scalar.copy(result, back[:])
             store(b, half(h), result)
 
-        for h in range(2):
-            gate_product(0, h)
+        for b in range(2):
+            for h in range(2):
+                gate_product(b, h)
         for h in range(2):
             keep_of(0, h, unit(f"keep_0{h}"))
         for h in range(2):
             gate_of(0, h, unit(f"gate_0{h}"))
-        load_late_wh(0, "rounded_0")
-        load_late_wh(1, "picked_1")
-        for h in range(2):
-            kept_term(0, h, unit(f"kept_0{h}"))
+        load_wh(1, 0, "rounded_00")
+        kept_term(0, 0, unit("kept_00"))
+        load_wh(1, 1, "keep_00")
+        kept_term(0, 1, unit("kept_01"))
         load_r(2, "keep_01")
-        made_term(0, 0, unit("made_00", "keep_00"))
-        made_term(0, 1, unit("made_01"))
-        load_r(3, "gate_00")
-
-        round_wh(1)
-        quantize_wh(1)
+        quantize_wh(0, (1,))
+        load_r(3, "rounded_01")
+        keep_of(1, 0, unit("keep_10", RAW_AT))
+        early_sigmoids = sbuf([P, 3 * HALF], F32, "early_sigmoids", RAW_AT + UNIT_BYTES)
+        keep_of(1, 1, early_sigmoids[:, half(2)])
         for h in range(2):
-            gate_product(1, h)
-        keep_of(1, 0, unit("keep_10", "picked_00"))
-        keep_of(1, 1, unit("keep_11"))
-        for h in range(2):
-            gate_of(1, h, unit(f"gate_1{h}"))
+            gate_of(1, h, early_sigmoids[:, half(h)])
         for h in range(2):
             kept_term(1, h, unit(f"kept_1{h}"))
-        made_term(1, 0, unit("made_10", "picked_00"))
-        made_term(1, 1, unit("made_11"))
-        gpsimd_sum(0, 0, unit("summed_00", "keep_11"))
+        early_mades = sbuf([P, 2 * J], F32, "early_mades", RAW_AT - 3 * UNIT_BYTES)
+        for b in range(2):
+            for h in range(2):
+                made_term(b, h, early_mades[:, half(2 * b + h)])
+        gpsimd_sum(0, 0, unit("summed_00"))
 
-        quantize_late_wh()
         for b in (2, 3):
             for h in range(2):
                 gate_product(b, h)
-        late_sigmoids = sbuf([P, 7 * HALF], F32, "late_sigmoids", "rounded_0")
-        keep_of(2, 0, unit("keep_20", "picked_1"))
-        keep_of(2, 1, late_sigmoids[:, half(0)])
+        quantize_wh(1, (0, 1))
+        late_sigmoids = sbuf([P, 7 * HALF], F32, "late_sigmoids", "rounded_00")
+        keep_of(2, 0, unit("keep_20", "keep_00"))
+        keep_of(2, 1, late_sigmoids[:, half(6)])
         for h in (1, 0):
-            gate_of(2, h, late_sigmoids[:, half(1 + h)])
+            gate_of(2, h, late_sigmoids[:, half(h)])
         for h in range(2):
-            keep_of(3, h, late_sigmoids[:, half(3 + h)])
+            keep_of(3, h, late_sigmoids[:, half(2 + h)])
         for h in range(2):
             kept_term(2, h, unit(f"kept_2{h}"))
-        late_mades = sbuf([P, J], F32, "late_mades", "picked_1")
+        late_mades = sbuf([P, J], F32, "late_mades", "keep_00")
         for h in (1, 0):
             made_term(2, h, late_mades[:, half(h)])
         for h in range(2):
@@ -290,18 +285,18 @@ def tile_list_hwayt_mix_relu_kernel(
         late_sums = sbuf([P, J], F32, "late_sums", "keep_01")
         gpsimd_sum(1, 1, late_sums[:, half(0)])
         gpsimd_sum(2, 0, late_sums[:, half(1)])
-        kept_3 = sbuf([P, J + HALF], F32, "kept_3", "late_codes")
+        kept_3 = sbuf([P, J + HALF], F32, "kept_3", "codes_11")
         nc.vector.tensor_tensor(kept_3[:, half(2)], mades[2, 1], kepts[2, 1], ALU.add)
         store(2, half(1), kept_3[:, half(2)])
         for h in range(2):
             kept_term(3, h, kept_3[:, half(h)])
 
-        turned_01 = late_sigmoids[:, half(5)]
-        turned_10 = late_sigmoids[:, half(6)]
-        turned_sum(0, 1, 2, turned_01)
-        turned_sum(1, 0, 3, turned_10)
-        turn_back(0, 1, 5, turned_01)
-        turn_back(1, 0, 4, turned_10)
+        turned_01 = late_sigmoids[:, half(4)]
+        turned_10 = late_sigmoids[:, half(5)]
+        turned_sum(0, 1, 6, turned_01)
+        turned_sum(1, 0, 7, turned_10)
+        turn_back(0, 1, 2, turned_01)
+        turn_back(1, 0, 3, turned_10)
 
         for h, first, width in ((0, 0, HALF), (1, 0, QUARTER), (1, QUARTER, QUARTER)):
             cols = slice(first, first + width)

@@ -151,9 +151,7 @@ def tile_list_hwayt_mix_relu_kernel(
             nc.vector.tensor_copy(parted, picked[:].bitcast(U16).rearrange("p (t d) -> p d t", d=2))
 
         parted_0 = sbuf([P, PASSES, HALF], U16, "parted_0")
-        quarters = [gather_words(f"picked_0{c}", c * QUARTER, QUARTER, (RAW_AT, None)[c]) for c in range(2)]
-        for c in range(2):
-            part_words(parted_0[:, :, c * QUARTER : (c + 1) * QUARTER], quarters[c])
+        part_words(parted_0[:], gather_words("picked_0", 0, HALF, RAW_AT))
         load_wh(0, 1, RAW_AT)
         picked_1 = gather_words("picked_1", HALF, HALF)
         load_r(1, "table")
@@ -181,7 +179,7 @@ def tile_list_hwayt_mix_relu_kernel(
             gate_banks[b, h] = ga
 
         def feature_product(b, h):
-            ha = bank("ha", (4, 6, 4, 0)[b] + h)
+            ha = bank("ha", 4 + 2 * (b % 2) + h)
             for a in range(PASSES):
                 codes, scales = wh_q[b, a]
                 nc.tensor.matmul_mx(
@@ -235,7 +233,7 @@ def tile_list_hwayt_mix_relu_kernel(
                 nc.tensor.transpose(back[:, cols], turned[:, cols], ident[:])
             result = unit(f"result_{b}{h}")
             nc.scalar.copy(result, back[:])
-            store(b, half(h), result)
+            nc.scalar.dma_start(out[b * P : (b + 1) * P, half(h)], result)
 
         for b in range(2):
             for h in range(2):
@@ -271,14 +269,14 @@ def tile_list_hwayt_mix_relu_kernel(
         late_sigmoids = sbuf([P, 7 * HALF], F32, "late_sigmoids", "rounded_00")
         keep_of(2, 0, unit("keep_20", "keep_00"))
         keep_of(2, 1, late_sigmoids[:, half(6)])
-        for h in (1, 0):
+        for h in range(2):
             gate_of(2, h, late_sigmoids[:, half(h)])
         for h in range(2):
             keep_of(3, h, late_sigmoids[:, half(2 + h)])
         for h in range(2):
             kept_term(2, h, unit(f"kept_2{h}"))
         late_mades = sbuf([P, J], F32, "late_mades", "keep_00")
-        for h in (1, 0):
+        for h in range(2):
             made_term(2, h, late_mades[:, half(h)])
         for h in range(2):
             made_term(3, h, unit(f"made_3{h}"))
@@ -293,8 +291,8 @@ def tile_list_hwayt_mix_relu_kernel(
 
         turned_01 = late_sigmoids[:, half(4)]
         turned_10 = late_sigmoids[:, half(5)]
-        turned_sum(0, 1, 6, turned_01)
-        turned_sum(1, 0, 7, turned_10)
+        turned_sum(0, 1, 0, turned_01)
+        turned_sum(1, 0, 1, turned_10)
         turn_back(0, 1, 2, turned_01)
         turn_back(1, 0, 3, turned_10)
 

@@ -28,7 +28,7 @@ QUARTER = 256
 PAIR = 2 * P
 SC_ROWS = 32
 UNIT_BYTES = 4 * HALF
-RAW_AT = 3 * UNIT_BYTES
+KEEP_AT = 4 * UNIT_BYTES - UNIT_BYTES // 2
 
 
 def tile_list_hwayt_mix_relu_kernel(
@@ -134,6 +134,7 @@ def tile_list_hwayt_mix_relu_kernel(
 
         load_wg(0, "wg8_0", "wg4_0")
         load_wh(0, 0, "raw_00")
+        load_wh(0, 1, "raw_01")
 
         picked_sc = sbuf([P, J], U8, "picked_sc")
         nc.vector.tensor_copy(picked_sc[:], tab_sc[:].indirect(offsets[:]))
@@ -151,14 +152,16 @@ def tile_list_hwayt_mix_relu_kernel(
             nc.vector.tensor_copy(parted, picked[:].bitcast(U16).rearrange("p (t d) -> p d t", d=2))
 
         parted_0 = sbuf([P, PASSES, HALF], U16, "parted_0")
-        part_words(parted_0[:], gather_words("picked_0", 0, HALF, RAW_AT))
-        load_wh(0, 1, RAW_AT)
+        part_words(parted_0[:], gather_words("picked_0", 0, HALF))
         picked_1 = gather_words("picked_1", HALF, HALF)
         load_r(1, "table")
-        parted_1 = sbuf([P, PASSES, HALF], U16, "parted_1")
-        part_words(parted_1[:], picked_1)
         quantize_wh(0, (0,))
-        load_wg(1, "picked_1", "raw_00")
+        parted_1 = sbuf([P, PASSES, HALF], U16, "parted_1", "raw_00")
+        part_words(parted_1[:], picked_1)
+        load_wg(1, "rounded_00", "picked_1")
+        quantize_wh(0, (1,))
+        load_wh(1, 0, "raw_01")
+        load_wh(1, 1, "rounded_01")
         parted = (parted_0, parted_1)
 
         def moving(a, h):
@@ -238,36 +241,34 @@ def tile_list_hwayt_mix_relu_kernel(
         for b in range(2):
             for h in range(2):
                 gate_product(b, h)
-        for h in range(2):
-            keep_of(0, h, unit(f"keep_0{h}"))
+        keep_of(0, 0, unit("keep_00", KEEP_AT))
+        keep_of(0, 1, unit("keep_01"))
         for h in range(2):
             gate_of(0, h, unit(f"gate_0{h}"))
-        load_wh(1, 0, "rounded_00")
         kept_term(0, 0, unit("kept_00"))
-        load_wh(1, 1, "keep_00")
+        load_r(2, 0)
         kept_term(0, 1, unit("kept_01"))
-        load_r(2, "keep_01")
-        quantize_wh(0, (1,))
-        load_r(3, "rounded_01")
-        keep_of(1, 0, unit("keep_10", RAW_AT))
-        early_sigmoids = sbuf([P, 3 * HALF], F32, "early_sigmoids", RAW_AT + UNIT_BYTES)
-        keep_of(1, 1, early_sigmoids[:, half(2)])
+        load_r(3, "keep_01")
+        made_0 = sbuf([P, J], F32, "made_0", 4 * UNIT_BYTES)
         for h in range(2):
-            gate_of(1, h, early_sigmoids[:, half(h)])
+            made_term(0, h, made_0[:, half(h)])
+        for h in range(2):
+            keep_of(1, h, unit(f"keep_1{h}"))
+        for h in range(2):
+            gate_of(1, h, unit(f"gate_1{h}"))
         for h in range(2):
             kept_term(1, h, unit(f"kept_1{h}"))
-        early_mades = sbuf([P, 2 * J], F32, "early_mades", RAW_AT - 3 * UNIT_BYTES)
-        for b in range(2):
-            for h in range(2):
-                made_term(b, h, early_mades[:, half(2 * b + h)])
-        gpsimd_sum(0, 0, unit("summed_00"))
+        made_1 = sbuf([P, J], F32, "made_1", "keep_10")
+        for h in range(2):
+            made_term(1, h, made_1[:, half(h)])
+        gpsimd_sum(0, 0, unit("summed_00", "keep_11"))
 
         for b in (2, 3):
             for h in range(2):
                 gate_product(b, h)
         quantize_wh(1, (0, 1))
-        late_sigmoids = sbuf([P, 7 * HALF], F32, "late_sigmoids", "rounded_00")
-        keep_of(2, 0, unit("keep_20", "keep_00"))
+        late_sigmoids = sbuf([P, 7 * HALF], F32, "late_sigmoids", "raw_01")
+        keep_of(2, 0, unit("keep_20", "rounded_01"))
         keep_of(2, 1, late_sigmoids[:, half(6)])
         for h in range(2):
             gate_of(2, h, late_sigmoids[:, half(h)])
@@ -275,12 +276,12 @@ def tile_list_hwayt_mix_relu_kernel(
             keep_of(3, h, late_sigmoids[:, half(2 + h)])
         for h in range(2):
             kept_term(2, h, unit(f"kept_2{h}"))
-        late_mades = sbuf([P, J], F32, "late_mades", "keep_00")
+        late_mades = sbuf([P, J], F32, "late_mades", "rounded_01")
         for h in range(2):
             made_term(2, h, late_mades[:, half(h)])
         for h in range(2):
             made_term(3, h, unit(f"made_3{h}"))
-        late_sums = sbuf([P, J], F32, "late_sums", "keep_01")
+        late_sums = sbuf([P, J], F32, "late_sums", 0)
         gpsimd_sum(1, 1, late_sums[:, half(0)])
         gpsimd_sum(2, 0, late_sums[:, half(1)])
         kept_3 = sbuf([P, J + HALF], F32, "kept_3", "codes_11")

@@ -217,9 +217,10 @@ def tile_list_hwayt_mix_relu_kernel(
         def store(b, cols, result):
             nc.sync.dma_start(out[b * P : (b + 1) * P, cols], result)
 
-        def gpsimd_sum(b, h, place):
-            nc.gpsimd.tensor_tensor(place, mades[b, h], kepts[b, h], ALU.add)
-            store(b, half(h), place)
+        def gpsimd_sum(b, first, width, place):
+            h, start = divmod(first, HALF)
+            cols = slice(start, start + width)
+            nc.gpsimd.tensor_tensor(place, mades[b, h][:, cols], kepts[b, h][:, cols], ALU.add)
 
         def turned_sum(b, h, number, place):
             acc = bank("acc", number)
@@ -249,19 +250,20 @@ def tile_list_hwayt_mix_relu_kernel(
         load_r(2, 0)
         kept_term(0, 1, unit("kept_01"))
         load_r(3, "keep_01")
-        made_0 = sbuf([P, J], F32, "made_0", 4 * UNIT_BYTES)
-        for h in range(2):
-            made_term(0, h, made_0[:, half(h)])
+        made_term(0, 0, unit("made_00", 4 * UNIT_BYTES))
         for h in range(2):
             keep_of(1, h, unit(f"keep_1{h}"))
         for h in range(2):
             gate_of(1, h, unit(f"gate_1{h}"))
         for h in range(2):
             kept_term(1, h, unit(f"kept_1{h}"))
-        made_1 = sbuf([P, J], F32, "made_1", "keep_10")
-        for h in range(2):
-            made_term(1, h, made_1[:, half(h)])
-        gpsimd_sum(0, 0, unit("summed_00", "keep_11"))
+        early_mades = sbuf([P, 3 * HALF], F32, "early_mades", "keep_10")
+        for place, (b, h) in enumerate(((0, 1), (1, 0), (1, 1))):
+            made_term(b, h, early_mades[:, half(place)])
+        early_sums = sbuf([P, HALF + P], F32, "early_sums", "keep_11")
+        gpsimd_sum(0, 0, HALF, early_sums[:, 0:HALF])
+        gpsimd_sum(0, HALF, P, early_sums[:, HALF:])
+        store(0, slice(0, HALF + P), early_sums[:])
 
         for b in (2, 3):
             for h in range(2):
@@ -282,20 +284,20 @@ def tile_list_hwayt_mix_relu_kernel(
         for h in range(2):
             made_term(3, h, unit(f"made_3{h}"))
         late_sums = sbuf([P, J], F32, "late_sums", 0)
-        gpsimd_sum(1, 1, late_sums[:, half(0)])
-        gpsimd_sum(2, 0, late_sums[:, half(1)])
+        gpsimd_sum(0, HALF + P, HALF - P, late_sums[:, 0 : HALF - P])
+        store(0, slice(HALF + P, J), late_sums[:, 0 : HALF - P])
+        gpsimd_sum(2, 0, HALF, late_sums[:, half(1)])
+        store(2, half(0), late_sums[:, half(1)])
         kept_3 = sbuf([P, J + HALF], F32, "kept_3", "codes_11")
         nc.vector.tensor_tensor(kept_3[:, half(2)], mades[2, 1], kepts[2, 1], ALU.add)
         store(2, half(1), kept_3[:, half(2)])
         for h in range(2):
             kept_term(3, h, kept_3[:, half(h)])
 
-        turned_01 = late_sigmoids[:, half(4)]
-        turned_10 = late_sigmoids[:, half(5)]
-        turned_sum(0, 1, 0, turned_01)
-        turned_sum(1, 0, 1, turned_10)
-        turn_back(0, 1, 2, turned_01)
-        turn_back(1, 0, 3, turned_10)
+        for h in range(2):
+            turned_sum(1, h, h, late_sigmoids[:, half(4 + h)])
+        for h in range(2):
+            turn_back(1, h, 2 + h, late_sigmoids[:, half(4 + h)])
 
         for h, first, width in ((0, 0, HALF), (1, 0, QUARTER), (1, QUARTER, QUARTER)):
             cols = slice(first, first + width)

@@ -29,6 +29,8 @@ PAIR = 2 * P
 SC_ROWS = 32
 UNIT_BYTES = 4 * HALF
 KEEP_AT = 4 * UNIT_BYTES - UNIT_BYTES // 2
+EARLY_AT = 8 * UNIT_BYTES
+LATE_AT = 12 * UNIT_BYTES
 
 
 def tile_list_hwayt_mix_relu_kernel(
@@ -103,19 +105,17 @@ def tile_list_hwayt_mix_relu_kernel(
             nc.sync.dma_start(raws[w, a][:], rows.rearrange("(p i) n -> p i n", i=PACK))
 
         def round_wh(w, a, place):
-            pieces = ((slice(0, PAIR), 1.0),) if w == 0 else ((slice(0, P), 1.0), (slice(P, PAIR), -1.0))
-            for cols, sign in pieces:
-                nc.scalar.activation(
-                    place[:, cols, :].rearrange("p (c e) i -> p c i e", e=4),
-                    raws[w, a][:, :, cols].rearrange("p i (c e) -> p c i e", e=4),
-                    ACT.Copy,
-                    scale=sign,
-                )
+            nc.scalar.activation(
+                place.rearrange("p (c e) i -> p c i e", e=4),
+                raws[w, a][:].rearrange("p i (c e) -> p c i e", e=4),
+                ACT.Copy,
+                scale=(1.0, -1.0)[w],
+            )
 
-        def quantize_wh(w, passes):
+        def quantize_wh(w, passes, slot=None):
             name = f"{w}{passes[-1]}"
             width = len(passes) * PAIR
-            grouped = sbuf([P, width, PACK], BF16, f"rounded_{name}")
+            grouped = sbuf([P, width, PACK], BF16, f"rounded_{name}", slot)
             for place, a in enumerate(passes):
                 round_wh(w, a, grouped[:, place * PAIR : (place + 1) * PAIR, :])
             codes = sbuf([P, width], U32, f"codes_{name}")
@@ -159,16 +159,16 @@ def tile_list_hwayt_mix_relu_kernel(
         parted_1 = sbuf([P, PASSES, HALF], U16, "parted_1", "raw_00")
         part_words(parted_1[:], picked_1)
         load_wg(1, "rounded_00", "picked_1")
-        quantize_wh(0, (1,))
+        quantize_wh(0, (1,), LATE_AT - UNIT_BYTES // 2)
         load_wh(1, 0, "raw_01")
-        load_wh(1, 1, "rounded_01")
+        load_wh(1, 1, LATE_AT - UNIT_BYTES // 2)
         parted = (parted_0, parted_1)
 
         def moving(a, h):
             return dict(rhs=parted[h][:, a, :].bitcast(FP4X4), rhs_scale=planes[:, a, half(h)])
 
         def gate_product(b, h):
-            ga = bank("ga", 2 * (b % 2) + h)
+            ga = bank("ga", (0, 2, 0, 5)[b] + h)
             scale_cols = slice(J + b * P, J + (b + 1) * P)
             own = slice((b % 2) * P, (b % 2 + 1) * P)
             nc.tensor.matmul_mx(
@@ -182,7 +182,7 @@ def tile_list_hwayt_mix_relu_kernel(
             gate_banks[b, h] = ga
 
         def feature_product(b, h):
-            ha = bank("ha", 4 + 2 * (b % 2) + h)
+            ha = bank("ha", ((4, 5), (6, 7), (4, 7), (2, 3))[b][h])
             for a in range(PASSES):
                 codes, scales = wh_q[b, a]
                 nc.tensor.matmul_mx(
@@ -202,15 +202,21 @@ def tile_list_hwayt_mix_relu_kernel(
             gates[b, h] = place
             nc.scalar.activation(place, gate_banks[b, h][:], ACT.Sigmoid, bias=bias[:, b : b + 1])
 
-        def kept_term(b, h, place):
+        def kept_term(b, h, place, pieces=1):
             kepts[b, h] = place
-            nc.vector.tensor_tensor(place, carried[b][:].indirect(listed(h * HALF, HALF)), keeps[b, h], ALU.mult)
+            width = HALF // pieces
+            for first in range(0, HALF, width):
+                cols = slice(first, first + width)
+                window = carried[b][:].indirect(listed(h * HALF + first, width))
+                nc.vector.tensor_tensor(place[:, cols], window, keeps[b, h][:, cols], ALU.mult)
 
         def made_term(b, h, place):
             mades[b, h] = place
             ha = feature_product(b, h)
-            if b == LAST:
+            if (b, h) not in gates:
                 nc.vector.scalar_tensor_tensor(place, keeps[b, h], 1.0, ha[:], ALU.subtract, ALU.mult)
+            elif b >= 2:
+                nc.vector.scalar_tensor_tensor(place, ha[:], 0.0, gates[b, h], ALU.min, ALU.mult)
             else:
                 nc.vector.scalar_tensor_tensor(place, ha[:], 0.0, gates[b, h], ALU.max, ALU.mult)
 
@@ -220,7 +226,13 @@ def tile_list_hwayt_mix_relu_kernel(
         def gpsimd_sum(b, first, width, place):
             h, start = divmod(first, HALF)
             cols = slice(start, start + width)
-            nc.gpsimd.tensor_tensor(place, mades[b, h][:, cols], kepts[b, h][:, cols], ALU.add)
+            nc.gpsimd.tensor_tensor(place, kepts[b, h][:, cols], mades[b, h][:, cols], ALU.subtract if b >= 2 else ALU.add)
+
+        def vector_sum(b, first, width, place):
+            h, start = divmod(first, HALF)
+            cols = slice(start, start + width)
+            nc.vector.scalar_tensor_tensor(place, mades[b, h][:, cols], 0.0, kepts[b, h][:, cols], ALU.max, ALU.add)
+            store(b, slice(first, first + width), place)
 
         def turned_sum(b, h, number, place):
             acc = bank("acc", number)
@@ -251,16 +263,16 @@ def tile_list_hwayt_mix_relu_kernel(
         kept_term(0, 1, unit("kept_01"))
         load_r(3, "keep_01")
         made_term(0, 0, unit("made_00", 4 * UNIT_BYTES))
-        for h in range(2):
-            keep_of(1, h, unit(f"keep_1{h}"))
+        keep_of(1, 0, unit("keep_10", EARLY_AT - UNIT_BYTES // 2))
+        keep_of(1, 1, unit("keep_11"))
         for h in range(2):
             gate_of(1, h, unit(f"gate_1{h}"))
         for h in range(2):
             kept_term(1, h, unit(f"kept_1{h}"))
-        early_mades = sbuf([P, 3 * HALF], F32, "early_mades", "keep_10")
+        early_mades = sbuf([P, 3 * HALF], F32, "early_mades", EARLY_AT - 3 * UNIT_BYTES)
         for place, (b, h) in enumerate(((0, 1), (1, 0), (1, 1))):
             made_term(b, h, early_mades[:, half(place)])
-        early_sums = sbuf([P, HALF + P], F32, "early_sums", "keep_11")
+        early_sums = sbuf([P, HALF + P], F32, "early_sums", EARLY_AT)
         gpsimd_sum(0, 0, HALF, early_sums[:, 0:HALF])
         gpsimd_sum(0, HALF, P, early_sums[:, HALF:])
         store(0, slice(0, HALF + P), early_sums[:])
@@ -269,38 +281,34 @@ def tile_list_hwayt_mix_relu_kernel(
             for h in range(2):
                 gate_product(b, h)
         quantize_wh(1, (0, 1))
-        late_sigmoids = sbuf([P, 7 * HALF], F32, "late_sigmoids", "raw_01")
-        keep_of(2, 0, unit("keep_20", "rounded_01"))
-        keep_of(2, 1, late_sigmoids[:, half(6)])
-        for h in range(2):
-            gate_of(2, h, late_sigmoids[:, half(h)])
+        late_sigmoids = sbuf([P, 6 * HALF], F32, "late_sigmoids", "raw_01")
+        keep_of(2, 0, unit("keep_20", LATE_AT - UNIT_BYTES // 2))
+        keep_of(2, 1, late_sigmoids[:, half(1)])
+        gate_of(2, 0, late_sigmoids[:, half(0)])
         for h in range(2):
             keep_of(3, h, late_sigmoids[:, half(2 + h)])
         for h in range(2):
             kept_term(2, h, unit(f"kept_2{h}"))
-        late_mades = sbuf([P, J], F32, "late_mades", "rounded_01")
+        late_mades = sbuf([P, J], F32, "late_mades", LATE_AT - 2 * UNIT_BYTES)
         for h in range(2):
             made_term(2, h, late_mades[:, half(h)])
         for h in range(2):
             made_term(3, h, unit(f"made_3{h}"))
-        late_sums = sbuf([P, J], F32, "late_sums", 0)
+        late_sums = sbuf([P, J], F32, "late_sums", LATE_AT)
         gpsimd_sum(0, HALF + P, HALF - P, late_sums[:, 0 : HALF - P])
         store(0, slice(HALF + P, J), late_sums[:, 0 : HALF - P])
         gpsimd_sum(2, 0, HALF, late_sums[:, half(1)])
         store(2, half(0), late_sums[:, half(1)])
         kept_3 = sbuf([P, J + HALF], F32, "kept_3", "codes_11")
-        nc.vector.tensor_tensor(kept_3[:, half(2)], mades[2, 1], kepts[2, 1], ALU.add)
-        store(2, half(1), kept_3[:, half(2)])
-        for h in range(2):
-            kept_term(3, h, kept_3[:, half(h)])
+        kept_term(3, 0, kept_3[:, half(0)])
+        vector_sum(2, HALF, HALF, kept_3[:, half(2)])
+        vector_sum(3, 0, HALF, unit("result_30"))
+        kept_term(3, 1, kept_3[:, half(1)], pieces=2)
 
         for h in range(2):
             turned_sum(1, h, h, late_sigmoids[:, half(4 + h)])
         for h in range(2):
-            turn_back(1, h, 2 + h, late_sigmoids[:, half(4 + h)])
+            turn_back(1, h, 5 + h, late_sigmoids[:, half(4 + h)])
 
-        for h, first, width in ((0, 0, HALF), (1, 0, QUARTER), (1, QUARTER, QUARTER)):
-            cols = slice(first, first + width)
-            result = sbuf([P, width], F32, f"result_3{h}{first}")
-            nc.vector.scalar_tensor_tensor(result[:], mades[3, h][:, cols], 0.0, kepts[3, h][:, cols], ALU.max, ALU.add)
-            store(3, slice(h * HALF + first, h * HALF + first + width), result[:])
+        for first in (HALF, HALF + QUARTER):
+            vector_sum(LAST, first, QUARTER, sbuf([P, QUARTER], F32, f"result_3{first}")[:])

@@ -90,7 +90,7 @@ def tile_list_hwayt_mix_relu_kernel(
         nc.scalar.activation(neg_bias[:], bias_bank[:, 0:BLOCKS], ACT.Copy, scale=-1.0)
 
         wg8, wg4, raws, rounded, wh_q, carried = {}, {}, {}, {}, {}, {}
-        gate_banks, gates, keeps, mades, kepts = {}, {}, {}, {}, {}
+        gate_banks, gates, keeps, mades, kepts, sum_banks = {}, {}, {}, {}, {}, {}
 
         def load_wg(w, slot8, slot4):
             wg8[w] = sbuf([P, PAIR], I32, f"wg8_{w}", slot8)
@@ -182,7 +182,7 @@ def tile_list_hwayt_mix_relu_kernel(
             gate_banks[b, h] = ga
 
         def feature_product(b, h):
-            ha = bank("ha", ((4, 5), (6, 7), (4, 7), (2, 3))[b][h])
+            ha = bank("ha", ((4, 5), (6, 7), (4, 7), (1, 3))[b][h])
             for a in range(PASSES):
                 codes, scales = wh_q[b, a]
                 nc.tensor.matmul_mx(
@@ -234,13 +234,20 @@ def tile_list_hwayt_mix_relu_kernel(
             nc.vector.scalar_tensor_tensor(place, mades[b, h][:, cols], 0.0, kepts[b, h][:, cols], ALU.max, ALU.add)
             store(b, slice(first, first + width), place)
 
-        def turned_sum(b, h, number, place):
-            acc = bank("acc", number)
+        def turn(b, h, term, opens):
             for c in range(HALF // P):
                 cols = slice(c * P, (c + 1) * P)
-                nc.tensor.matmul(acc[:, cols], mades[b, h][:, cols], ident[:], start=True, stop=False, is_transpose=True)
-                nc.tensor.matmul(acc[:, cols], kepts[b, h][:, cols], ident[:], start=False, stop=True, is_transpose=True)
-            nc.scalar.copy(place, acc[:])
+                nc.tensor.matmul(
+                    sum_banks[b, h][:, cols], term[:, cols], ident[:],
+                    start=(opens and c == 0), stop=(not opens and c == HALF // P - 1), is_transpose=True,
+                )
+
+        def turn_kept(b, h, number):
+            sum_banks[b, h] = bank("turned_sum", number)
+            turn(b, h, kepts[b, h], True)
+
+        def turn_made(b, h):
+            turn(b, h, mades[b, h], False)
 
         def turn_back(b, h, number, turned):
             back = bank("back", number)
@@ -269,6 +276,7 @@ def tile_list_hwayt_mix_relu_kernel(
             gate_of(1, h, unit(f"gate_1{h}"))
         for h in range(2):
             kept_term(1, h, unit(f"kept_1{h}"))
+        turn_kept(1, 0, 2)
         early_mades = sbuf([P, 3 * HALF], F32, "early_mades", EARLY_AT - 3 * UNIT_BYTES)
         for place, (b, h) in enumerate(((0, 1), (1, 0), (1, 1))):
             made_term(b, h, early_mades[:, half(place)])
@@ -280,6 +288,7 @@ def tile_list_hwayt_mix_relu_kernel(
         for b in (2, 3):
             for h in range(2):
                 gate_product(b, h)
+        turn_made(1, 0)
         quantize_wh(1, (0, 1))
         late_sigmoids = sbuf([P, 6 * HALF], F32, "late_sigmoids", "raw_01")
         keep_of(2, 0, unit("keep_20", LATE_AT - UNIT_BYTES // 2))
@@ -305,8 +314,10 @@ def tile_list_hwayt_mix_relu_kernel(
         vector_sum(3, 0, HALF, unit("result_30"))
         kept_term(3, 1, kept_3[:, half(1)], pieces=2)
 
+        turn_kept(1, 1, 0)
+        turn_made(1, 1)
         for h in range(2):
-            turned_sum(1, h, h, late_sigmoids[:, half(4 + h)])
+            nc.scalar.copy(late_sigmoids[:, half(4 + h)], sum_banks[1, h][:])
         for h in range(2):
             turn_back(1, h, 5 + h, late_sigmoids[:, half(4 + h)])
 

@@ -22,15 +22,12 @@ PACK = 4
 K_PASS = P * PACK
 PASSES = K // K_PASS
 BLOCKS = N // P
-LAST = BLOCKS - 1
 HALF = 512
 QUARTER = 256
 PAIR = 2 * P
 SC_ROWS = 32
-UNIT_BYTES = 4 * HALF
-KEEP_AT = 4 * UNIT_BYTES - UNIT_BYTES // 2
-EARLY_AT = 8 * UNIT_BYTES
-LATE_AT = 12 * UNIT_BYTES
+KIB = 1024
+LATE_RAW = 37 * KIB + KIB // 2
 
 
 def tile_list_hwayt_mix_relu_kernel(
@@ -42,16 +39,19 @@ def tile_list_hwayt_mix_relu_kernel(
         laid = ctx.enter_context(tc.tile_pool(name="laid", bufs=1))
         psum = ctx.enter_context(tc.psum_pool(name="psum", bufs=1))
 
-        def sbuf(shape, dtype, name, slot=None):
-            if isinstance(slot, int):
-                return laid.tile(shape, dtype, name=name, offset=slot, align_bytes=64)
-            return held.tile(shape, dtype, name=name, tag=slot or name, align_bytes=64)
+        def sbuf(shape, dtype, name, at=None):
+            if at is None:
+                return held.tile(shape, dtype, name=name, align_bytes=64)
+            return laid.tile(shape, dtype, name=name, offset=at, align_bytes=256)
 
         def bank(name, number, width=HALF):
             return psum.tile([P, width], F32, name=name, tag=f"bank_{number}")
 
         def half(h):
             return slice(h * HALF, (h + 1) * HALF)
+
+        def unit(name, at=None):
+            return sbuf([P, HALF], F32, name, at)[:]
 
         offsets = held.tile([P, J // 16], U16, name="offsets")
         nc.sync.dma_start(offsets[:], offs)
@@ -64,7 +64,7 @@ def tile_list_hwayt_mix_relu_kernel(
         nc.vector.memset(tab_sc[32:64, :].bitcast(I32), 0)
         nc.vector.memset(tab_sc[64:128, :].bitcast(I32), 0)
 
-        table = sbuf([P, T], I32, "table")
+        table = sbuf([P, T], I32, "table", 24 * KIB)
         nc.sync.dma_start(table[:], tab_words[0].rearrange("p t b -> p (t b)").bitcast(I32))
 
         joined = sbuf([SC_ROWS, J + N], U8, "joined")
@@ -89,86 +89,87 @@ def tile_list_hwayt_mix_relu_kernel(
         neg_bias = sbuf([P, BLOCKS], F32, "neg_bias")
         nc.scalar.activation(neg_bias[:], bias_bank[:, 0:BLOCKS], ACT.Copy, scale=-1.0)
 
-        wg8, wg4, raws, rounded, wh_q, carried = {}, {}, {}, {}, {}, {}
-        gate_banks, gates, keeps, mades, kepts, sum_banks = {}, {}, {}, {}, {}, {}
+        wg8, wg4, raws, wh_q, carried = {}, {}, {}, {}, {}
+        gate_banks, feature_banks, sum_banks = {}, {}, {}
+        gates, keeps, mades, kepts = {}, {}, {}, {}
 
-        def load_wg(w, slot8, slot4):
-            wg8[w] = sbuf([P, PAIR], I32, f"wg8_{w}", slot8)
+        def load_wg(w, at8=None, at4=None):
+            wg8[w] = sbuf([P, PAIR], I32, f"wg8_{w}", at8)
             words8 = wg8_words[0].rearrange("p n b -> p (n b)").bitcast(I32)
             nc.sync.dma_start(wg8[w][:], words8[:, w * PAIR : (w + 1) * PAIR])
-            wg4[w] = sbuf([P, 2 * PAIR], U8, f"wg4_{w}", slot4)
+            wg4[w] = sbuf([P, 2 * PAIR], U8, f"wg4_{w}", at4)
             nc.sync.dma_start(wg4[w][:].bitcast(I32), wg4_words[0][:, 2 * w * PAIR : 2 * (w + 1) * PAIR].bitcast(I32))
 
-        def load_wh(w, a, slot):
-            raws[w, a] = sbuf([P, PACK, PAIR], F32, f"raw_{w}{a}", slot)
+        def load_wh(w, a, at=None):
+            raws[w, a] = sbuf([P, PACK, PAIR], F32, f"raw_{w}{a}", at)
             rows = wh[a * K_PASS : (a + 1) * K_PASS, w * PAIR : (w + 1) * PAIR]
             nc.sync.dma_start(raws[w, a][:], rows.rearrange("(p i) n -> p i n", i=PACK))
 
-        def round_wh(w, a, place):
+        def load_r(b, at):
+            carried[b] = sbuf([P, T], F32, f"carried_{b}", at)
+            nc.sync.dma_start(carried[b][:], rT[b * P : (b + 1) * P, :])
+
+        def round_wh(b, a, place, blocks=1):
+            own = slice((b % 2) * P, (b % 2 + blocks) * P)
             nc.scalar.activation(
                 place.rearrange("p (c e) i -> p c i e", e=4),
-                raws[w, a][:].rearrange("p i (c e) -> p c i e", e=4),
+                raws[b // 2, a][:, :, own].rearrange("p i (c e) -> p c i e", e=4),
                 ACT.Copy,
-                scale=(1.0, -1.0)[w],
+                scale=-1.0 if b == BLOCKS - 1 else 1.0,
             )
 
-        def quantize_wh(w, passes, slot=None):
-            name = f"{w}{passes[-1]}"
-            width = len(passes) * PAIR
-            grouped = sbuf([P, width, PACK], BF16, f"rounded_{name}", slot)
-            for place, a in enumerate(passes):
-                round_wh(w, a, grouped[:, place * PAIR : (place + 1) * PAIR, :])
-            codes = sbuf([P, width], U32, f"codes_{name}")
-            scales = sbuf([P, width], U8, f"scales_{name}")
+        def quantize_wh(pieces, grouped, at=None):
+            name = "".join(f"{b}{a}" for b, a in pieces)
+            codes = sbuf([P, len(pieces) * P], U32, f"codes_{name}", at)
+            scales = sbuf([P, len(pieces) * P], U8, f"scales_{name}")
             nc.vector.quantize_mx(
                 out=codes[:].bitcast(FP8X4), scales=scales[:], in_=grouped[:].rearrange("p n i -> p (n i)")
             )
-            for place, a in enumerate(passes):
-                for c in range(2):
-                    cols = slice(place * PAIR + c * P, place * PAIR + (c + 1) * P)
-                    wh_q[2 * w + c, a] = (codes[:, cols], scales[:, cols])
+            for place, piece in enumerate(pieces):
+                cols = slice(place * P, (place + 1) * P)
+                wh_q[piece] = (codes[:, cols], scales[:, cols])
 
-        def load_r(b, slot):
-            carried[b] = sbuf([P, T], F32, f"carried_{b}", slot)
-            nc.sync.dma_start(carried[b][:], rT[b * P : (b + 1) * P, :])
+        def gather_words(h, at):
+            picked = sbuf([P, HALF], U32, f"picked_{h}", at)
+            nc.vector.tensor_copy(picked[:], table[:].bitcast(U32).indirect(listed(h * HALF, HALF)))
+            return picked
 
-        load_wg(0, "wg8_0", "wg4_0")
-        load_wh(0, 0, "raw_00")
-        load_wh(0, 1, "raw_01")
+        def part_words(h, picked):
+            words = sbuf([P, PASSES, HALF], U16, f"parted_{h}")
+            nc.vector.tensor_copy(words[:], picked[:].bitcast(U16).rearrange("p (t d) -> p d t", d=2))
+            return words
 
-        picked_sc = sbuf([P, J], U8, "picked_sc")
+        load_wg(0)
+        for a in range(PASSES):
+            load_wh(0, a)
+
+        picked_sc = sbuf([P, J], U8, "picked_sc", 0)
         nc.vector.tensor_copy(picked_sc[:], tab_sc[:].indirect(offsets[:]))
         nc.vector.tensor_copy(joined[:, 0:J].bitcast(I32), picked_sc[0:SC_ROWS, :].bitcast(I32))
         for q in (0, 2, 1, 3):
             nc.sync.dma_start(planes[32 * q : 32 * q + 4].bitcast(I32), joined[8 * q : 8 * q + 8, :].bitcast(I32))
-        load_r(0, "picked_sc")
+        load_r(0, 0)
 
-        def gather_words(name, first, count, slot=None):
-            picked = sbuf([P, count], U32, name, slot)
-            nc.vector.tensor_copy(picked[:], table[:].bitcast(U32).indirect(listed(first, count)))
-            return picked
-
-        def part_words(parted, picked):
-            nc.vector.tensor_copy(parted, picked[:].bitcast(U16).rearrange("p (t d) -> p d t", d=2))
-
-        parted_0 = sbuf([P, PASSES, HALF], U16, "parted_0")
-        part_words(parted_0[:], gather_words("picked_0", 0, HALF))
-        picked_1 = gather_words("picked_1", HALF, HALF)
-        load_r(1, "table")
-        quantize_wh(0, (0,))
-        parted_1 = sbuf([P, PASSES, HALF], U16, "parted_1", "raw_00")
-        part_words(parted_1[:], picked_1)
-        load_wg(1, "rounded_00", "picked_1")
-        quantize_wh(0, (1,), LATE_AT - UNIT_BYTES // 2)
-        load_wh(1, 0, "raw_01")
-        load_wh(1, 1, LATE_AT - UNIT_BYTES // 2)
-        parted = (parted_0, parted_1)
+        parted = [part_words(0, gather_words(0, 36 * KIB - 256))]
+        picked_1 = gather_words(1, 53 * KIB - KIB)
+        load_r(1, 24 * KIB)
+        load_wh(1, 0, 32 * KIB)
+        load_wh(1, 1, LATE_RAW)
+        load_wg(1, 36 * KIB, 37 * KIB)
+        for a in range(PASSES):
+            grouped = sbuf([P, PAIR, PACK], BF16, f"grouped_0{a}")
+            round_wh(0, a, grouped[:], 2)
+            quantize_wh(((0, a), (1, a)), grouped)
+            if a == 0:
+                parted.append(part_words(1, picked_1))
+        load_r(2, 45 * KIB)
+        load_r(3, 53 * KIB)
 
         def moving(a, h):
             return dict(rhs=parted[h][:, a, :].bitcast(FP4X4), rhs_scale=planes[:, a, half(h)])
 
-        def gate_product(b, h):
-            ga = bank("ga", (0, 2, 0, 5)[b] + h)
+        def gate_product(b, h, number):
+            ga = bank("ga", number)
             scale_cols = slice(J + b * P, J + (b + 1) * P)
             own = slice((b % 2) * P, (b % 2 + 1) * P)
             nc.tensor.matmul_mx(
@@ -176,65 +177,53 @@ def tile_list_hwayt_mix_relu_kernel(
                 start=True, stop=False, **moving(0, h),
             )
             nc.tensor.matmul_mx(
-                out=ga[:], lhsT=wg4[b // 2][:, 2 * own.start : 2 * own.stop].bitcast(FP4X4), lhsT_scale=planes[:, 1, scale_cols],
-                start=False, stop=True, **moving(1, h),
+                out=ga[:], lhsT=wg4[b // 2][:, 2 * own.start : 2 * own.stop].bitcast(FP4X4),
+                lhsT_scale=planes[:, 1, scale_cols], start=False, stop=True, **moving(1, h),
             )
             gate_banks[b, h] = ga
 
-        def feature_product(b, h):
-            ha = bank("ha", ((4, 5), (6, 7), (4, 7), (1, 3))[b][h])
-            for a in range(PASSES):
+        def feature_product(b, h, number, passes=(0, 1)):
+            feature_banks[b, h] = bank("ha", number)
+            for a in passes:
                 codes, scales = wh_q[b, a]
                 nc.tensor.matmul_mx(
-                    out=ha[:], lhsT=codes.bitcast(FP8X4), lhsT_scale=scales,
-                    start=(a == 0), stop=(a == PASSES - 1), **moving(a, h),
+                    out=feature_banks[b, h][:], lhsT=codes.bitcast(FP8X4), lhsT_scale=scales,
+                    start=(a == passes[0]), stop=(a == passes[-1]), **moving(a, h),
                 )
-            return ha
 
-        def unit(name, slot=None):
-            return sbuf([P, HALF], F32, name, slot)[:]
-
-        def keep_of(b, h, place):
-            keeps[b, h] = place
-            nc.scalar.activation(place, gate_banks[b, h][:], ACT.Sigmoid, bias=neg_bias[:, b : b + 1], scale=-1.0)
+        def keep_of(b, h, place, first=0, width=HALF):
+            keeps[b, h, first] = place
+            ga = gate_banks[b, h][:, first : first + width]
+            nc.scalar.activation(place, ga, ACT.Sigmoid, bias=neg_bias[:, b : b + 1], scale=-1.0)
 
         def gate_of(b, h, place):
             gates[b, h] = place
             nc.scalar.activation(place, gate_banks[b, h][:], ACT.Sigmoid, bias=bias[:, b : b + 1])
 
-        def kept_term(b, h, place, pieces=1):
+        def kept_term(b, h, place, first=0, width=HALF, keep_first=0):
             kepts[b, h] = place
-            width = HALF // pieces
-            for first in range(0, HALF, width):
-                cols = slice(first, first + width)
-                window = carried[b][:].indirect(listed(h * HALF + first, width))
-                nc.vector.tensor_tensor(place[:, cols], window, keeps[b, h][:, cols], ALU.mult)
+            window = carried[b][:].indirect(listed(h * HALF + first, width))
+            keep = keeps[b, h, keep_first][:, first - keep_first : first - keep_first + width]
+            nc.vector.tensor_tensor(place[:, first : first + width], window, keep, ALU.mult)
 
         def made_term(b, h, place):
             mades[b, h] = place
-            ha = feature_product(b, h)
-            if (b, h) not in gates:
-                nc.vector.scalar_tensor_tensor(place, keeps[b, h], 1.0, ha[:], ALU.subtract, ALU.mult)
-            elif b >= 2:
-                nc.vector.scalar_tensor_tensor(place, ha[:], 0.0, gates[b, h], ALU.min, ALU.mult)
+            ha = feature_banks[b, h]
+            if b == BLOCKS - 1:
+                nc.vector.scalar_tensor_tensor(place, keeps[b, h, 0], 1.0, ha[:], ALU.subtract, ALU.mult)
             else:
                 nc.vector.scalar_tensor_tensor(place, ha[:], 0.0, gates[b, h], ALU.max, ALU.mult)
 
-        def store(b, cols, result):
-            nc.sync.dma_start(out[b * P : (b + 1) * P, cols], result)
+        def vector_sum(h, first, width):
+            cols = slice(first, first + width)
+            result = sbuf([P, width], F32, f"result_3{h}{first}")
+            nc.vector.scalar_tensor_tensor(result[:], mades[3, h][:, cols], 0.0, kepts[3, h][:, cols], ALU.max, ALU.add)
+            nc.sync.dma_start(out[3 * P :, h * HALF + first : h * HALF + first + width], result[:])
 
-        def gpsimd_sum(b, first, width, place):
-            h, start = divmod(first, HALF)
-            cols = slice(start, start + width)
-            nc.gpsimd.tensor_tensor(place, kepts[b, h][:, cols], mades[b, h][:, cols], ALU.subtract if b >= 2 else ALU.add)
-
-        def vector_sum(b, first, width, place):
-            h, start = divmod(first, HALF)
-            cols = slice(start, start + width)
-            nc.vector.scalar_tensor_tensor(place, mades[b, h][:, cols], 0.0, kepts[b, h][:, cols], ALU.max, ALU.add)
-            store(b, slice(first, first + width), place)
-
-        def turn(b, h, term, opens):
+        def turn(b, h, term, number=None):
+            opens = number is not None
+            if opens:
+                sum_banks[b, h] = bank("turned_sum", number)
             for c in range(HALF // P):
                 cols = slice(c * P, (c + 1) * P)
                 nc.tensor.matmul(
@@ -242,14 +231,12 @@ def tile_list_hwayt_mix_relu_kernel(
                     start=(opens and c == 0), stop=(not opens and c == HALF // P - 1), is_transpose=True,
                 )
 
-        def turn_kept(b, h, number):
-            sum_banks[b, h] = bank("turned_sum", number)
-            turn(b, h, kepts[b, h], True)
+        def leave_bank(b, h):
+            turned = unit(f"turned_{b}{h}")
+            nc.scalar.copy(turned, sum_banks[b, h][:])
+            return turned
 
-        def turn_made(b, h):
-            turn(b, h, mades[b, h], False)
-
-        def turn_back(b, h, number, turned):
+        def turn_back(b, h, turned, number):
             back = bank("back", number)
             for c in range(HALF // P):
                 cols = slice(c * P, (c + 1) * P)
@@ -260,66 +247,77 @@ def tile_list_hwayt_mix_relu_kernel(
 
         for b in range(2):
             for h in range(2):
-                gate_product(b, h)
-        keep_of(0, 0, unit("keep_00", KEEP_AT))
-        keep_of(0, 1, unit("keep_01"))
+                gate_product(b, h, 2 * b + h)
+            for h in range(2 - 2 * b):
+                feature_product(b, h, 4 + h)
+        for h in range(2):
+            keep_of(0, h, unit(f"keep_0{h}", (66 * KIB, None)[h]))
         for h in range(2):
             gate_of(0, h, unit(f"gate_0{h}"))
-        kept_term(0, 0, unit("kept_00"))
-        load_r(2, 0)
-        kept_term(0, 1, unit("kept_01"))
-        load_r(3, "keep_01")
-        made_term(0, 0, unit("made_00", 4 * UNIT_BYTES))
-        keep_of(1, 0, unit("keep_10", EARLY_AT - UNIT_BYTES // 2))
-        keep_of(1, 1, unit("keep_11"))
+        kept_0 = sbuf([P, J], F32, "kept_0")
+        made_0 = sbuf([P, J], F32, "made_0", 66 * KIB)
         for h in range(2):
-            gate_of(1, h, unit(f"gate_1{h}"))
+            kept_term(0, h, kept_0[:, half(h)])
+        for h in range(2):
+            made_term(0, h, made_0[:, half(h)])
+        for h in range(2):
+            keep_of(1, h, unit(f"keep_1{h}"))
+        gate_of(1, 0, unit("gate_10"))
         for h in range(2):
             kept_term(1, h, unit(f"kept_1{h}"))
-        turn_kept(1, 0, 2)
-        early_mades = sbuf([P, 3 * HALF], F32, "early_mades", EARLY_AT - 3 * UNIT_BYTES)
-        for place, (b, h) in enumerate(((0, 1), (1, 0), (1, 1))):
-            made_term(b, h, early_mades[:, half(place)])
-        early_sums = sbuf([P, HALF + P], F32, "early_sums", EARLY_AT)
-        gpsimd_sum(0, 0, HALF, early_sums[:, 0:HALF])
-        gpsimd_sum(0, HALF, P, early_sums[:, HALF:])
-        store(0, slice(0, HALF + P), early_sums[:])
+        for h in range(2):
+            feature_product(1, h, (5, 2)[h])
 
-        for b in (2, 3):
-            for h in range(2):
-                gate_product(b, h)
-        turn_made(1, 0)
-        quantize_wh(1, (0, 1))
-        late_sigmoids = sbuf([P, 6 * HALF], F32, "late_sigmoids", "raw_01")
-        keep_of(2, 0, unit("keep_20", LATE_AT - UNIT_BYTES // 2))
-        keep_of(2, 1, late_sigmoids[:, half(1)])
-        gate_of(2, 0, late_sigmoids[:, half(0)])
+        grouped = [sbuf([P, PAIR, PACK], BF16, f"grouped_1{a}", (None, 62 * KIB)[a]) for a in range(PASSES)]
+        for a in range(PASSES):
+            for b in (2, 3):
+                round_wh(b, a, grouped[a][:, (b - 2) * P : (b - 1) * P, :])
+        gate_of(1, 1, unit("gate_11", LATE_RAW + KIB))
+        quantize_wh(((2, 1), (3, 1)), grouped[1])
+        quantize_wh(((2, 0), (3, 0)), grouped[0], LATE_RAW)
         for h in range(2):
-            keep_of(3, h, late_sigmoids[:, half(2 + h)])
+            gate_product(2, h, h)
         for h in range(2):
-            kept_term(2, h, unit(f"kept_2{h}"))
-        late_mades = sbuf([P, J], F32, "late_mades", LATE_AT - 2 * UNIT_BYTES)
+            feature_product(2, h, 6 + h, (1, 0))
+        gate_product(3, 0, 3)
+        result_0 = sbuf([P, J], F32, "result_0", 62 * KIB)
+        nc.gpsimd.tensor_tensor(result_0[:], kept_0[:], made_0[:], ALU.add)
+        nc.sync.dma_start(out[0:P, :], result_0[:])
+        made_1 = sbuf([P, J], F32, "made_1", LATE_RAW + 3 * KIB)
         for h in range(2):
-            made_term(2, h, late_mades[:, half(h)])
+            made_term(1, h, made_1[:, half(h)])
+        gate_product(3, 1, 5)
+        for h in range(2):
+            turn(1, h, mades[1, h], (4, 2)[h])
+            turn(1, h, kepts[1, h])
+        for h in range(2):
+            gate_of(2, h, unit(f"gate_2{h}"))
+        for h in range(2):
+            made_term(2, h, unit(f"made_2{h}"))
+        turn(2, 0, mades[2, 0], 6)
+        for h in range(2):
+            keep_of(2, h, unit(f"keep_2{h}"))
+        keep_of(3, 0, unit("keep_30", 70 * KIB))
+        keep_of(3, 1, unit("keep_31"))
+        kept_term(2, 0, unit("kept_20"))
+        turn(2, 0, kepts[2, 0])
+        kept_term(2, 1, unit("kept_21"))
+        result_21 = unit("result_21")
+        nc.gpsimd.tensor_tensor(result_21, kepts[2, 1], mades[2, 1], ALU.add)
+        nc.sync.dma_start(out[2 * P : 3 * P, half(1)], result_21)
+        kept_term(3, 0, unit("kept_30"))
+
+        for h in range(2):
+            feature_product(3, h, (3, 5)[h])
+        turned = {piece: leave_bank(*piece) for piece in ((1, 0), (1, 1), (2, 0))}
         for h in range(2):
             made_term(3, h, unit(f"made_3{h}"))
-        late_sums = sbuf([P, J], F32, "late_sums", LATE_AT)
-        gpsimd_sum(0, HALF + P, HALF - P, late_sums[:, 0 : HALF - P])
-        store(0, slice(HALF + P, J), late_sums[:, 0 : HALF - P])
-        gpsimd_sum(2, 0, HALF, late_sums[:, half(1)])
-        store(2, half(0), late_sums[:, half(1)])
-        kept_3 = sbuf([P, J + HALF], F32, "kept_3", "codes_11")
-        kept_term(3, 0, kept_3[:, half(0)])
-        vector_sum(2, HALF, HALF, kept_3[:, half(2)])
-        vector_sum(3, 0, HALF, unit("result_30"))
-        kept_term(3, 1, kept_3[:, half(1)], pieces=2)
+        for number, (b, h) in zip((0, 1, 7), turned):
+            turn_back(b, h, turned[b, h], number)
 
-        turn_kept(1, 1, 0)
-        turn_made(1, 1)
-        for h in range(2):
-            nc.scalar.copy(late_sigmoids[:, half(4 + h)], sum_banks[1, h][:])
-        for h in range(2):
-            turn_back(1, h, 5 + h, late_sigmoids[:, half(4 + h)])
-
-        for first in (HALF, HALF + QUARTER):
-            vector_sum(LAST, first, QUARTER, sbuf([P, QUARTER], F32, f"result_3{first}")[:])
+        vector_sum(0, 0, HALF)
+        kept_31 = unit("kept_31", 70 * KIB)
+        for first in (0, QUARTER):
+            kept_term(3, 1, kept_31, first, QUARTER)
+        for first in (0, QUARTER):
+            vector_sum(1, first, QUARTER)

@@ -100,20 +100,22 @@ def tile_list_hwayt_mix_relu_kernel(
             wg4[w] = sbuf([P, 2 * PAIR], U8, f"wg4_{w}", at4)
             nc.sync.dma_start(wg4[w][:].bitcast(I32), wg4_words[0][:, 2 * w * PAIR : 2 * (w + 1) * PAIR].bitcast(I32))
 
-        def load_wh(w, a, at=None):
-            raws[w, a] = sbuf([P, PACK, PAIR], F32, f"raw_{w}{a}", at)
-            rows = wh[a * K_PASS : (a + 1) * K_PASS, w * PAIR : (w + 1) * PAIR]
-            nc.sync.dma_start(raws[w, a][:], rows.rearrange("(p i) n -> p i n", i=PACK))
+        def load_wh(b, a, blocks, at=None):
+            raw = sbuf([P, PACK, blocks * P], F32, f"raw_{b}{a}", at)
+            rows = wh[a * K_PASS : (a + 1) * K_PASS, b * P : (b + blocks) * P]
+            nc.sync.dma_start(raw[:], rows.rearrange("(p i) n -> p i n", i=PACK))
+            for c in range(blocks):
+                raws[b + c, a] = (raw, c * P)
 
         def load_r(b, at):
             carried[b] = sbuf([P, T], F32, f"carried_{b}", at)
             nc.sync.dma_start(carried[b][:], rT[b * P : (b + 1) * P, :])
 
         def round_wh(b, a, place, blocks=1):
-            own = slice((b % 2) * P, (b % 2 + blocks) * P)
+            raw, first = raws[b, a]
             nc.scalar.activation(
                 place.rearrange("p (c e) i -> p c i e", e=4),
-                raws[b // 2, a][:, :, own].rearrange("p i (c e) -> p c i e", e=4),
+                raw[:, :, first : first + blocks * P].rearrange("p i (c e) -> p c i e", e=4),
                 ACT.Copy,
                 scale=-1.0 if b == BLOCKS - 1 else 1.0,
             )
@@ -141,7 +143,7 @@ def tile_list_hwayt_mix_relu_kernel(
 
         load_wg(0)
         for a in range(PASSES):
-            load_wh(0, a)
+            load_wh(0, a, 2, (None, 64 * KIB)[a])
 
         picked_sc = sbuf([P, J], U8, "picked_sc", 0)
         nc.vector.tensor_copy(picked_sc[:], tab_sc[:].indirect(offsets[:]))
@@ -151,10 +153,10 @@ def tile_list_hwayt_mix_relu_kernel(
         load_r(0, 0)
 
         parted = [part_words(0, gather_words(0, 36 * KIB - 256))]
-        picked_1 = gather_words(1, 53 * KIB - KIB)
+        picked_1 = gather_words(1, 53 * KIB - KIB // 4)
         load_r(1, 24 * KIB)
-        load_wh(1, 0, 32 * KIB)
-        load_wh(1, 1, LATE_RAW)
+        load_wh(2, 0, 2, 32 * KIB)
+        load_wh(2, 1, 1, LATE_RAW)
         load_wg(1, 36 * KIB, 37 * KIB)
         for a in range(PASSES):
             grouped = sbuf([P, PAIR, PACK], BF16, f"grouped_0{a}")
@@ -163,7 +165,8 @@ def tile_list_hwayt_mix_relu_kernel(
             if a == 0:
                 parted.append(part_words(1, picked_1))
         load_r(2, 45 * KIB)
-        load_r(3, 53 * KIB)
+        load_wh(3, 1, 1, 54 * KIB + KIB // 2)
+        load_r(3, 64 * KIB)
 
         def moving(a, h):
             return dict(rhs=parted[h][:, a, :].bitcast(FP4X4), rhs_scale=planes[:, a, half(h)])
@@ -231,10 +234,9 @@ def tile_list_hwayt_mix_relu_kernel(
                     start=(opens and c == 0), stop=(not opens and c == HALF // P - 1), is_transpose=True,
                 )
 
-        def leave_bank(b, h):
-            turned = unit(f"turned_{b}{h}")
-            nc.scalar.copy(turned, sum_banks[b, h][:])
-            return turned
+        def leave_bank(b, h, place):
+            nc.scalar.copy(place, sum_banks[b, h][:])
+            return place
 
         def turn_back(b, h, turned, number):
             back = bank("back", number)
@@ -251,56 +253,60 @@ def tile_list_hwayt_mix_relu_kernel(
             for h in range(2 - 2 * b):
                 feature_product(b, h, 4 + h)
         for h in range(2):
-            keep_of(0, h, unit(f"keep_0{h}", (66 * KIB, None)[h]))
+            keep_of(0, h, unit(f"keep_0{h}", (80 * KIB, None)[h]))
         for h in range(2):
             gate_of(0, h, unit(f"gate_0{h}"))
         kept_0 = sbuf([P, J], F32, "kept_0")
-        made_0 = sbuf([P, J], F32, "made_0", 66 * KIB)
+        made_0 = sbuf([P, J], F32, "made_0", 80 * KIB)
         for h in range(2):
             kept_term(0, h, kept_0[:, half(h)])
         for h in range(2):
             made_term(0, h, made_0[:, half(h)])
         for h in range(2):
             keep_of(1, h, unit(f"keep_1{h}"))
-        gate_of(1, 0, unit("gate_10"))
+        for h in range(2):
+            gate_of(1, h, unit(f"gate_1{h}"))
         for h in range(2):
             kept_term(1, h, unit(f"kept_1{h}"))
         for h in range(2):
             feature_product(1, h, (5, 2)[h])
 
-        grouped = [sbuf([P, PAIR, PACK], BF16, f"grouped_1{a}", (None, 62 * KIB)[a]) for a in range(PASSES)]
-        for a in range(PASSES):
-            for b in (2, 3):
-                round_wh(b, a, grouped[a][:, (b - 2) * P : (b - 1) * P, :])
-        gate_of(1, 1, unit("gate_11", LATE_RAW + KIB))
-        quantize_wh(((2, 1), (3, 1)), grouped[1])
-        quantize_wh(((2, 0), (3, 0)), grouped[0], LATE_RAW)
+        grouped_c = sbuf([P, PAIR, PACK], BF16, "grouped_c")
+        for b in (2, 3):
+            round_wh(b, 0, grouped_c[:, (b - 2) * P : (b - 1) * P, :])
+        grouped_21 = sbuf([P, P, PACK], BF16, "grouped_21", 72 * KIB)
+        round_wh(2, 1, grouped_21[:])
+        quantize_wh(((2, 1),), grouped_21)
+        quantize_wh(((2, 0), (3, 0)), grouped_c, LATE_RAW + KIB // 4)
         for h in range(2):
             gate_product(2, h, h)
         for h in range(2):
             feature_product(2, h, 6 + h, (1, 0))
-        gate_product(3, 0, 3)
-        result_0 = sbuf([P, J], F32, "result_0", 62 * KIB)
+        result_0 = sbuf([P, J], F32, "result_0", 72 * KIB)
         nc.gpsimd.tensor_tensor(result_0[:], kept_0[:], made_0[:], ALU.add)
         nc.sync.dma_start(out[0:P, :], result_0[:])
-        made_1 = sbuf([P, J], F32, "made_1", LATE_RAW + 3 * KIB)
+        made_1 = sbuf([P, J], F32, "made_1", LATE_RAW + KIB + KIB // 4)
         for h in range(2):
             made_term(1, h, made_1[:, half(h)])
-        gate_product(3, 1, 5)
         for h in range(2):
-            turn(1, h, mades[1, h], (4, 2)[h])
+            gate_product(3, h, (5, 2)[h])
+            turn(1, h, mades[1, h], (4, 3)[h])
             turn(1, h, kepts[1, h])
         for h in range(2):
             gate_of(2, h, unit(f"gate_2{h}"))
         for h in range(2):
             made_term(2, h, unit(f"made_2{h}"))
         turn(2, 0, mades[2, 0], 6)
-        for h in range(2):
-            keep_of(2, h, unit(f"keep_2{h}"))
-        keep_of(3, 0, unit("keep_30", 70 * KIB))
-        keep_of(3, 1, unit("keep_31"))
+        keep_of(2, 0, unit("keep_20"))
+        grouped_31 = sbuf([P, P, PACK], BF16, "grouped_31")
+        round_wh(3, 1, grouped_31[:])
+        late = sbuf([P, 4 * HALF], F32, "late", 55 * KIB)
+        keep_of(2, 1, late[:, half(0)])
+        keep_of(3, 0, unit("keep_30", 53 * KIB))
+        keep_of(3, 1, late[:, half(1)])
         kept_term(2, 0, unit("kept_20"))
         turn(2, 0, kepts[2, 0])
+        quantize_wh(((3, 1),), grouped_31)
         kept_term(2, 1, unit("kept_21"))
         result_21 = unit("result_21")
         nc.gpsimd.tensor_tensor(result_21, kepts[2, 1], mades[2, 1], ALU.add)
@@ -308,15 +314,16 @@ def tile_list_hwayt_mix_relu_kernel(
         kept_term(3, 0, unit("kept_30"))
 
         for h in range(2):
-            feature_product(3, h, (3, 5)[h])
-        turned = {piece: leave_bank(*piece) for piece in ((1, 0), (1, 1), (2, 0))}
+            feature_product(3, h, (5, 2)[h])
+        turned = {(1, h): leave_bank(1, h, late[:, half(2 + h)]) for h in range(2)}
+        turned[2, 0] = leave_bank(2, 0, unit("turned_20"))
         for h in range(2):
             made_term(3, h, unit(f"made_3{h}"))
         for number, (b, h) in zip((0, 1, 7), turned):
             turn_back(b, h, turned[b, h], number)
 
         vector_sum(0, 0, HALF)
-        kept_31 = unit("kept_31", 70 * KIB)
+        kept_31 = unit("kept_31", 53 * KIB)
         for first in (0, QUARTER):
             kept_term(3, 1, kept_31, first, QUARTER)
         for first in (0, QUARTER):

@@ -223,6 +223,11 @@ def tile_list_hwayt_mix_relu_kernel(
             nc.vector.scalar_tensor_tensor(result[:], mades[3, h][:, cols], 0.0, kepts[3, h][:, cols], ALU.max, ALU.add)
             nc.sync.dma_start(out[3 * P :, h * HALF + first : h * HALF + first + width], result[:])
 
+        def gpsimd_sum(b, h, at=None):
+            result = unit(f"result_{b}{h}", at)
+            nc.gpsimd.tensor_tensor(result, kepts[b, h], mades[b, h], ALU.add)
+            nc.sync.dma_start(out[b * P : (b + 1) * P, half(h)], result)
+
         def turn(b, h, term, number=None):
             opens = number is not None
             if opens:
@@ -238,38 +243,40 @@ def tile_list_hwayt_mix_relu_kernel(
             nc.scalar.copy(place, sum_banks[b, h][:])
             return place
 
-        def turn_back(b, h, turned, number):
+        def turn_back(turned, number):
             back = bank("back", number)
             for c in range(HALF // P):
                 cols = slice(c * P, (c + 1) * P)
                 nc.tensor.transpose(back[:, cols], turned[:, cols], ident[:])
-            result = unit(f"result_{b}{h}")
+            return back
+
+        def store_back(b, h, back, result):
             nc.scalar.copy(result, back[:])
             nc.scalar.dma_start(out[b * P : (b + 1) * P, half(h)], result)
 
         for b in range(2):
             for h in range(2):
                 gate_product(b, h, 2 * b + h)
-            for h in range(2 - 2 * b):
-                feature_product(b, h, 4 + h)
+            for h in range(2 - b):
+                feature_product(b, h, ((4, 5), (7,))[b][h])
         for h in range(2):
             keep_of(0, h, unit(f"keep_0{h}", (80 * KIB, None)[h]))
         for h in range(2):
             gate_of(0, h, unit(f"gate_0{h}"))
-        kept_0 = sbuf([P, J], F32, "kept_0")
         made_0 = sbuf([P, J], F32, "made_0", 80 * KIB)
         for h in range(2):
-            kept_term(0, h, kept_0[:, half(h)])
+            kept_term(0, h, unit(f"kept_0{h}"))
+        turn(0, 0, kepts[0, 0], 6)
         for h in range(2):
             made_term(0, h, made_0[:, half(h)])
+        turn(0, 0, mades[0, 0])
         for h in range(2):
             keep_of(1, h, unit(f"keep_1{h}"))
         for h in range(2):
             gate_of(1, h, unit(f"gate_1{h}"))
         for h in range(2):
             kept_term(1, h, unit(f"kept_1{h}"))
-        for h in range(2):
-            feature_product(1, h, (5, 2)[h])
+        feature_product(1, 1, 2)
 
         grouped_c = sbuf([P, PAIR, PACK], BF16, "grouped_c")
         for b in (2, 3):
@@ -278,49 +285,48 @@ def tile_list_hwayt_mix_relu_kernel(
         round_wh(2, 1, grouped_21[:])
         quantize_wh(((2, 1),), grouped_21)
         quantize_wh(((2, 0), (3, 0)), grouped_c, LATE_RAW + KIB // 4)
+        middle = sbuf([P, 3 * HALF], F32, "middle", LATE_RAW + KIB + KIB // 4)
+        turned_00 = leave_bank(0, 0, middle[:, half(2)])
         for h in range(2):
             gate_product(2, h, h)
         for h in range(2):
-            feature_product(2, h, 6 + h, (1, 0))
-        result_0 = sbuf([P, J], F32, "result_0", 72 * KIB)
-        nc.gpsimd.tensor_tensor(result_0[:], kept_0[:], made_0[:], ALU.add)
-        nc.sync.dma_start(out[0:P, :], result_0[:])
-        made_1 = sbuf([P, J], F32, "made_1", LATE_RAW + KIB + KIB // 4)
+            feature_product(2, h, 4 + h, (1, 0))
+        back_00 = turn_back(turned_00, 3)
+        gpsimd_sum(0, 1, 72 * KIB)
         for h in range(2):
-            made_term(1, h, made_1[:, half(h)])
-        for h in range(2):
-            gate_product(3, h, (5, 2)[h])
-            turn(1, h, mades[1, h], (4, 3)[h])
-            turn(1, h, kepts[1, h])
+            made_term(1, h, middle[:, half(h)])
+        gpsimd_sum(1, 0)
         for h in range(2):
             gate_of(2, h, unit(f"gate_2{h}"))
+        keep_of(2, 0, unit("keep_20"))
+        for h in range(2):
+            gate_product(3, h, (7, 2)[h])
+        turn(1, 1, mades[1, 1], 6)
+        turn(1, 1, kepts[1, 1])
         for h in range(2):
             made_term(2, h, unit(f"made_2{h}"))
-        turn(2, 0, mades[2, 0], 6)
-        keep_of(2, 0, unit("keep_20"))
+        turn(2, 0, mades[2, 0], 4)
         grouped_31 = sbuf([P, P, PACK], BF16, "grouped_31")
         round_wh(3, 1, grouped_31[:])
         late = sbuf([P, 4 * HALF], F32, "late", 55 * KIB)
         keep_of(2, 1, late[:, half(0)])
-        keep_of(3, 0, unit("keep_30", 53 * KIB))
-        keep_of(3, 1, late[:, half(1)])
+        store_back(0, 0, back_00, late[:, half(3)])
         kept_term(2, 0, unit("kept_20"))
         turn(2, 0, kepts[2, 0])
         quantize_wh(((3, 1),), grouped_31)
+        feature_product(3, 1, 5)
         kept_term(2, 1, unit("kept_21"))
-        result_21 = unit("result_21")
-        nc.gpsimd.tensor_tensor(result_21, kepts[2, 1], mades[2, 1], ALU.add)
-        nc.sync.dma_start(out[2 * P : 3 * P, half(1)], result_21)
+        gpsimd_sum(2, 1)
+        keep_of(3, 0, unit("keep_30", 53 * KIB))
+        keep_of(3, 1, late[:, half(2)])
+        turned_11 = leave_bank(1, 1, late[:, half(1)])
         kept_term(3, 0, unit("kept_30"))
-
-        for h in range(2):
-            feature_product(3, h, (5, 2)[h])
-        turned = {(1, h): leave_bank(1, h, late[:, half(2 + h)]) for h in range(2)}
-        turned[2, 0] = leave_bank(2, 0, unit("turned_20"))
+        feature_product(3, 0, 7)
+        turned_20 = leave_bank(2, 0, unit("turned_20"))
+        store_back(1, 1, turn_back(turned_11, 0), unit("result_11"))
+        store_back(2, 0, turn_back(turned_20, 1), unit("result_20"))
         for h in range(2):
             made_term(3, h, unit(f"made_3{h}"))
-        for number, (b, h) in zip((0, 1, 7), turned):
-            turn_back(b, h, turned[b, h], number)
 
         vector_sum(0, 0, HALF)
         kept_31 = unit("kept_31", 53 * KIB)

@@ -152,7 +152,15 @@ def tile_list_hwayt_mix_relu_kernel(
             nc.sync.dma_start(planes[32 * q : 32 * q + 4].bitcast(I32), joined[8 * q : 8 * q + 8, :].bitcast(I32))
         load_r(0, 0)
 
-        parted = [part_words(0, gather_words(0, 36 * KIB - 256))]
+        picked_0 = gather_words(0, 36 * KIB - 256)
+        warm_bank = bank("warm_bank", 7)
+        for count in range(3):
+            nc.tensor.matmul_mx(
+                out=warm_bank[:], lhsT=wg8[0][:, 0:P].bitcast(FP8X4), lhsT_scale=tab_sc[:, 0:P],
+                rhs=picked_0[:, 0:QUARTER].bitcast(U16).bitcast(FP4X4), rhs_scale=tab_sc[:, 0:HALF],
+                start=True, stop=True,
+            )
+        parted = [part_words(0, picked_0)]
         picked_1 = gather_words(1, 53 * KIB - KIB // 4)
         load_r(1, 24 * KIB)
         load_wh(2, 0, 2, 32 * KIB)

@@ -64,7 +64,7 @@ def tile_list_hwayt_mix_relu_kernel(
         nc.vector.memset(tab_sc[32:64, :].bitcast(I32), 0)
         nc.vector.memset(tab_sc[64:128, :].bitcast(I32), 0)
 
-        table = sbuf([P, T], I32, "table", 24 * KIB)
+        table = sbuf([P, T], I32, "table")
         nc.sync.dma_start(table[:], tab_words[0].rearrange("p t b -> p (t b)").bitcast(I32))
 
         joined = sbuf([SC_ROWS, J + N], U8, "joined")
@@ -131,28 +131,27 @@ def tile_list_hwayt_mix_relu_kernel(
                 cols = slice(place * P, (place + 1) * P)
                 wh_q[piece] = (codes[:, cols], scales[:, cols])
 
-        def gather_words(h, at):
-            picked = sbuf([P, HALF], U32, f"picked_{h}", at)
-            nc.vector.tensor_copy(picked[:], table[:].bitcast(U32).indirect(listed(h * HALF, HALF)))
-            return picked
+        def gather_words(place, first, count):
+            nc.vector.tensor_copy(place, table[:].bitcast(U32).indirect(listed(first, count)))
 
-        def part_words(h, picked):
-            words = sbuf([P, PASSES, HALF], U16, f"parted_{h}")
-            nc.vector.tensor_copy(words[:], picked[:].bitcast(U16).rearrange("p (t d) -> p d t", d=2))
-            return words
+        def part_words(place, picked):
+            nc.vector.tensor_copy(place, picked.bitcast(U16).rearrange("p (t d) -> p d t", d=2))
 
         load_wg(0)
         for a in range(PASSES):
-            load_wh(0, a, 2, (None, 64 * KIB)[a])
+            load_wh(0, a, 2, (53 * KIB, 64 * KIB)[a])
 
-        picked_sc = sbuf([P, J], U8, "picked_sc", 0)
+        picked_sc = sbuf([P, J], U8, "picked_sc", 8 * KIB - J // 2)
         nc.vector.tensor_copy(picked_sc[:], tab_sc[:].indirect(offsets[:]))
         nc.vector.tensor_copy(joined[:, 0:J].bitcast(I32), picked_sc[0:SC_ROWS, :].bitcast(I32))
         for q in (0, 2, 1, 3):
             nc.sync.dma_start(planes[32 * q : 32 * q + 4].bitcast(I32), joined[8 * q : 8 * q + 8, :].bitcast(I32))
         load_r(0, 0)
+        load_r(1, 8 * KIB)
 
-        picked_0 = gather_words(0, 36 * KIB - 256)
+        picked_0 = sbuf([P, HALF], U32, "picked_0", 36 * KIB - 256)
+        for first in (0, QUARTER):
+            gather_words(picked_0[:, first : first + QUARTER], first, QUARTER)
         warm_bank = bank("warm_bank", 7)
         for count in range(3):
             nc.tensor.matmul_mx(
@@ -160,18 +159,23 @@ def tile_list_hwayt_mix_relu_kernel(
                 rhs=picked_0[:, 0:QUARTER].bitcast(U16).bitcast(FP4X4), rhs_scale=tab_sc[:, 0:HALF],
                 start=True, stop=True,
             )
-        parted = [part_words(0, picked_0)]
-        picked_1 = gather_words(1, 53 * KIB - KIB // 4)
-        load_r(1, 24 * KIB)
+        picked_2 = sbuf([P, P], U32, "picked_2", 52 * KIB)
+        gather_words(picked_2[:], HALF, P)
+        parted = [sbuf([P, PASSES, HALF], U16, f"parted_{h}") for h in range(2)]
+        part_words(parted[0][:], picked_0[:])
         load_wh(2, 0, 2, 32 * KIB)
         load_wh(2, 1, 1, LATE_RAW)
         load_wg(1, 36 * KIB, 37 * KIB)
         for a in range(PASSES):
             grouped = sbuf([P, PAIR, PACK], BF16, f"grouped_0{a}")
             round_wh(0, a, grouped[:], 2)
+            if a == 0:
+                picked_3 = sbuf([P, HALF - P], U32, "picked_3", 53 * KIB + KIB // 2)
+                gather_words(picked_3[:], HALF + P, HALF - P)
+                part_words(parted[1][:, :, 0:P], picked_2[:])
             quantize_wh(((0, a), (1, a)), grouped)
             if a == 0:
-                parted.append(part_words(1, picked_1))
+                part_words(parted[1][:, :, P:], picked_3[:])
         load_r(2, 45 * KIB)
         load_wh(3, 1, 1, 54 * KIB + KIB // 2)
         load_r(3, 64 * KIB)

@@ -41,7 +41,7 @@ def tile_list_hwayt_mix_relu_kernel(
 
         def sbuf(shape, dtype, name, at=None):
             if at is None:
-                return held.tile(shape, dtype, name=name, align_bytes=64)
+                return held.tile(shape, dtype, name=name, align_bytes=256)
             return laid.tile(shape, dtype, name=name, offset=at, align_bytes=256)
 
         def bank(name, number, width=HALF):
@@ -86,7 +86,7 @@ def tile_list_hwayt_mix_relu_kernel(
         nc.tensor.transpose(bias_bank[:], bias_rows[:], ident[:])
         bias = sbuf([P, BLOCKS], F32, "bias")
         nc.scalar.copy(bias[:], bias_bank[:, 0:BLOCKS])
-        neg_bias = sbuf([P, BLOCKS], F32, "neg_bias")
+        neg_bias = sbuf([P, BLOCKS], F32, "neg_bias", 88 * KIB)
         nc.scalar.activation(neg_bias[:], bias_bank[:, 0:BLOCKS], ACT.Copy, scale=-1.0)
 
         wg8, wg4, raws, wh_q, carried = {}, {}, {}, {}, {}
@@ -311,8 +311,8 @@ def tile_list_hwayt_mix_relu_kernel(
         for h in range(2):
             gate_of(2, h, unit(f"gate_2{h}"))
         keep_of(2, 0, unit("keep_20"))
-        for h in range(2):
-            gate_product(3, h, (7, 2)[h])
+        for h in (1, 0):
+            gate_product(3, h, (2, 7)[h])
         turn(1, 1, mades[1, 1], 6)
         turn(1, 1, kepts[1, 1])
         for h in range(2):
@@ -326,23 +326,23 @@ def tile_list_hwayt_mix_relu_kernel(
         kept_term(2, 0, unit("kept_20"))
         turn(2, 0, kepts[2, 0])
         quantize_wh(((3, 1),), grouped_31)
-        feature_product(3, 1, 5)
+        for h in (1, 0):
+            feature_product(3, h, (0, 5)[h])
         kept_term(2, 1, unit("kept_21"))
         gpsimd_sum(2, 1)
-        keep_of(3, 0, unit("keep_30", 53 * KIB))
         keep_of(3, 1, late[:, half(2)])
+        keep_of(3, 0, unit("keep_30", 53 * KIB))
         turned_11 = leave_bank(1, 1, late[:, half(1)])
-        kept_term(3, 0, unit("kept_30"))
-        feature_product(3, 0, 7)
         turned_20 = leave_bank(2, 0, unit("turned_20"))
-        store_back(1, 1, turn_back(turned_11, 0), unit("result_11"))
+        store_back(1, 1, turn_back(turned_11, 7), unit("result_11"))
         store_back(2, 0, turn_back(turned_20, 1), unit("result_20"))
-        for h in range(2):
+        for h in (1, 0):
             made_term(3, h, unit(f"made_3{h}"))
 
+        kept_3 = sbuf([P, J], F32, "kept_3", 88 * KIB)
+        kept_term(3, 0, kept_3[:, half(0)])
+        kept_term(3, 1, kept_3[:, half(1)], 0, QUARTER)
         vector_sum(0, 0, HALF)
-        kept_31 = unit("kept_31", 53 * KIB)
-        for first in (0, QUARTER):
-            kept_term(3, 1, kept_31, first, QUARTER)
+        kept_term(3, 1, kept_3[:, half(1)], QUARTER, QUARTER)
         for first in (0, QUARTER):
             vector_sum(1, first, QUARTER)

@@ -266,26 +266,32 @@ def tile_list_hwayt_mix_relu_kernel(
             nc.scalar.copy(result, back[:])
             nc.scalar.dma_start(out[b * P : (b + 1) * P, half(h)], result)
 
-        for b in range(2):
-            for h in range(2):
-                gate_product(b, h, 2 * b + h)
-            for h in range(2 - b):
-                feature_product(b, h, ((4, 5), (7,))[b][h])
+        for b, h in ((0, 0), (0, 1), (1, 1)):
+            gate_product(b, h, 2 * b + h)
         for h in range(2):
-            keep_of(0, h, unit(f"keep_0{h}", (80 * KIB, None)[h]))
+            feature_product(0, h, 4 + h)
+        gate_product(1, 0, 2)
+        feature_product(1, 0, 7)
+        keep_00 = unit("keep_00", 80 * KIB)
+        for first in (0, QUARTER):
+            keep_of(0, 0, keep_00[:, first : first + QUARTER], first, QUARTER)
+        keep_of(0, 1, unit("keep_01"))
+        gate_of(1, 1, unit("gate_11"))
         for h in range(2):
             gate_of(0, h, unit(f"gate_0{h}"))
-        made_0 = sbuf([P, J], F32, "made_0", 80 * KIB)
-        for h in range(2):
-            kept_term(0, h, unit(f"kept_0{h}"))
+        made_0 = sbuf([P, J], F32, "made_0", 81 * KIB)
+        kept_00 = unit("kept_00")
+        for first in (0, QUARTER):
+            kept_term(0, 0, kept_00, first, QUARTER, first)
+        kept_term(0, 1, unit("kept_01"))
         turn(0, 0, kepts[0, 0], 6)
         for h in range(2):
             made_term(0, h, made_0[:, half(h)])
         turn(0, 0, mades[0, 0])
-        for h in range(2):
-            keep_of(1, h, unit(f"keep_1{h}"))
-        for h in range(2):
-            gate_of(1, h, unit(f"gate_1{h}"))
+        keep_of(1, 0, unit("keep_10"))
+        gate_of(1, 0, unit("gate_10"))
+        keeps[1, 1, 0] = unit("keep_11", 79 * KIB)
+        nc.gpsimd.tensor_scalar(keeps[1, 1, 0], gates[1, 1], -1.0, 1.0, ALU.mult, ALU.add)
         for h in range(2):
             kept_term(1, h, unit(f"kept_1{h}"))
         feature_product(1, 1, 2)
@@ -322,7 +328,6 @@ def tile_list_hwayt_mix_relu_kernel(
         round_wh(3, 1, grouped_31[:])
         late = sbuf([P, 4 * HALF], F32, "late", 55 * KIB)
         keep_of(2, 1, late[:, half(0)])
-        store_back(0, 0, back_00, late[:, half(3)])
         kept_term(2, 0, unit("kept_20"))
         turn(2, 0, kepts[2, 0])
         quantize_wh(((3, 1),), grouped_31)
@@ -332,6 +337,7 @@ def tile_list_hwayt_mix_relu_kernel(
         gpsimd_sum(2, 1)
         keep_of(3, 1, late[:, half(2)])
         keep_of(3, 0, unit("keep_30", 53 * KIB))
+        store_back(0, 0, back_00, late[:, half(3)])
         turned_11 = leave_bank(1, 1, late[:, half(1)])
         turned_20 = leave_bank(2, 0, unit("turned_20"))
         store_back(1, 1, turn_back(turned_11, 7), unit("result_11"))

from contextlib import ExitStack

import concourse.mybir as mybir
from concourse.masks import make_identity

K, N, T, J = 1024, 512, 2048, 1024
FLOPS = 2 * 2 * K * N * J

F32 = mybir.dt.float32
BF16 = mybir.dt.bfloat16
I32 = mybir.dt.int32
U32 = mybir.dt.uint32
U16 = mybir.dt.uint16
U8 = mybir.dt.uint8
FP8X4 = mybir.dt.float8_e4m3fn_x4
FP4X4 = mybir.dt.float4_e2m1fn_x4
ALU = mybir.AluOpType
ACT = mybir.ActivationFunctionType

P = 128
PACK = 4
K_PASS = P * PACK
PASSES = K // K_PASS
BLOCKS = N // P
HALF = 512
QUARTER = 256
PAIR = 2 * P
SC_ROWS = 32
KIB = 1024
LATE_RAW = 37 * KIB + KIB // 2


def tile_list_hwayt_mix_relu_kernel(
    tc, tab_words, tab_scales, wg8_words, wg8_scales, wg4_words, wg4_scales, wh, bg, rT, offs, out
):
    nc = tc.nc
    with ExitStack() as ctx:
        held = ctx.enter_context(tc.tile_pool(name="held", bufs=1))
        laid = ctx.enter_context(tc.tile_pool(name="laid", bufs=1))
        psum = ctx.enter_context(tc.psum_pool(name="psum", bufs=1))

        def sbuf(shape, dtype, name, at=None):
            if at is None:
                return held.tile(shape, dtype, name=name, align_bytes=256)
            return laid.tile(shape, dtype, name=name, offset=at, align_bytes=256)

        def bank(name, number, width=HALF):
            return psum.tile([P, width], F32, name=name, tag=f"bank_{number}")

        def half(h):
            return slice(h * HALF, (h + 1) * HALF)

        def unit(name, at=None):
            return sbuf([P, HALF], F32, name, at)[:]

        offsets = held.tile([P, J // 16], U16, name="offsets")
        nc.sync.dma_start(offsets[:], offs)

        def listed(first, count):
            return offsets[:, first // 16 : (first + count) // 16]

        tab_sc = sbuf([P, T], U8, "tab_sc")
        nc.sync.dma_start(tab_sc[0:SC_ROWS, :].bitcast(I32), tab_scales.rearrange("a q t -> q a t").bitcast(I32))
        nc.vector.memset(tab_sc[32:64, :].bitcast(I32), 0)
        nc.vector.memset(tab_sc[64:128, :].bitcast(I32), 0)

        table = sbuf([P, T], I32, "table")
        nc.sync.dma_start(table[:], tab_words[0].rearrange("p t b -> p (t b)").bitcast(I32))

        joined = sbuf([SC_ROWS, J + N], U8, "joined")
        nc.sync.dma_start(joined[0:SC_ROWS:2, J:].bitcast(I32), wg8_scales[0].bitcast(I32))
        nc.sync.dma_start(joined[1:SC_ROWS:2, J:].bitcast(I32), wg4_scales[0].bitcast(I32))
        planes = sbuf([P, PASSES, J + N], U8, "planes")

        bias_rows = sbuf([P, P], F32, "bias_rows")
        nc.gpsimd.memset(bias_rows[:], 0.0)
        nc.scalar.dma_start(bias_rows[0:BLOCKS, :], bg.rearrange("(b p) -> b p", p=P))
        warm = sbuf([P, 8], F32, "warm")
        warm_out = sbuf([P, 8], F32, "warm_out")
        nc.gpsimd.memset(warm[:], 0.0)
        nc.scalar.activation(warm_out[:], warm[:], ACT.Sigmoid)

        ident = sbuf([P, P], F32, "ident")
        make_identity(nc, ident[:])
        bias_bank = bank("bias_bank", 7, P)
        nc.tensor.transpose(bias_bank[:], bias_rows[:], ident[:])
        bias = sbuf([P, BLOCKS], F32, "bias")
        nc.scalar.copy(bias[:], bias_bank[:, 0:BLOCKS])
        neg_bias = sbuf([P, BLOCKS], F32, "neg_bias", 88 * KIB)
        nc.scalar.activation(neg_bias[:], bias_bank[:, 0:BLOCKS], ACT.Copy, scale=-1.0)

        wg8, wg4, raws, wh_q, carried = {}, {}, {}, {}, {}
        gate_banks, feature_banks, sum_banks = {}, {}, {}
        gates, keeps, mades, kepts = {}, {}, {}, {}

        def load_wg(w, at8=None, at4=None):
            wg8[w] = sbuf([P, PAIR], I32, f"wg8_{w}", at8)
            words8 = wg8_words[0].rearrange("p n b -> p (n b)").bitcast(I32)
            nc.sync.dma_start(wg8[w][:], words8[:, w * PAIR : (w + 1) * PAIR])
            wg4[w] = sbuf([P, 2 * PAIR], U8, f"wg4_{w}", at4)
            nc.sync.dma_start(wg4[w][:].bitcast(I32), wg4_words[0][:, 2 * w * PAIR : 2 * (w + 1) * PAIR].bitcast(I32))

        def load_wh(b, a, blocks, at=None):
            raw = sbuf([P, PACK, blocks * P], F32, f"raw_{b}{a}", at)
            rows = wh[a * K_PASS : (a + 1) * K_PASS, b * P : (b + blocks) * P]
            nc.sync.dma_start(raw[:], rows.rearrange("(p i) n -> p i n", i=PACK))
            for c in range(blocks):
                raws[b + c, a] = (raw, c * P)

        def load_r(b, at):
            carried[b] = sbuf([P, T], F32, f"carried_{b}", at)
            nc.sync.dma_start(carried[b][:], rT[b * P : (b + 1) * P, :])

        def round_wh(b, a, place, blocks=1):
            raw, first = raws[b, a]
            nc.scalar.activation(
                place.rearrange("p (c e) i -> p c i e", e=4),
                raw[:, :, first : first + blocks * P].rearrange("p i (c e) -> p c i e", e=4),
                ACT.Copy,
                scale=-1.0 if b == BLOCKS - 1 else 1.0,
            )

        def quantize_wh(pieces, grouped, at=None):
            name = "".join(f"{b}{a}" for b, a in pieces)
            codes = sbuf([P, len(pieces) * P], U32, f"codes_{name}", at)
            scales = sbuf([P, len(pieces) * P], U8, f"scales_{name}")
            nc.vector.quantize_mx(
                out=codes[:].bitcast(FP8X4), scales=scales[:], in_=grouped[:].rearrange("p n i -> p (n i)")
            )
            for place, piece in enumerate(pieces):
                cols = slice(place * P, (place + 1) * P)
                wh_q[piece] = (codes[:, cols], scales[:, cols])

        def gather_words(place, first, count):
            nc.vector.tensor_copy(place, table[:].bitcast(U32).indirect(listed(first, count)))

        def part_words(place, picked):
            nc.vector.tensor_copy(place, picked.bitcast(U16).rearrange("p (t d) -> p d t", d=2))

        load_wg(0)
        for a in range(PASSES):
            load_wh(0, a, 2, (53 * KIB, 64 * KIB)[a])

        picked_sc = sbuf([P, J], U8, "picked_sc", 8 * KIB - J // 2)
        nc.vector.tensor_copy(picked_sc[:], tab_sc[:].indirect(offsets[:]))
        nc.vector.tensor_copy(joined[:, 0:J].bitcast(I32), picked_sc[0:SC_ROWS, :].bitcast(I32))
        for q in (0, 2, 1, 3):
            nc.sync.dma_start(planes[32 * q : 32 * q + 4].bitcast(I32), joined[8 * q : 8 * q + 8, :].bitcast(I32))
        load_r(0, 0)
        load_r(1, 8 * KIB)

        picked_0 = sbuf([P, HALF], U32, "picked_0", 36 * KIB - 256)
        for first in (0, QUARTER):
            gather_words(picked_0[:, first : first + QUARTER], first, QUARTER)
        warm_bank = bank("warm_bank", 7)
        for count in range(3):
            nc.tensor.matmul_mx(
                out=warm_bank[:], lhsT=wg8[0][:, 0:P].bitcast(FP8X4), lhsT_scale=tab_sc[:, 0:P],
                rhs=picked_0[:, 0:QUARTER].bitcast(U16).bitcast(FP4X4), rhs_scale=tab_sc[:, 0:HALF],
                start=True, stop=True,
            )
        picked_2 = sbuf([P, P], U32, "picked_2", 52 * KIB)
        gather_words(picked_2[:], HALF, P)
        parted = [sbuf([P, PASSES, HALF], U16, f"parted_{h}") for h in range(2)]
        part_words(parted[0][:], picked_0[:])
        load_wh(2, 0, 2, 32 * KIB)
        load_wh(2, 1, 1, LATE_RAW)
        load_wg(1, 36 * KIB, 37 * KIB)
        for a in range(PASSES):
            grouped = sbuf([P, PAIR, PACK], BF16, f"grouped_0{a}")
            round_wh(0, a, grouped[:], 2)
            if a == 0:
                picked_3 = sbuf([P, HALF - P], U32, "picked_3", 53 * KIB + KIB // 2)
                gather_words(picked_3[:], HALF + P, HALF - P)
                part_words(parted[1][:, :, 0:P], picked_2[:])
            quantize_wh(((0, a), (1, a)), grouped)
            if a == 0:
                part_words(parted[1][:, :, P:], picked_3[:])
        load_r(2, 45 * KIB)
        load_wh(3, 1, 1, 54 * KIB + KIB // 2)
        load_r(3, 64 * KIB)

        def moving(a, h):
            return dict(rhs=parted[h][:, a, :].bitcast(FP4X4), rhs_scale=planes[:, a, half(h)])

        def gate_product(b, h, number):
            ga = bank("ga", number)
            scale_cols = slice(J + b * P, J + (b + 1) * P)
            own = slice((b % 2) * P, (b % 2 + 1) * P)
            nc.tensor.matmul_mx(
                out=ga[:], lhsT=wg8[b // 2][:, own].bitcast(FP8X4), lhsT_scale=planes[:, 0, scale_cols],
                start=True, stop=False, **moving(0, h),
            )
            nc.tensor.matmul_mx(
                out=ga[:], lhsT=wg4[b // 2][:, 2 * own.start : 2 * own.stop].bitcast(FP4X4),
                lhsT_scale=planes[:, 1, scale_cols], start=False, stop=True, **moving(1, h),
            )
            gate_banks[b, h] = ga

        def feature_product(b, h, number, passes=(0, 1)):
            feature_banks[b, h] = bank("ha", number)
            for a in passes:
                codes, scales = wh_q[b, a]
                nc.tensor.matmul_mx(
                    out=feature_banks[b, h][:], lhsT=codes.bitcast(FP8X4), lhsT_scale=scales,
                    start=(a == passes[0]), stop=(a == passes[-1]), **moving(a, h),
                )

        def keep_of(b, h, place, first=0, width=HALF):
            keeps[b, h, first] = place
            ga = gate_banks[b, h][:, first : first + width]
            nc.scalar.activation(place, ga, ACT.Sigmoid, bias=neg_bias[:, b : b + 1], scale=-1.0)

        def gate_of(b, h, place):
            gates[b, h] = place
            nc.scalar.activation(place, gate_banks[b, h][:], ACT.Sigmoid, bias=bias[:, b : b + 1])

        def kept_term(b, h, place, first=0, width=HALF, keep_first=0):
            kepts[b, h] = place
            window = carried[b][:].indirect(listed(h * HALF + first, width))
            keep = keeps[b, h, keep_first][:, first - keep_first : first - keep_first + width]
            nc.vector.tensor_tensor(place[:, first : first + width], window, keep, ALU.mult)

        def made_term(b, h, place):
            mades[b, h] = place
            ha = feature_banks[b, h]
            if b == BLOCKS - 1:
                nc.vector.scalar_tensor_tensor(place, keeps[b, h, 0], 1.0, ha[:], ALU.subtract, ALU.mult)
            else:
                nc.vector.scalar_tensor_tensor(place, ha[:], 0.0, gates[b, h], ALU.max, ALU.mult)

        def vector_sum(h, first, width):
            cols = slice(first, first + width)
            result = sbuf([P, width], F32, f"result_3{h}{first}")
            nc.vector.scalar_tensor_tensor(result[:], mades[3, h][:, cols], 0.0, kepts[3, h][:, cols], ALU.max, ALU.add)
            nc.sync.dma_start(out[3 * P :, h * HALF + first : h * HALF + first + width], result[:])

        def gpsimd_sum(b, h, at=None):
            result = unit(f"result_{b}{h}", at)
            nc.gpsimd.tensor_tensor(result, kepts[b, h], mades[b, h], ALU.add)
            nc.sync.dma_start(out[b * P : (b + 1) * P, half(h)], result)

        def turn(b, h, term, number=None):
            opens = number is not None
            if opens:
                sum_banks[b, h] = bank("turned_sum", number)
            for c in range(HALF // P):
                cols = slice(c * P, (c + 1) * P)
                nc.tensor.matmul(
                    sum_banks[b, h][:, cols], term[:, cols], ident[:],
                    start=(opens and c == 0), stop=(not opens and c == HALF // P - 1), is_transpose=True,
                )

        def leave_bank(b, h, place):
            nc.scalar.copy(place, sum_banks[b, h][:])
            return place

        def turn_back(turned, number):
            back = bank("back", number)
            for c in range(HALF // P):
                cols = slice(c * P, (c + 1) * P)
                nc.tensor.transpose(back[:, cols], turned[:, cols], ident[:])
            return back

        def store_back(b, h, back, result):
            nc.scalar.copy(result, back[:])
            nc.scalar.dma_start(out[b * P : (b + 1) * P, half(h)], result)

        for b, h in ((0, 0), (0, 1), (1, 1)):
            gate_product(b, h, 2 * b + h)
        for h in range(2):
            feature_product(0, h, 4 + h)
        gate_product(1, 0, 2)
        feature_product(1, 0, 7)
        keep_00 = unit("keep_00", 80 * KIB)
        for first in (0, QUARTER):
            keep_of(0, 0, keep_00[:, first : first + QUARTER], first, QUARTER)
        keep_of(0, 1, unit("keep_01"))
        gate_of(1, 1, unit("gate_11"))
        for h in range(2):
            gate_of(0, h, unit(f"gate_0{h}"))
        made_0 = sbuf([P, J], F32, "made_0", 81 * KIB)
        kept_00 = unit("kept_00")
        for first in (0, QUARTER):
            kept_term(0, 0, kept_00, first, QUARTER, first)
        kept_term(0, 1, unit("kept_01"))
        turn(0, 0, kepts[0, 0], 6)
        for h in range(2):
            made_term(0, h, made_0[:, half(h)])
        turn(0, 0, mades[0, 0])
        keep_of(1, 0, unit("keep_10"))
        gate_of(1, 0, unit("gate_10"))
        keeps[1, 1, 0] = unit("keep_11", 79 * KIB)
        nc.gpsimd.tensor_scalar(keeps[1, 1, 0], gates[1, 1], -1.0, 1.0, ALU.mult, ALU.add)
        for h in range(2):
            kept_term(1, h, unit(f"kept_1{h}"))
        feature_product(1, 1, 2)

        grouped_c = sbuf([P, PAIR, PACK], BF16, "grouped_c")
        for b in (2, 3):
            round_wh(b, 0, grouped_c[:, (b - 2) * P : (b - 1) * P, :])
        grouped_21 = sbuf([P, P, PACK], BF16, "grouped_21", 72 * KIB)
        round_wh(2, 1, grouped_21[:])
        quantize_wh(((2, 1),), grouped_21)
        quantize_wh(((2, 0), (3, 0)), grouped_c, LATE_RAW + KIB // 4)
        middle = sbuf([P, 3 * HALF], F32, "middle", LATE_RAW + KIB + KIB // 4)
        turned_00 = leave_bank(0, 0, middle[:, half(2)])
        for h in range(2):
            gate_product(2, h, h)
        for h in range(2):
            feature_product(2, h, 4 + h, (1, 0))
        back_00 = turn_back(turned_00, 3)
        gpsimd_sum(0, 1, 72 * KIB)
        for h in range(2):
            made_term(1, h, middle[:, half(h)])
        gpsimd_sum(1, 0)
        for h in range(2):
            gate_of(2, h, unit(f"gate_2{h}"))
        keep_of(2, 0, unit("keep_20"))
        for h in (1, 0):
            gate_product(3, h, (2, 7)[h])
        turn(1, 1, mades[1, 1], 6)
        turn(1, 1, kepts[1, 1])
        for h in range(2):
            made_term(2, h, unit(f"made_2{h}"))
        turn(2, 0, mades[2, 0], 4)
        grouped_31 = sbuf([P, P, PACK], BF16, "grouped_31")
        round_wh(3, 1, grouped_31[:])
        late = sbuf([P, 4 * HALF], F32, "late", 55 * KIB)
        keep_of(2, 1, late[:, half(0)])
        kept_term(2, 0, unit("kept_20"))
        turn(2, 0, kepts[2, 0])
        quantize_wh(((3, 1),), grouped_31)
        for h in (1, 0):
            feature_product(3, h, (0, 5)[h])
        kept_term(2, 1, unit("kept_21"))
        gpsimd_sum(2, 1)
        keep_of(3, 1, late[:, half(2)])
        keep_of(3, 0, unit("keep_30", 53 * KIB))
        store_back(0, 0, back_00, late[:, half(3)])
        turned_11 = leave_bank(1, 1, late[:, half(1)])
        turned_20 = leave_bank(2, 0, unit("turned_20"))
        store_back(1, 1, turn_back(turned_11, 7), unit("result_11"))
        store_back(2, 0, turn_back(turned_20, 1), unit("result_20"))
        for h in (1, 0):
            made_term(3, h, unit(f"made_3{h}"))

        kept_3 = sbuf([P, J], F32, "kept_3", 88 * KIB)
        kept_term(3, 0, kept_3[:, half(0)])
        kept_term(3, 1, kept_3[:, half(1)], 0, QUARTER)
        vector_sum(0, 0, HALF)
        kept_term(3, 1, kept_3[:, half(1)], QUARTER, QUARTER)
        for first in (0, QUARTER):
            vector_sum(1, first, QUARTER)
